import numpy as np
import ml_dtypes


def mxq(x, axis, fmt="e4m3"):
    dtype, down = {"e4m3": (ml_dtypes.float8_e4m3fn, 7), "e5m2": (ml_dtypes.float8_e5m2, 14)}[fmt]
    v = np.moveaxis(np.asarray(x, np.float32).astype(ml_dtypes.bfloat16).astype(np.float64), axis, -1)
    blocks = v.reshape(v.shape[:-1] + (-1, 32))
    amax = np.abs(blocks).max(-1, keepdims=True)
    byte = np.maximum(np.where(amax > 0, np.frexp(amax)[1] - 1 + 127, 0) - down, 1)
    scale = np.exp2(byte - 127.0)
    codes = (blocks / scale).astype(np.float32).astype(dtype).astype(np.float64)
    return np.moveaxis((codes * scale).reshape(v.shape), -1, axis)


WIDE = False


def mx_kscale(k):
    if not WIDE:
        return np.ones(k)
    levels = np.array([30, -30])
    if k % 512:
        return np.exp2(np.random.permutation(np.resize(levels, k // 32))).repeat(32)
    a = np.empty((k // 512, 16))
    for p in range(k // 512):
        a[p, :8] = np.random.permutation(np.resize(levels, 8))
        for g in range(8):
            far = levels[np.abs(levels - a[p, g]) >= 10]
            a[p, g + 8] = far[np.random.randint(len(far))]
    return np.exp2(a.ravel()).repeat(32)


def f64(x):
    return np.asarray(x).astype(np.float64)


def striped(idx):
    return np.tile(idx.reshape(-1, 16).T, (8, 1)).astype(np.uint16)


def unstriped(offs):
    return offs[:16].T.reshape(-1).astype(np.int64)


def d_relu(v):
    return (v > 0).astype(np.float64)


K, T, E, C, H, N = 384, 1024, 2, 512, 512, 512


def by_expert(wq, xq):
    return np.concatenate([wq[e].T @ xq[:, e * C:(e + 1) * C] for e in range(E)], axis=1)


def setup_inputs():
    n = np.random.standard_normal
    slot_token = np.random.permutation(T)[:E * C]
    s = mx_kscale(N)[:, None]
    z = np.ones(T); z[slot_token] = mx_kscale(E * C)
    return {
        "xT": (n((K, T)) * z[None, :]).astype(np.float32),
        "dyT": (n((N, T)) * s).astype(np.float32),
        "a": n((H, E * C)).astype(np.float32),
        "w2": (n((E, N, H)) / np.sqrt(N) / s[None]).astype(np.float32),
        "gate": np.tile(np.random.uniform(0.2, 1.0, E * C) / z[slot_token], (N, 1)).astype(np.float32),
        "offs": striped(slot_token),
    }


def reference(xT, dyT, a, w2, gate, offs):
    idx = unstriped(offs)
    gq = mxq(f64(gate) * f64(dyT)[:, idx], 0, "e5m2")
    dh = by_expert(mxq(f64(w2), 1, "e4m3"), gq)
    da = mxq(dh * d_relu(f64(a)), 1, "e5m2")
    xq = mxq(f64(xT)[:, idx], 1, "e4m3")
    return np.stack([(xq[:, e * C:(e + 1) * C] @ da[:, e * C:(e + 1) * C].T) for e in range(E)])

@@ -1,0 +1,279 @@
+from contextlib import ExitStack
+
+import concourse.mybir as mybir
+from concourse.masks import make_identity
+
+K, T, E, C, H, N = 384, 1024, 2, 512, 512, 512
+FLOPS = 2 * E * C * H * (N + K)
+BYTES = 4 * (K * T + N * T + H * E * C + E * N * H + E * C + E * K * H) + 2 * 128 * 64
+
+F32 = mybir.dt.float32
+BF16 = mybir.dt.bfloat16
+U32 = mybir.dt.uint32
+U16 = mybir.dt.uint16
+U8 = mybir.dt.uint8
+E4M3 = mybir.dt.float8_e4m3fn_x4
+E5M2 = mybir.dt.float8_e5m2_x4
+COPY = mybir.ActivationFunctionType.Copy
+MULT = mybir.AluOpType.mult
+ADD = mybir.AluOpType.add
+IS_GT = mybir.AluOpType.is_gt
+
+P = 128
+PACK = 4
+KT = K // P
+HT = H // P
+OC = C // 16
+HALF = 2 * P
+
+
+def interleave(copy, dst, src):
+    copy(out=dst.rearrange("p (c i) t -> p c t i", i=4), in_=src.rearrange("p t (c i) -> p c t i", i=4))
+
+
+def tile_moe_mlp_relu_kernel(tc, xT, dyT, a, w2, gate, offs, out):
+    nc = tc.nc
+    with ExitStack() as ctx:
+        keep = ctx.enter_context(tc.tile_pool(name="keep", bufs=1))
+        psum = ctx.enter_context(tc.psum_pool(name="psum", bufs=8))
+
+        def held(name, shape, dtype):
+            return keep.tile(shape, dtype, name=name, align_bytes=64)
+
+        offsets = keep.tile([P, E * OC], U16, name="offsets")
+        gates = [held("gate%d" % e, [P, C], F32) for e in range(E)]
+        dy = [held("dy%d" % t, [P, T], F32) for t in range(PACK)]
+        x32 = [held("x32_%d" % k, [P, T], F32) for k in range(KT)]
+        x16 = [held("x16_%d" % k, [P, T], BF16) for k in range(KT)]
+        w32 = [[held("w32_%d_%d" % (e, h), [P, PACK, HALF], F32) for h in range(2)] for e in range(E)]
+        pre = [[held("a%d_%d" % (e, h), [P, 2, C], F32) for h in range(2)] for e in range(E)]
+        g32 = [held("g32_%d" % e, [P, PACK, C], F32) for e in range(E)]
+        g16 = [[held("g16_%d_%d" % (e, h), [P, HALF, PACK], BF16) for h in range(2)] for e in range(E)]
+        w16 = [[held("w16_%d_%d" % (e, h), [P, HALF, PACK], BF16) for h in range(2)] for e in range(E)]
+        g_codes = [held("gc%d" % e, [P, C], U32) for e in range(E)]
+        g_scales = [held("gs%d" % e, [P, C], U8) for e in range(E)]
+        w_codes = [held("wc%d" % e, [P, H], U32) for e in range(E)]
+        w_scales = [held("ws%d" % e, [P, H], U8) for e in range(E)]
+        x_slots = [[held("xs%d_%d" % (e, k), [P, 2, C // 2], BF16) for k in range(KT)] for e in range(E)]
+        x_turned = [held("xt%d" % e, [P, KT, P, 2], F32) for e in range(E)]
+        x_codes = [held("xc%d" % e, [P, K], U32) for e in range(E)]
+        x_scales = [held("xsc%d" % e, [P, K], U8) for e in range(E)]
+        da = [[held("da%d_%d" % (e, b), [P, 2, C // 2], BF16) for b in range(HT)] for e in range(E)]
+        da_turned = [held("dt%d" % e, [P, HT, P, 2], F32) for e in range(E)]
+        d_codes = [held("dc%d" % e, [P, H], U32) for e in range(E)]
+        d_scales = [held("ds%d" % e, [P, H], U8) for e in range(E)]
+        results = [[held("res%d_%d" % (e, k), [P, H], F32) for k in range(KT)] for e in range(E)]
+
+        ident16 = held("ident16", [P, P], BF16)
+        ident = held("ident", [P, P], F32)
+        make_identity(nc, ident16[:])
+        nc.scalar.activation(ident[:], ident16[:], COPY)
+
+        dy_rows = dyT.rearrange("(p t) c -> t p c", t=PACK)
+
+        def load_gate(e):
+            nc.sync.dma_start(gates[e][:], gate[0:P, e * C:(e + 1) * C])
+
+        def load_dy(t):
+            nc.sync.dma_start(dy[t][:], dy_rows[t])
+
+        def load_x(k):
+            nc.sync.dma_start(x32[k][:], xT[k * P:(k + 1) * P, :])
+
+        def load_w(e, h):
+            cols = w2[e, :, h * HALF:(h + 1) * HALF]
+            nc.sync.dma_start(w32[e][h][:], cols.rearrange("(p t) i -> p t i", t=PACK))
+
+        def load_a(e, h):
+            rows = a[h * HALF:(h + 1) * HALF, e * C:(e + 1) * C]
+            nc.sync.dma_start(pre[e][h][:], rows.rearrange("(b p) c -> p b c", p=P))
+
+        nc.sync.dma_start(offsets[:], offs)
+        load_x(0)
+        load_gate(1)
+        load_dy(0)
+        load_x(1)
+        load_gate(0)
+        load_dy(3)
+        load_dy(1)
+        load_w(0, 1)
+        load_dy(2)
+        load_w(0, 0)
+        load_a(0, 0)
+        load_a(0, 1)
+        load_w(1, 0)
+        load_x(2)
+        load_w(1, 1)
+        load_a(1, 0)
+        load_a(1, 1)
+
+        banks = {}
+
+        def new_bank(key, shape):
+            banks[key] = psum.tile(shape, F32, name="bank")
+            return banks[key]
+
+        def slots(e):
+            return offsets[:, e * OC:(e + 1) * OC]
+
+        def gpsimd_copy(out, in_):
+            nc.gpsimd.tensor_scalar(out, in_, 1.0, 0.0, MULT, ADD)
+
+        def gather_g(t, e):
+            nc.vector.tensor_tensor(g32[e][:, t, :], dy[t][:].indirect(slots(e)), gates[e][:], MULT)
+
+        def round_x(k, copy):
+            copy(out=x16[k][:], in_=x32[k][:])
+
+        def gather_x(k, e):
+            nc.scalar.activation(x_slots[e][k][:].rearrange("p u q -> p q u"), x16[k][:].indirect(slots(e)), COPY)
+
+        def turn(key, sources):
+            bank = new_bank(key, [P, len(sources), 2, P])
+            for j, source in enumerate(sources):
+                for u in range(2):
+                    nc.tensor.transpose(bank[:, j, u, :], source[:, u, :].bitcast(F32), ident[:])
+
+        def take(key, turned, copy):
+            copy(out=turned, in_=banks[key][:].rearrange("p j u m -> p j m u"))
+
+        def quantize(codes, scales, values, fmt):
+            nc.vector.quantize_mx(out=codes.bitcast(fmt), scales=scales, in_=values)
+
+        def quantize_turned(codes, scales, turned, j0, j1, fmt):
+            cols = slice(P * j0, P * j1)
+            values = turned[:, j0:j1].rearrange("p j m u -> p (j m u)").bitcast(BF16)
+            quantize(codes[:, cols], scales[:, cols], values, fmt)
+
+        def half(h):
+            return slice(h * HALF, (h + 1) * HALF)
+
+        def round_w(e, h, copy):
+            interleave(copy, w16[e][h][:], w32[e][h][:])
+
+        def round_g(e, h, copy):
+            interleave(copy, g16[e][h][:], g32[e][:, :, half(h)])
+
+        def quantize_w(e, h):
+            quantize(w_codes[e][:, half(h)], w_scales[e][:, half(h)], w16[e][h][:].rearrange("p i t -> p (i t)"), E4M3)
+
+        def quantize_g(e, h):
+            quantize(g_codes[e][:, half(h)], g_scales[e][:, half(h)], g16[e][h][:].rearrange("p c t -> p (c t)"), E5M2)
+
+        def product_dh(e, b):
+            cols = slice(b * P, (b + 1) * P)
+            dh = new_bank(("dh", e, b), [P, C])
+            nc.tensor.matmul_mx(out=dh[:], lhsT=w_codes[e][:, cols].bitcast(E4M3), lhsT_scale=w_scales[e][:, cols],
+                                rhs=g_codes[e][:].bitcast(E5M2), rhs_scale=g_scales[e][:], start=True, stop=True)
+
+        def mask_dh(e, b):
+            nc.vector.scalar_tensor_tensor(
+                da[e][b][:], pre[e][b // 2][:, b % 2, :].rearrange("p (q u) -> p u q", u=2), 0.0,
+                banks[("dh", e, b)][:].rearrange("p (q u) -> p u q", u=2), IS_GT, MULT)
+
+        def product_out(e, k):
+            cols = slice(k * P, (k + 1) * P)
+            acc = new_bank(("out", e, k), [P, H])
+            nc.tensor.matmul_mx(out=acc[:], lhsT=x_codes[e][:, cols].bitcast(E4M3), lhsT_scale=x_scales[e][:, cols],
+                                rhs=d_codes[e][:].bitcast(E5M2), rhs_scale=d_scales[e][:], start=True, stop=True)
+
+        def take_out(e, k, copy):
+            copy(out=results[e][k][:], in_=banks[("out", e, k)][:])
+
+        def store(e, k):
+            nc.sync.dma_start(out[e, k * P:(k + 1) * P, :], results[e][k][:])
+
+        round_x(0, nc.vector.tensor_copy)
+        gather_x(0, 1)
+        gather_g(0, 1)
+        gather_x(0, 0)
+        gather_g(0, 0)
+        round_x(1, nc.scalar.copy)
+        gather_g(3, 1)
+        gather_x(1, 0)
+        gather_g(3, 0)
+        gather_x(1, 1)
+        turn(("x", 0, 0), x_slots[0][0:2])
+        gather_g(1, 1)
+        round_w(0, 1, nc.scalar.copy)
+        turn(("x", 1, 0), x_slots[1][0:2])
+        gather_g(1, 0)
+        take(("x", 0, 0), x_turned[0][:, 0:2], nc.scalar.copy)
+        take(("x", 1, 0), x_turned[1][:, 0:2], nc.scalar.copy)
+        gather_g(2, 0)
+        round_w(0, 0, nc.scalar.copy)
+        gather_g(2, 1)
+        round_g(0, 1, nc.scalar.copy)
+        quantize_w(0, 0)
+        round_g(0, 0, nc.scalar.copy)
+        quantize_w(0, 1)
+        round_g(1, 0, nc.vector.tensor_copy)
+        quantize_g(0, 1)
+        round_g(1, 1, nc.scalar.copy)
+        round_w(1, 0, nc.vector.tensor_copy)
+        quantize_g(0, 0)
+        round_x(2, nc.scalar.copy)
+        quantize_g(1, 0)
+        quantize_turned(x_codes[1], x_scales[1], x_turned[1], 0, 2, E4M3)
+        product_dh(0, 0)
+        quantize_g(1, 1)
+        product_dh(0, 2)
+        quantize_turned(x_codes[0], x_scales[0], x_turned[0], 0, 2, E4M3)
+        round_w(1, 1, nc.scalar.copy)
+        quantize_w(1, 0)
+        product_dh(0, 3)
+        mask_dh(0, 0)
+        product_dh(0, 1)
+        gather_x(2, 1)
+        product_dh(1, 0)
+        mask_dh(0, 2)
+        product_dh(1, 1)
+        mask_dh(0, 3)
+        gather_x(2, 0)
+        mask_dh(0, 1)
+        turn(("da", 0, 2), da[0][2:4])
+        quantize_w(1, 1)
+        mask_dh(1, 0)
+        turn(("da", 0, 0), da[0][0:2])
+        take(("da", 0, 2), da_turned[0][:, 2:4], nc.scalar.copy)
+        product_dh(1, 2)
+        mask_dh(1, 1)
+        product_dh(1, 3)
+        take(("da", 0, 0), da_turned[0][:, 0:2], nc.scalar.copy)
+        turn(("x", 0, 2), x_slots[0][2:3])
+        mask_dh(1, 2)
+        turn(("x", 1, 2), x_slots[1][2:3])
+        turn(("da", 1, 0), da[1][0:2])
+        take(("x", 0, 2), x_turned[0][:, 2:3], nc.scalar.copy)
+        quantize_turned(d_codes[0], d_scales[0], da_turned[0], 2, 4, E5M2)
+        take(("x", 1, 2), x_turned[1][:, 2:3], nc.scalar.copy)
+        quantize_turned(d_codes[0], d_scales[0], da_turned[0], 0, 2, E5M2)
+        turn(("da", 1, 2), da[1][2:3])
+        take(("da", 1, 0), da_turned[1][:, 0:2], nc.scalar.copy)
+        mask_dh(1, 3)
+        product_out(0, 0)
+        take(("da", 1, 2), da_turned[1][:, 2:3], nc.vector.tensor_copy)
+        quantize_turned(x_codes[1], x_scales[1], x_turned[1], 2, 3, E4M3)
+        turn(("da", 1, 3), da[1][3:4])
+        take_out(0, 0, nc.scalar.copy)
+        quantize_turned(x_codes[0], x_scales[0], x_turned[0], 2, 3, E4M3)
+        product_out(0, 1)
+        quantize_turned(d_codes[1], d_scales[1], da_turned[1], 2, 3, E5M2)
+        quantize_turned(d_codes[1], d_scales[1], da_turned[1], 0, 2, E5M2)
+        take(("da", 1, 3), da_turned[1][:, 3:4], nc.scalar.copy)
+        product_out(0, 2)
+        take_out(0, 1, nc.scalar.copy)
+        store(0, 0)
+        quantize_turned(d_codes[1], d_scales[1], da_turned[1], 3, 4, E5M2)
+        take_out(0, 2, nc.vector.tensor_copy)
+        product_out(1, 0)
+        store(0, 1)
+        product_out(1, 1)
+        product_out(1, 2)
+        take_out(1, 0, nc.scalar.copy)
+        store(0, 2)
+        take_out(1, 1, nc.vector.tensor_copy)
+        take_out(1, 2, nc.scalar.copy)
+        store(1, 0)
+        store(1, 1)
+        store(1, 2)

@@ -1,7 +1,6 @@
 from contextlib import ExitStack
 
 import concourse.mybir as mybir
-from concourse.masks import make_identity
 
 K, T, E, C, H, N = 384, 1024, 2, 512, 512, 512
 FLOPS = 2 * E * C * H * (N + K)
@@ -17,6 +16,7 @@ E5M2 = mybir.dt.float8_e5m2_x4
 COPY = mybir.ActivationFunctionType.Copy
 MULT = mybir.AluOpType.mult
 ADD = mybir.AluOpType.add
+IS_EQUAL = mybir.AluOpType.is_equal
 IS_GT = mybir.AluOpType.is_gt
 
 P = 128
@@ -25,6 +25,7 @@ KT = K // P
 HT = H // P
 OC = C // 16
 HALF = 2 * P
+QUAD = 32
 
 
 def interleave(copy, dst, src):
@@ -45,10 +46,10 @@ def tile_moe_mlp_relu_kernel(tc, xT, dyT, a, w2, gate, offs, out):
         dy = [held("dy%d" % t, [P, T], F32) for t in range(PACK)]
         x32 = [held("x32_%d" % k, [P, T], F32) for k in range(KT)]
         x16 = [held("x16_%d" % k, [P, T], BF16) for k in range(KT)]
-        w32 = [[held("w32_%d_%d" % (e, h), [P, PACK, HALF], F32) for h in range(2)] for e in range(E)]
+        w32 = [held("w32_%d" % e, [P, PACK, H], F32) for e in range(E)]
         pre = [[held("a%d_%d" % (e, h), [P, 2, C], F32) for h in range(2)] for e in range(E)]
         g32 = [held("g32_%d" % e, [P, PACK, C], F32) for e in range(E)]
-        g16 = [[held("g16_%d_%d" % (e, h), [P, HALF, PACK], BF16) for h in range(2)] for e in range(E)]
+        g16 = [held("g16_%d" % e, [P, C, PACK], BF16) for e in range(E)]
         w16 = [[held("w16_%d_%d" % (e, h), [P, HALF, PACK], BF16) for h in range(2)] for e in range(E)]
         g_codes = [held("gc%d" % e, [P, C], U32) for e in range(E)]
         g_scales = [held("gs%d" % e, [P, C], U8) for e in range(E)]
@@ -64,10 +65,21 @@ def tile_moe_mlp_relu_kernel(tc, xT, dyT, a, w2, gate, offs, out):
         d_scales = [held("ds%d" % e, [P, H], U8) for e in range(E)]
         results = [[held("res%d_%d" % (e, k), [P, H], F32) for k in range(KT)] for e in range(E)]
 
-        ident16 = held("ident16", [P, P], BF16)
         ident = held("ident", [P, P], F32)
-        make_identity(nc, ident16[:])
-        nc.scalar.activation(ident[:], ident16[:], COPY)
+        ones = held("ones", [P, QUAD], F32)
+        column = held("column", [P, QUAD], F32)
+        row = held("row", [P, QUAD], F32)
+        nc.vector.memset(ones[:], 1.0)
+        nc.vector.memset(ident[:], 0.0)
+        nc.vector.tensor_tensor_scan(column[:], ones[:], ones[:], 0.0, MULT, ADD)
+        nc.vector.transpose(row[:], column[:])
+        for q0 in range(0, P, QUAD):
+            part = slice(q0, q0 + QUAD)
+            nc.vector.tensor_tensor(ident[part, part], column[part, :], row[part, :], IS_EQUAL)
+        warm_in = held("warm_in", [P, 16], BF16)
+        warm_out = held("warm_out", [P, 16], BF16)
+        nc.vector.memset(warm_in[:], 0.0)
+        nc.scalar.activation(warm_out[:], warm_in[:], COPY)
 
         dy_rows = dyT.rearrange("(p t) c -> t p c", t=PACK)
 
@@ -77,33 +89,31 @@ def tile_moe_mlp_relu_kernel(tc, xT, dyT, a, w2, gate, offs, out):
         def load_dy(t):
             nc.sync.dma_start(dy[t][:], dy_rows[t])
 
-        def load_x(k):
-            nc.sync.dma_start(x32[k][:], xT[k * P:(k + 1) * P, :])
+        def load_x(k, c0, c1):
+            nc.sync.dma_start(x32[k][:, c0:c1], xT[k * P:(k + 1) * P, c0:c1])
 
-        def load_w(e, h):
-            cols = w2[e, :, h * HALF:(h + 1) * HALF]
-            nc.sync.dma_start(w32[e][h][:], cols.rearrange("(p t) i -> p t i", t=PACK))
+        def load_w(e):
+            nc.sync.dma_start(w32[e][:], w2[e].rearrange("(p t) i -> p t i", t=PACK))
 
         def load_a(e, h):
             rows = a[h * HALF:(h + 1) * HALF, e * C:(e + 1) * C]
             nc.sync.dma_start(pre[e][h][:], rows.rearrange("(b p) c -> p b c", p=P))
 
-        nc.sync.dma_start(offsets[:], offs)
-        load_x(0)
-        load_gate(1)
         load_dy(0)
-        load_x(1)
+        load_gate(1)
+        nc.sync.dma_start(offsets[:], offs)
         load_gate(0)
-        load_dy(3)
-        load_dy(1)
-        load_w(0, 1)
         load_dy(2)
-        load_w(0, 0)
+        load_x(1, 0, T)
+        load_dy(3)
+        load_x(0, 512, 1024)
+        load_x(0, 0, 512)
+        load_dy(1)
+        load_w(0)
         load_a(0, 0)
+        load_w(1)
+        load_x(2, 0, T)
         load_a(0, 1)
-        load_w(1, 0)
-        load_x(2)
-        load_w(1, 1)
         load_a(1, 0)
         load_a(1, 1)
 
@@ -116,14 +126,12 @@ def tile_moe_mlp_relu_kernel(tc, xT, dyT, a, w2, gate, offs, out):
         def slots(e):
             return offsets[:, e * OC:(e + 1) * OC]
 
-        def gpsimd_copy(out, in_):
-            nc.gpsimd.tensor_scalar(out, in_, 1.0, 0.0, MULT, ADD)
 
         def gather_g(t, e):
             nc.vector.tensor_tensor(g32[e][:, t, :], dy[t][:].indirect(slots(e)), gates[e][:], MULT)
 
-        def round_x(k, copy):
-            copy(out=x16[k][:], in_=x32[k][:])
+        def round_x(k, c0, c1, copy):
+            copy(out=x16[k][:, c0:c1], in_=x32[k][:, c0:c1])
 
         def gather_x(k, e):
             nc.scalar.activation(x_slots[e][k][:].rearrange("p u q -> p q u"), x16[k][:].indirect(slots(e)), COPY)
@@ -149,16 +157,16 @@ def tile_moe_mlp_relu_kernel(tc, xT, dyT, a, w2, gate, offs, out):
             return slice(h * HALF, (h + 1) * HALF)
 
         def round_w(e, h, copy):
-            interleave(copy, w16[e][h][:], w32[e][h][:])
+            interleave(copy, w16[e][h][:], w32[e][:, :, half(h)])
 
         def round_g(e, h, copy):
-            interleave(copy, g16[e][h][:], g32[e][:, :, half(h)])
+            interleave(copy, g16[e][:, half(h), :], g32[e][:, :, half(h)])
 
         def quantize_w(e, h):
             quantize(w_codes[e][:, half(h)], w_scales[e][:, half(h)], w16[e][h][:].rearrange("p i t -> p (i t)"), E4M3)
 
-        def quantize_g(e, h):
-            quantize(g_codes[e][:, half(h)], g_scales[e][:, half(h)], g16[e][h][:].rearrange("p c t -> p (c t)"), E5M2)
+        def quantize_g(e):
+            quantize(g_codes[e][:], g_scales[e][:], g16[e][:].rearrange("p c t -> p (c t)"), E5M2)
 
         def product_dh(e, b):
             cols = slice(b * P, (b + 1) * P)
@@ -183,97 +191,96 @@ def tile_moe_mlp_relu_kernel(tc, xT, dyT, a, w2, gate, offs, out):
         def store(e, k):
             nc.sync.dma_start(out[e, k * P:(k + 1) * P, :], results[e][k][:])
 
-        round_x(0, nc.vector.tensor_copy)
-        gather_x(0, 1)
-        gather_g(0, 1)
-        gather_x(0, 0)
         gather_g(0, 0)
-        round_x(1, nc.scalar.copy)
-        gather_g(3, 1)
-        gather_x(1, 0)
-        gather_g(3, 0)
-        gather_x(1, 1)
-        turn(("x", 0, 0), x_slots[0][0:2])
-        gather_g(1, 1)
-        round_w(0, 1, nc.scalar.copy)
-        turn(("x", 1, 0), x_slots[1][0:2])
-        gather_g(1, 0)
-        take(("x", 0, 0), x_turned[0][:, 0:2], nc.scalar.copy)
-        take(("x", 1, 0), x_turned[1][:, 0:2], nc.scalar.copy)
-        gather_g(2, 0)
-        round_w(0, 0, nc.scalar.copy)
+        gather_g(0, 1)
+        round_x(1, 0, T, nc.scalar.copy)
         gather_g(2, 1)
-        round_g(0, 1, nc.scalar.copy)
+        gather_x(1, 1)
+        gather_g(3, 1)
+        round_x(0, 0, 512, nc.scalar.copy)
+        gather_g(3, 0)
+        gather_g(2, 0)
+        round_x(0, 512, 1024, nc.scalar.copy)
+        gather_x(0, 1)
+        gather_x(1, 0)
+        gather_g(1, 0)
+        round_w(0, 0, nc.vector.tensor_copy)
+        gather_g(1, 1)
+        gather_x(0, 0)
+        round_g(0, 1, nc.vector.tensor_copy)
+        turn(("x", 0, 0), x_slots[0][0:2])
+        round_g(0, 0, nc.vector.tensor_copy)
+        turn(("x", 1, 0), x_slots[1][0:2])
+        quantize_g(0)
+        round_x(2, 0, T, nc.scalar.copy)
+        round_g(1, 1, nc.vector.tensor_copy)
+        take(("x", 0, 0), x_turned[0][:, 0:2], nc.scalar.copy)
         quantize_w(0, 0)
-        round_g(0, 0, nc.scalar.copy)
-        quantize_w(0, 1)
-        round_g(1, 0, nc.vector.tensor_copy)
-        quantize_g(0, 1)
-        round_g(1, 1, nc.scalar.copy)
-        round_w(1, 0, nc.vector.tensor_copy)
-        quantize_g(0, 0)
-        round_x(2, nc.scalar.copy)
-        quantize_g(1, 0)
-        quantize_turned(x_codes[1], x_scales[1], x_turned[1], 0, 2, E4M3)
+        take(("x", 1, 0), x_turned[1][:, 0:2], nc.scalar.copy)
+        round_w(0, 1, nc.vector.tensor_copy)
+        product_dh(0, 1)
+        round_w(1, 0, nc.scalar.copy)
         product_dh(0, 0)
-        quantize_g(1, 1)
-        product_dh(0, 2)
+        quantize_w(0, 1)
         quantize_turned(x_codes[0], x_scales[0], x_turned[0], 0, 2, E4M3)
-        round_w(1, 1, nc.scalar.copy)
-        quantize_w(1, 0)
+        product_dh(0, 2)
+        mask_dh(0, 1)
         product_dh(0, 3)
         mask_dh(0, 0)
-        product_dh(0, 1)
-        gather_x(2, 1)
-        product_dh(1, 0)
-        mask_dh(0, 2)
-        product_dh(1, 1)
+        quantize_turned(x_codes[1], x_scales[1], x_turned[1], 0, 2, E4M3)
+        round_g(1, 0, nc.scalar.copy)
+        round_w(1, 1, nc.scalar.copy)
+        turn(("da", 0, 0), da[0][0:2])
+        quantize_g(1)
+        take(("da", 0, 0), da_turned[0][:, 0:2], nc.scalar.copy)
         mask_dh(0, 3)
+        quantize_w(1, 0)
+        product_dh(1, 1)
+        mask_dh(0, 2)
+        mask_dh(1, 1)
+        product_dh(1, 0)
         gather_x(2, 0)
-        mask_dh(0, 1)
+        gather_x(2, 1)
         turn(("da", 0, 2), da[0][2:4])
         quantize_w(1, 1)
         mask_dh(1, 0)
-        turn(("da", 0, 0), da[0][0:2])
+        quantize_turned(d_codes[0], d_scales[0], da_turned[0], 0, 2, E5M2)
+        product_dh(1, 3)
         take(("da", 0, 2), da_turned[0][:, 2:4], nc.scalar.copy)
         product_dh(1, 2)
-        mask_dh(1, 1)
-        product_dh(1, 3)
-        take(("da", 0, 0), da_turned[0][:, 0:2], nc.scalar.copy)
-        turn(("x", 0, 2), x_slots[0][2:3])
-        mask_dh(1, 2)
-        turn(("x", 1, 2), x_slots[1][2:3])
-        turn(("da", 1, 0), da[1][0:2])
-        take(("x", 0, 2), x_turned[0][:, 2:3], nc.scalar.copy)
-        quantize_turned(d_codes[0], d_scales[0], da_turned[0], 2, 4, E5M2)
-        take(("x", 1, 2), x_turned[1][:, 2:3], nc.scalar.copy)
-        quantize_turned(d_codes[0], d_scales[0], da_turned[0], 0, 2, E5M2)
-        turn(("da", 1, 2), da[1][2:3])
-        take(("da", 1, 0), da_turned[1][:, 0:2], nc.scalar.copy)
         mask_dh(1, 3)
-        product_out(0, 0)
-        take(("da", 1, 2), da_turned[1][:, 2:3], nc.vector.tensor_copy)
-        quantize_turned(x_codes[1], x_scales[1], x_turned[1], 2, 3, E4M3)
+        turn(("da", 1, 0), da[1][0:2])
+        turn(("x", 0, 2), x_slots[0][2:3])
         turn(("da", 1, 3), da[1][3:4])
-        take_out(0, 0, nc.scalar.copy)
-        quantize_turned(x_codes[0], x_scales[0], x_turned[0], 2, 3, E4M3)
+        mask_dh(1, 2)
+        turn(("da", 1, 2), da[1][2:3])
+        quantize_turned(d_codes[0], d_scales[0], da_turned[0], 2, 4, E5M2)
+        take(("x", 0, 2), x_turned[0][:, 2:3], nc.scalar.copy)
+        turn(("x", 1, 2), x_slots[1][2:3])
+        take(("da", 1, 0), da_turned[1][:, 0:2], nc.scalar.copy)
+        product_out(0, 0)
+        take(("x", 1, 2), x_turned[1][:, 2:3], nc.vector.tensor_copy)
         product_out(0, 1)
-        quantize_turned(d_codes[1], d_scales[1], da_turned[1], 2, 3, E5M2)
         quantize_turned(d_codes[1], d_scales[1], da_turned[1], 0, 2, E5M2)
-        take(("da", 1, 3), da_turned[1][:, 3:4], nc.scalar.copy)
-        product_out(0, 2)
+        quantize_turned(x_codes[0], x_scales[0], x_turned[0], 2, 3, E4M3)
+        quantize_turned(x_codes[1], x_scales[1], x_turned[1], 2, 3, E4M3)
         take_out(0, 1, nc.scalar.copy)
+        product_out(0, 2)
+        take_out(0, 0, nc.scalar.copy)
         store(0, 0)
+        take(("da", 1, 3), da_turned[1][:, 3:4], nc.scalar.copy)
         quantize_turned(d_codes[1], d_scales[1], da_turned[1], 3, 4, E5M2)
         take_out(0, 2, nc.vector.tensor_copy)
-        product_out(1, 0)
         store(0, 1)
-        product_out(1, 1)
-        product_out(1, 2)
-        take_out(1, 0, nc.scalar.copy)
         store(0, 2)
-        take_out(1, 1, nc.vector.tensor_copy)
+        take(("da", 1, 2), da_turned[1][:, 2:3], nc.scalar.copy)
+        quantize_turned(d_codes[1], d_scales[1], da_turned[1], 2, 3, E5M2)
+        product_out(1, 0)
+        product_out(1, 2)
+        take_out(1, 0, nc.vector.tensor_copy)
         take_out(1, 2, nc.scalar.copy)
         store(1, 0)
-        store(1, 1)
         store(1, 2)
+        product_out(1, 1)
+        take_out(1, 1, nc.scalar.copy)
+        store(1, 1)

@@ -21,33 +21,36 @@ IS_GT = mybir.AluOpType.is_gt
 
 P = 128
 PACK = 4
-KT = K // P
-HT = H // P
-OC = C // 16
+K_TILES = K // P
+H_TILES = H // P
+LIST_COLS = C // 16
 HALF = 2 * P
 QUAD = 32
+BANKS = 8
 
 
 def interleave(copy, dst, src):
-    copy(out=dst.rearrange("p (c i) t -> p c t i", i=4), in_=src.rearrange("p t (c i) -> p c t i", i=4))
+    copy(out=dst.rearrange("p (c i) t -> p c t i", i=2), in_=src.rearrange("p t (c i) -> p c t i", i=2))
 
 
 def tile_moe_mlp_relu_kernel(tc, xT, dyT, a, w2, gate, offs, out):
     nc = tc.nc
+    on_scalar = nc.scalar.copy
+    on_vector = nc.vector.tensor_copy
     with ExitStack() as ctx:
         keep = ctx.enter_context(tc.tile_pool(name="keep", bufs=1))
-        psum = ctx.enter_context(tc.psum_pool(name="psum", bufs=8))
+        psum = ctx.enter_context(tc.psum_pool(name="psum", bufs=BANKS))
 
         def held(name, shape, dtype):
             return keep.tile(shape, dtype, name=name, align_bytes=64)
 
-        offsets = keep.tile([P, E * OC], U16, name="offsets")
+        offsets = keep.tile([P, E * LIST_COLS], U16, name="offsets")
         gates = [held("gate%d" % e, [P, C], F32) for e in range(E)]
         dy = [held("dy%d" % t, [P, T], F32) for t in range(PACK)]
-        x32 = [held("x32_%d" % k, [P, T], F32) for k in range(KT)]
-        x16 = [held("x16_%d" % k, [P, T], BF16) for k in range(KT)]
+        x32 = [held("x32_%d" % k, [P, T], F32) for k in range(K_TILES)]
+        x16 = [held("x16_%d" % k, [P, T], BF16) for k in range(K_TILES)]
         w32 = [held("w32_%d" % e, [P, PACK, H], F32) for e in range(E)]
-        pre = [[held("a%d_%d" % (e, h), [P, 2, C], F32) for h in range(2)] for e in range(E)]
+        saved = [[held("a%d_%d" % (e, h), [P, 2, C], F32) for h in range(2)] for e in range(E)]
         g32 = [held("g32_%d" % e, [P, PACK, C], F32) for e in range(E)]
         g16 = [held("g16_%d" % e, [P, C, PACK], BF16) for e in range(E)]
         w16 = [[held("w16_%d_%d" % (e, h), [P, HALF, PACK], BF16) for h in range(2)] for e in range(E)]
@@ -55,31 +58,27 @@ def tile_moe_mlp_relu_kernel(tc, xT, dyT, a, w2, gate, offs, out):
         g_scales = [held("gs%d" % e, [P, C], U8) for e in range(E)]
         w_codes = [held("wc%d" % e, [P, H], U32) for e in range(E)]
         w_scales = [held("ws%d" % e, [P, H], U8) for e in range(E)]
-        x_slots = [[held("xs%d_%d" % (e, k), [P, 2, C // 2], BF16) for k in range(KT)] for e in range(E)]
-        x_turned = [held("xt%d" % e, [P, KT, P, 2], F32) for e in range(E)]
+        x_slots = [[held("xs%d_%d" % (e, k), [P, 2, C // 2], BF16) for k in range(K_TILES)] for e in range(E)]
+        x_turned = [held("xt%d" % e, [P, K_TILES, P, 2], F32) for e in range(E)]
         x_codes = [held("xc%d" % e, [P, K], U32) for e in range(E)]
         x_scales = [held("xsc%d" % e, [P, K], U8) for e in range(E)]
-        da = [[held("da%d_%d" % (e, b), [P, 2, C // 2], BF16) for b in range(HT)] for e in range(E)]
-        da_turned = [held("dt%d" % e, [P, HT, P, 2], F32) for e in range(E)]
-        d_codes = [held("dc%d" % e, [P, H], U32) for e in range(E)]
-        d_scales = [held("ds%d" % e, [P, H], U8) for e in range(E)]
-        results = [[held("res%d_%d" % (e, k), [P, H], F32) for k in range(KT)] for e in range(E)]
+        da = [[held("da%d_%d" % (e, b), [P, C], BF16) for b in range(H_TILES)] for e in range(E)]
+        da_turned = [held("dt%d" % e, [P, H_TILES, P, 2], F32) for e in range(E)]
+        da_codes = [held("dc%d" % e, [P, H], U32) for e in range(E)]
+        da_scales = [held("ds%d" % e, [P, H], U8) for e in range(E)]
+        results = [[held("res%d_%d" % (e, k), [P, H], F32) for k in range(K_TILES)] for e in range(E)]
 
         ident = held("ident", [P, P], F32)
         ones = held("ones", [P, QUAD], F32)
         column = held("column", [P, QUAD], F32)
         row = held("row", [P, QUAD], F32)
-        nc.vector.memset(ones[:], 1.0)
         nc.vector.memset(ident[:], 0.0)
+        nc.scalar.activation(ones[:], ident[:, 0:QUAD], COPY, bias=1.0)
         nc.vector.tensor_tensor_scan(column[:], ones[:], ones[:], 0.0, MULT, ADD)
         nc.vector.transpose(row[:], column[:])
         for q0 in range(0, P, QUAD):
             part = slice(q0, q0 + QUAD)
             nc.vector.tensor_tensor(ident[part, part], column[part, :], row[part, :], IS_EQUAL)
-        warm_in = held("warm_in", [P, 16], BF16)
-        warm_out = held("warm_out", [P, 16], BF16)
-        nc.vector.memset(warm_in[:], 0.0)
-        nc.scalar.activation(warm_out[:], warm_in[:], COPY)
 
         dy_rows = dyT.rearrange("(p t) c -> t p c", t=PACK)
 
@@ -97,22 +96,22 @@ def tile_moe_mlp_relu_kernel(tc, xT, dyT, a, w2, gate, offs, out):
 
         def load_a(e, h):
             rows = a[h * HALF:(h + 1) * HALF, e * C:(e + 1) * C]
-            nc.sync.dma_start(pre[e][h][:], rows.rearrange("(b p) c -> p b c", p=P))
+            nc.sync.dma_start(saved[e][h][:], rows.rearrange("(b p) c -> p b c", p=P))
 
-        load_dy(0)
-        load_gate(1)
-        nc.sync.dma_start(offsets[:], offs)
         load_gate(0)
-        load_dy(2)
-        load_x(1, 0, T)
-        load_dy(3)
-        load_x(0, 512, 1024)
-        load_x(0, 0, 512)
         load_dy(1)
+        nc.sync.dma_start(offsets[:], offs)
+        load_x(1, 0, T)
+        load_gate(1)
+        load_dy(0)
+        load_dy(3)
+        load_x(2, 0, T)
+        load_x(0, 0, T // 2)
+        load_dy(2)
         load_w(0)
         load_a(0, 0)
         load_w(1)
-        load_x(2, 0, T)
+        load_x(0, T // 2, T)
         load_a(0, 1)
         load_a(1, 0)
         load_a(1, 1)
@@ -124,49 +123,28 @@ def tile_moe_mlp_relu_kernel(tc, xT, dyT, a, w2, gate, offs, out):
             return banks[key]
 
         def slots(e):
-            return offsets[:, e * OC:(e + 1) * OC]
-
-
-        def gather_g(t, e):
-            nc.vector.tensor_tensor(g32[e][:, t, :], dy[t][:].indirect(slots(e)), gates[e][:], MULT)
-
-        def round_x(k, c0, c1, copy):
-            copy(out=x16[k][:, c0:c1], in_=x32[k][:, c0:c1])
-
-        def gather_x(k, e):
-            nc.scalar.activation(x_slots[e][k][:].rearrange("p u q -> p q u"), x16[k][:].indirect(slots(e)), COPY)
-
-        def turn(key, sources):
-            bank = new_bank(key, [P, len(sources), 2, P])
-            for j, source in enumerate(sources):
-                for u in range(2):
-                    nc.tensor.transpose(bank[:, j, u, :], source[:, u, :].bitcast(F32), ident[:])
-
-        def take(key, turned, copy):
-            copy(out=turned, in_=banks[key][:].rearrange("p j u m -> p j m u"))
-
-        def quantize(codes, scales, values, fmt):
-            nc.vector.quantize_mx(out=codes.bitcast(fmt), scales=scales, in_=values)
-
-        def quantize_turned(codes, scales, turned, j0, j1, fmt):
-            cols = slice(P * j0, P * j1)
-            values = turned[:, j0:j1].rearrange("p j m u -> p (j m u)").bitcast(BF16)
-            quantize(codes[:, cols], scales[:, cols], values, fmt)
+            return offsets[:, e * LIST_COLS:(e + 1) * LIST_COLS]
 
         def half(h):
             return slice(h * HALF, (h + 1) * HALF)
 
-        def round_w(e, h, copy):
-            interleave(copy, w16[e][h][:], w32[e][:, :, half(h)])
+        def quantize(codes, scales, values, fmt):
+            nc.vector.quantize_mx(out=codes.bitcast(fmt), scales=scales, in_=values)
+
+        def gather_g(t, e):
+            nc.vector.tensor_tensor(g32[e][:, t, :], dy[t][:].indirect(slots(e)), gates[e][:], MULT)
 
         def round_g(e, h, copy):
             interleave(copy, g16[e][:, half(h), :], g32[e][:, :, half(h)])
 
-        def quantize_w(e, h):
-            quantize(w_codes[e][:, half(h)], w_scales[e][:, half(h)], w16[e][h][:].rearrange("p i t -> p (i t)"), E4M3)
+        def round_w(e, h, copy):
+            interleave(copy, w16[e][h][:], w32[e][:, :, half(h)])
 
         def quantize_g(e):
             quantize(g_codes[e][:], g_scales[e][:], g16[e][:].rearrange("p c t -> p (c t)"), E5M2)
+
+        def quantize_w(e, h):
+            quantize(w_codes[e][:, half(h)], w_scales[e][:, half(h)], w16[e][h][:].rearrange("p i t -> p (i t)"), E4M3)
 
         def product_dh(e, b):
             cols = slice(b * P, (b + 1) * P)
@@ -176,14 +154,51 @@ def tile_moe_mlp_relu_kernel(tc, xT, dyT, a, w2, gate, offs, out):
 
         def mask_dh(e, b):
             nc.vector.scalar_tensor_tensor(
-                da[e][b][:], pre[e][b // 2][:, b % 2, :].rearrange("p (q u) -> p u q", u=2), 0.0,
-                banks[("dh", e, b)][:].rearrange("p (q u) -> p u q", u=2), IS_GT, MULT)
+                da[e][b][:], saved[e][b // 2][:, b % 2, :], 0.0, banks[("dh", e, b)][:], IS_GT, MULT)
+
+        def round_x(k, c0, c1, copy):
+            copy(out=x16[k][:, c0:c1], in_=x32[k][:, c0:c1])
+
+        def gather_x(k, e):
+            nc.scalar.activation(x_slots[e][k][:].rearrange("p u (r s) -> p r u s", s=2), x16[k][:].indirect(slots(e)), COPY)
+
+        def turn(key, pairs):
+            bank = new_bank(key, [P, len(pairs), 2, P])
+            for j, words in enumerate(pairs):
+                for u in range(2):
+                    nc.tensor.transpose(bank[:, j, u, :], words[u], ident[:])
+
+        def turn_x(e, j0, j1):
+            turn(("x", e, j0), [[x_slots[e][k][:, u, :].bitcast(F32) for u in range(2)] for k in range(j0, j1)])
+
+        def turn_da(e, j0, j1):
+            turn(("da", e, j0), [[da[e][b][:].bitcast(F32)[:, u:C // 2:2] for u in range(2)] for b in range(j0, j1)])
+
+        def take(key, turned, copy):
+            copy(out=turned, in_=banks[key][:].rearrange("p j u m -> p j m u"))
+
+        def take_x(e, j0, j1, copy):
+            take(("x", e, j0), x_turned[e][:, j0:j1], copy)
+
+        def take_da(e, j0, j1, copy):
+            take(("da", e, j0), da_turned[e][:, j0:j1], copy)
+
+        def quantize_turned(codes, scales, turned, j0, j1, fmt):
+            cols = slice(P * j0, P * j1)
+            values = turned[:, j0:j1].rearrange("p j m u -> p (j m u)").bitcast(BF16)
+            quantize(codes[:, cols], scales[:, cols], values, fmt)
+
+        def quantize_x(e, j0, j1):
+            quantize_turned(x_codes[e], x_scales[e], x_turned[e], j0, j1, E4M3)
+
+        def quantize_da(e, j0, j1):
+            quantize_turned(da_codes[e], da_scales[e], da_turned[e], j0, j1, E5M2)
 
         def product_out(e, k):
             cols = slice(k * P, (k + 1) * P)
             acc = new_bank(("out", e, k), [P, H])
             nc.tensor.matmul_mx(out=acc[:], lhsT=x_codes[e][:, cols].bitcast(E4M3), lhsT_scale=x_scales[e][:, cols],
-                                rhs=d_codes[e][:].bitcast(E5M2), rhs_scale=d_scales[e][:], start=True, stop=True)
+                                rhs=da_codes[e][:].bitcast(E5M2), rhs_scale=da_scales[e][:], start=True, stop=True)
 
         def take_out(e, k, copy):
             copy(out=results[e][k][:], in_=banks[("out", e, k)][:])
@@ -191,96 +206,96 @@ def tile_moe_mlp_relu_kernel(tc, xT, dyT, a, w2, gate, offs, out):
         def store(e, k):
             nc.sync.dma_start(out[e, k * P:(k + 1) * P, :], results[e][k][:])
 
-        gather_g(0, 0)
-        gather_g(0, 1)
-        round_x(1, 0, T, nc.scalar.copy)
-        gather_g(2, 1)
-        gather_x(1, 1)
-        gather_g(3, 1)
-        round_x(0, 0, 512, nc.scalar.copy)
-        gather_g(3, 0)
-        gather_g(2, 0)
-        round_x(0, 512, 1024, nc.scalar.copy)
-        gather_x(0, 1)
-        gather_x(1, 0)
         gather_g(1, 0)
-        round_w(0, 0, nc.vector.tensor_copy)
+        round_x(1, 0, T, on_scalar)
         gather_g(1, 1)
-        gather_x(0, 0)
-        round_g(0, 1, nc.vector.tensor_copy)
-        turn(("x", 0, 0), x_slots[0][0:2])
-        round_g(0, 0, nc.vector.tensor_copy)
-        turn(("x", 1, 0), x_slots[1][0:2])
-        quantize_g(0)
-        round_x(2, 0, T, nc.scalar.copy)
-        round_g(1, 1, nc.vector.tensor_copy)
-        take(("x", 0, 0), x_turned[0][:, 0:2], nc.scalar.copy)
-        quantize_w(0, 0)
-        take(("x", 1, 0), x_turned[1][:, 0:2], nc.scalar.copy)
-        round_w(0, 1, nc.vector.tensor_copy)
-        product_dh(0, 1)
-        round_w(1, 0, nc.scalar.copy)
-        product_dh(0, 0)
-        quantize_w(0, 1)
-        quantize_turned(x_codes[0], x_scales[0], x_turned[0], 0, 2, E4M3)
-        product_dh(0, 2)
-        mask_dh(0, 1)
-        product_dh(0, 3)
-        mask_dh(0, 0)
-        quantize_turned(x_codes[1], x_scales[1], x_turned[1], 0, 2, E4M3)
-        round_g(1, 0, nc.scalar.copy)
-        round_w(1, 1, nc.scalar.copy)
-        turn(("da", 0, 0), da[0][0:2])
-        quantize_g(1)
-        take(("da", 0, 0), da_turned[0][:, 0:2], nc.scalar.copy)
-        mask_dh(0, 3)
-        quantize_w(1, 0)
-        product_dh(1, 1)
-        mask_dh(0, 2)
-        mask_dh(1, 1)
-        product_dh(1, 0)
-        gather_x(2, 0)
+        gather_x(1, 1)
+        gather_g(0, 1)
+        gather_x(1, 0)
+        gather_g(0, 0)
+        round_x(2, 0, T, on_scalar)
+        gather_g(3, 0)
+        round_x(0, 0, T // 2, on_scalar)
+        gather_g(3, 1)
         gather_x(2, 1)
-        turn(("da", 0, 2), da[0][2:4])
+        gather_g(2, 0)
+        gather_x(2, 0)
+        turn_x(1, 2, 3)
+        gather_g(2, 1)
+        round_g(0, 0, on_scalar)
+        turn_x(0, 2, 3)
+        round_g(0, 1, on_vector)
+        round_g(1, 1, on_vector)
+        round_g(1, 0, on_scalar)
+        quantize_g(0)
+        round_w(0, 0, on_vector)
+        take_x(1, 2, 3, on_scalar)
+        quantize_g(1)
+        take_x(0, 2, 3, on_scalar)
+        round_w(1, 0, on_scalar)
+        quantize_w(0, 0)
+        round_w(0, 1, on_vector)
+        product_dh(0, 1)
+        quantize_x(1, 2, 3)
+        quantize_x(0, 2, 3)
+        product_dh(0, 0)
+        round_x(0, T // 2, T, on_scalar)
+        quantize_w(0, 1)
+        mask_dh(0, 1)
+        round_w(1, 1, on_scalar)
+        product_dh(0, 2)
+        mask_dh(0, 0)
+        product_dh(0, 3)
+        quantize_w(1, 0)
+        mask_dh(0, 2)
+        turn_da(0, 0, 2)
+        gather_x(0, 0)
+        product_dh(1, 1)
+        mask_dh(0, 3)
+        product_dh(1, 0)
+        take_da(0, 0, 2, on_scalar)
         quantize_w(1, 1)
-        mask_dh(1, 0)
-        quantize_turned(d_codes[0], d_scales[0], da_turned[0], 0, 2, E5M2)
+        mask_dh(1, 1)
+        turn_da(0, 2, 4)
+        gather_x(0, 1)
         product_dh(1, 3)
-        take(("da", 0, 2), da_turned[0][:, 2:4], nc.scalar.copy)
+        mask_dh(1, 0)
         product_dh(1, 2)
+        turn_x(0, 0, 2)
+        take_da(0, 2, 4, on_scalar)
+        quantize_da(0, 0, 2)
         mask_dh(1, 3)
-        turn(("da", 1, 0), da[1][0:2])
-        turn(("x", 0, 2), x_slots[0][2:3])
-        turn(("da", 1, 3), da[1][3:4])
+        turn_x(1, 0, 2)
+        take_x(0, 0, 2, on_scalar)
+        turn_da(1, 0, 2)
         mask_dh(1, 2)
-        turn(("da", 1, 2), da[1][2:3])
-        quantize_turned(d_codes[0], d_scales[0], da_turned[0], 2, 4, E5M2)
-        take(("x", 0, 2), x_turned[0][:, 2:3], nc.scalar.copy)
-        turn(("x", 1, 2), x_slots[1][2:3])
-        take(("da", 1, 0), da_turned[1][:, 0:2], nc.scalar.copy)
-        product_out(0, 0)
-        take(("x", 1, 2), x_turned[1][:, 2:3], nc.vector.tensor_copy)
-        product_out(0, 1)
-        quantize_turned(d_codes[1], d_scales[1], da_turned[1], 0, 2, E5M2)
-        quantize_turned(x_codes[0], x_scales[0], x_turned[0], 2, 3, E4M3)
-        quantize_turned(x_codes[1], x_scales[1], x_turned[1], 2, 3, E4M3)
-        take_out(0, 1, nc.scalar.copy)
+        turn_da(1, 3, 4)
+        take_x(1, 0, 2, on_scalar)
+        quantize_da(0, 2, 4)
+        quantize_x(0, 0, 2)
+        turn_da(1, 2, 3)
+        take_da(1, 0, 2, on_scalar)
         product_out(0, 2)
-        take_out(0, 0, nc.scalar.copy)
-        store(0, 0)
-        take(("da", 1, 3), da_turned[1][:, 3:4], nc.scalar.copy)
-        quantize_turned(d_codes[1], d_scales[1], da_turned[1], 3, 4, E5M2)
-        take_out(0, 2, nc.vector.tensor_copy)
-        store(0, 1)
-        store(0, 2)
-        take(("da", 1, 2), da_turned[1][:, 2:3], nc.scalar.copy)
-        quantize_turned(d_codes[1], d_scales[1], da_turned[1], 2, 3, E5M2)
+        quantize_x(1, 0, 2)
+        take_da(1, 3, 4, on_vector)
+        take_da(1, 2, 3, on_scalar)
+        product_out(0, 0)
+        quantize_da(1, 0, 2)
+        take_out(0, 2, on_scalar)
+        quantize_da(1, 3, 4)
+        product_out(0, 1)
+        quantize_da(1, 2, 3)
+        take_out(0, 0, on_scalar)
         product_out(1, 0)
-        product_out(1, 2)
-        take_out(1, 0, nc.vector.tensor_copy)
-        take_out(1, 2, nc.scalar.copy)
-        store(1, 0)
-        store(1, 2)
+        store(0, 2)
         product_out(1, 1)
-        take_out(1, 1, nc.scalar.copy)
+        take_out(0, 1, on_vector)
+        product_out(1, 2)
+        take_out(1, 0, on_scalar)
+        store(0, 0)
+        take_out(1, 1, on_vector)
+        store(0, 1)
+        take_out(1, 2, on_vector)
+        store(1, 0)
         store(1, 1)
+        store(1, 2)

@@ -30,7 +30,7 @@ BANKS = 8
 
 
 def interleave(copy, dst, src):
-    copy(out=dst.rearrange("p (c i) t -> p c t i", i=2), in_=src.rearrange("p t (c i) -> p c t i", i=2))
+    copy(out=dst.rearrange("p (c i) t -> p c t i", i=4), in_=src.rearrange("p t (c i) -> p c t i", i=4))
 
 
 def tile_moe_mlp_relu_kernel(tc, xT, dyT, a, w2, gate, offs, out):

@@ -51,7 +51,7 @@ def tile_moe_mlp_relu_kernel(tc, xT, dyT, a, w2, gate, offs, out):
         x16 = [held("x16_%d" % k, [P, T], BF16) for k in range(K_TILES)]
         w32 = [held("w32_%d" % e, [P, PACK, H], F32) for e in range(E)]
         saved = [[held("a%d_%d" % (e, h), [P, 2, C], F32) for h in range(2)] for e in range(E)]
-        g32 = [held("g32_%d" % e, [P, PACK, C], F32) for e in range(E)]
+        g32 = [keep.tile([P, PACK, C], F32, name="g32_%d" % e, tag="g32_%d" % e, align_bytes=64) for e in range(E)]
         g16 = [held("g16_%d" % e, [P, C, PACK], BF16) for e in range(E)]
         w16 = [[held("w16_%d_%d" % (e, h), [P, HALF, PACK], BF16) for h in range(2)] for e in range(E)]
         g_codes = [held("gc%d" % e, [P, C], U32) for e in range(E)]
@@ -59,7 +59,8 @@ def tile_moe_mlp_relu_kernel(tc, xT, dyT, a, w2, gate, offs, out):
         w_codes = [held("wc%d" % e, [P, H], U32) for e in range(E)]
         w_scales = [held("ws%d" % e, [P, H], U8) for e in range(E)]
         x_slots = [[held("xs%d_%d" % (e, k), [P, 2, C // 2], BF16) for k in range(K_TILES)] for e in range(E)]
-        x_turned = [held("xt%d" % e, [P, K_TILES, P, 2], F32) for e in range(E)]
+        x_turned = {}
+        gate_column = held("gate_column", [P, PACK], F32)
         x_codes = [held("xc%d" % e, [P, K], U32) for e in range(E)]
         x_scales = [held("xsc%d" % e, [P, K], U8) for e in range(E)]
         da = [[held("da%d_%d" % (e, b), [P, C], BF16) for b in range(H_TILES)] for e in range(E)]
@@ -72,8 +73,8 @@ def tile_moe_mlp_relu_kernel(tc, xT, dyT, a, w2, gate, offs, out):
         ones = held("ones", [P, QUAD], F32)
         column = held("column", [P, QUAD], F32)
         row = held("row", [P, QUAD], F32)
+        nc.vector.memset(ones[:], 1.0)
         nc.vector.memset(ident[:], 0.0)
-        nc.scalar.activation(ones[:], ident[:, 0:QUAD], COPY, bias=1.0)
         nc.vector.tensor_tensor_scan(column[:], ones[:], ones[:], 0.0, MULT, ADD)
         nc.vector.transpose(row[:], column[:])
         for q0 in range(0, P, QUAD):
@@ -82,8 +83,11 @@ def tile_moe_mlp_relu_kernel(tc, xT, dyT, a, w2, gate, offs, out):
 
         dy_rows = dyT.rearrange("(p t) c -> t p c", t=PACK)
 
-        def load_gate(e):
-            nc.sync.dma_start(gates[e][:], gate[0:P, e * C:(e + 1) * C])
+        def load_gate(c0, c1):
+            nc.sync.dma_start(gates[0][:, c0:c1], gate[0:P, c0:c1])
+
+        def load_gate_column():
+            nc.sync.dma_start(gate_column[:], gate[0, C:2 * C].rearrange("(n q) -> n q", q=PACK))
 
         def load_dy(t):
             nc.sync.dma_start(dy[t][:], dy_rows[t])
@@ -98,23 +102,24 @@ def tile_moe_mlp_relu_kernel(tc, xT, dyT, a, w2, gate, offs, out):
             rows = a[h * HALF:(h + 1) * HALF, e * C:(e + 1) * C]
             nc.sync.dma_start(saved[e][h][:], rows.rearrange("(b p) c -> p b c", p=P))
 
-        load_gate(0)
-        load_dy(1)
         nc.sync.dma_start(offsets[:], offs)
-        load_x(1, 0, T)
-        load_gate(1)
+        load_gate_column()
         load_dy(0)
-        load_dy(3)
-        load_x(2, 0, T)
-        load_x(0, 0, T // 2)
+        load_gate(0, P)
+        load_gate(P, C)
+        load_x(0,0,1024)
+        load_dy(1)
+        load_x(1,0,1024)
         load_dy(2)
+        load_x(2,0,512)
+        load_dy(3)
         load_w(0)
-        load_a(0, 0)
+        load_a(0,0)
         load_w(1)
-        load_x(0, T // 2, T)
-        load_a(0, 1)
-        load_a(1, 0)
-        load_a(1, 1)
+        load_x(2,512,1024)
+        load_a(0,1)
+        load_a(1,0)
+        load_a(1,1)
 
         banks = {}
 
@@ -122,8 +127,14 @@ def tile_moe_mlp_relu_kernel(tc, xT, dyT, a, w2, gate, offs, out):
             banks[key] = psum.tile(shape, F32, name="bank")
             return banks[key]
 
-        def slots(e):
-            return offsets[:, e * LIST_COLS:(e + 1) * LIST_COLS]
+        def slots(e, c0=0, c1=C):
+            return offsets[:, (e * C + c0) // 16:(e * C + c1) // 16]
+
+        def spread_gate():
+            bank = new_bank("gate", [P, PACK, P])
+            for q in range(PACK):
+                nc.tensor.transpose(bank[:, q, :], gate_column[:, q:q + 1].to_broadcast([P, P]), ident[:])
+            nc.scalar.activation(gates[1][:].rearrange("p (n q) -> p n q", q=PACK), bank[:].rearrange("p q n -> p n q"), COPY)
 
         def half(h):
             return slice(h * HALF, (h + 1) * HALF)
@@ -131,8 +142,8 @@ def tile_moe_mlp_relu_kernel(tc, xT, dyT, a, w2, gate, offs, out):
         def quantize(codes, scales, values, fmt):
             nc.vector.quantize_mx(out=codes.bitcast(fmt), scales=scales, in_=values)
 
-        def gather_g(t, e):
-            nc.vector.tensor_tensor(g32[e][:, t, :], dy[t][:].indirect(slots(e)), gates[e][:], MULT)
+        def gather_g(t, e, c0=0, c1=C):
+            nc.vector.tensor_tensor(g32[e][:, t, c0:c1], dy[t][:].indirect(slots(e, c0, c1)), gates[e][:, c0:c1], MULT)
 
         def round_g(e, h, copy):
             interleave(copy, g16[e][:, half(h), :], g32[e][:, :, half(h)])
@@ -178,6 +189,8 @@ def tile_moe_mlp_relu_kernel(tc, xT, dyT, a, w2, gate, offs, out):
             copy(out=turned, in_=banks[key][:].rearrange("p j u m -> p j m u"))
 
         def take_x(e, j0, j1, copy):
+            if j0 == 0:
+                x_turned[e] = keep.tile([P, K_TILES, P, 2], F32, name="xt%d" % e, tag="g32_%d" % e, align_bytes=64)
             take(("x", e, j0), x_turned[e][:, j0:j1], copy)
 
         def take_da(e, j0, j1, copy):
@@ -206,96 +219,74 @@ def tile_moe_mlp_relu_kernel(tc, xT, dyT, a, w2, gate, offs, out):
         def store(e, k):
             nc.sync.dma_start(out[e, k * P:(k + 1) * P, :], results[e][k][:])
 
-        gather_g(1, 0)
-        round_x(1, 0, T, on_scalar)
-        gather_g(1, 1)
-        gather_x(1, 1)
-        gather_g(0, 1)
-        gather_x(1, 0)
-        gather_g(0, 0)
-        round_x(2, 0, T, on_scalar)
-        gather_g(3, 0)
-        round_x(0, 0, T // 2, on_scalar)
-        gather_g(3, 1)
-        gather_x(2, 1)
-        gather_g(2, 0)
-        gather_x(2, 0)
-        turn_x(1, 2, 3)
-        gather_g(2, 1)
-        round_g(0, 0, on_scalar)
-        turn_x(0, 2, 3)
-        round_g(0, 1, on_vector)
-        round_g(1, 1, on_vector)
-        round_g(1, 0, on_scalar)
+        spread_gate()
+        gather_g(0, 0, 0, P)
+        gather_g(0, 0, P, C)
+        gather_g(0,1)
+        for t in range(1,4):
+            for e in range(2):
+                gather_g(t,e)
+        for k in range(2):
+            round_x(k,0,1024,on_scalar)
+            for e in range(2):
+                gather_x(k,e)
+        round_x(2,0,512,on_scalar)
+        for e in range(2):
+            round_g(e,0,on_scalar)
+            round_g(e,1,on_vector)
         quantize_g(0)
-        round_w(0, 0, on_vector)
-        take_x(1, 2, 3, on_scalar)
+        round_w(0,0,on_vector)
         quantize_g(1)
-        take_x(0, 2, 3, on_scalar)
-        round_w(1, 0, on_scalar)
-        quantize_w(0, 0)
-        round_w(0, 1, on_vector)
-        product_dh(0, 1)
-        quantize_x(1, 2, 3)
-        quantize_x(0, 2, 3)
-        product_dh(0, 0)
-        round_x(0, T // 2, T, on_scalar)
-        quantize_w(0, 1)
-        mask_dh(0, 1)
-        round_w(1, 1, on_scalar)
-        product_dh(0, 2)
-        mask_dh(0, 0)
-        product_dh(0, 3)
-        quantize_w(1, 0)
-        mask_dh(0, 2)
-        turn_da(0, 0, 2)
-        gather_x(0, 0)
-        product_dh(1, 1)
-        mask_dh(0, 3)
-        product_dh(1, 0)
-        take_da(0, 0, 2, on_scalar)
-        quantize_w(1, 1)
-        mask_dh(1, 1)
-        turn_da(0, 2, 4)
-        gather_x(0, 1)
-        product_dh(1, 3)
-        mask_dh(1, 0)
-        product_dh(1, 2)
-        turn_x(0, 0, 2)
-        take_da(0, 2, 4, on_scalar)
-        quantize_da(0, 0, 2)
-        mask_dh(1, 3)
-        turn_x(1, 0, 2)
-        take_x(0, 0, 2, on_scalar)
-        turn_da(1, 0, 2)
-        mask_dh(1, 2)
-        turn_da(1, 3, 4)
-        take_x(1, 0, 2, on_scalar)
-        quantize_da(0, 2, 4)
-        quantize_x(0, 0, 2)
-        turn_da(1, 2, 3)
-        take_da(1, 0, 2, on_scalar)
-        product_out(0, 2)
-        quantize_x(1, 0, 2)
-        take_da(1, 3, 4, on_vector)
-        take_da(1, 2, 3, on_scalar)
-        product_out(0, 0)
-        quantize_da(1, 0, 2)
-        take_out(0, 2, on_scalar)
-        quantize_da(1, 3, 4)
-        product_out(0, 1)
-        quantize_da(1, 2, 3)
-        take_out(0, 0, on_scalar)
-        product_out(1, 0)
-        store(0, 2)
-        product_out(1, 1)
-        take_out(0, 1, on_vector)
-        product_out(1, 2)
-        take_out(1, 0, on_scalar)
-        store(0, 0)
-        take_out(1, 1, on_vector)
-        store(0, 1)
-        take_out(1, 2, on_vector)
-        store(1, 0)
-        store(1, 1)
-        store(1, 2)
+        quantize_w(0,0)
+        round_w(0,1,on_vector)
+        for e in range(2):
+            turn_x(e,0,2)
+            take_x(e,0,2,on_scalar)
+        quantize_x(0,0,2)
+        quantize_w(0,1)
+        round_w(1,0,on_scalar)
+        round_x(2,512,1024,on_scalar)
+        round_w(1,1,on_scalar)
+        for b in range(2):
+            product_dh(0,b)
+            mask_dh(0,b)
+        quantize_w(1,0)
+        for b in range(2,4):
+            product_dh(0,b)
+            mask_dh(0,b)
+        quantize_w(1,1)
+        turn_da(0,0,2)
+        gather_x(2,0)
+        for b in range(2):
+            product_dh(1,b)
+            mask_dh(1,b)
+        take_da(0,0,2,on_scalar)
+        turn_da(0,2,4)
+        gather_x(2,1)
+        quantize_da(0,0,2)
+        for b in range(2,4):
+            product_dh(1,b)
+            mask_dh(1,b)
+        take_da(0,2,4,on_scalar)
+        quantize_da(0,2,4)
+        quantize_x(1,0,2)
+        turn_x(0,2,3)
+        take_x(0,2,3,on_scalar)
+        quantize_x(0,2,3)
+        turn_da(1,0,2)
+        take_da(1,0,2,on_scalar)
+        turn_x(1,2,3)
+        take_x(1,2,3,on_scalar)
+        turn_da(1,2,3)
+        take_da(1,2,3,on_scalar)
+        turn_da(1,3,4)
+        take_da(1,3,4,on_vector)
+        quantize_da(1,0,2)
+        quantize_x(1,2,3)
+        quantize_da(1,2,3)
+        quantize_da(1,3,4)
+        for e in range(2):
+            for k in range(3):
+                product_out(e,k)
+                take_out(e,k,on_vector if e==1 and k!=1 else on_scalar)
+                store(e,k)

@@ -50,7 +50,7 @@ def tile_moe_mlp_relu_kernel(tc, xT, dyT, a, w2, gate, offs, out):
         x32 = [held("x32_%d" % k, [P, T], F32) for k in range(K_TILES)]
         x16 = [held("x16_%d" % k, [P, T], BF16) for k in range(K_TILES)]
         w32 = [held("w32_%d" % e, [P, PACK, H], F32) for e in range(E)]
-        saved = [[held("a%d_%d" % (e, h), [P, 2, C], F32) for h in range(2)] for e in range(E)]
+        saved = [[keep.tile([P, 2, C], F32, name="a%d_%d" % (e, h), tag="a%d_%d" % (e, h), align_bytes=64) for h in range(2)] for e in range(E)]
         g32 = [keep.tile([P, PACK, C], F32, name="g32_%d" % e, tag="g32_%d" % e, align_bytes=64) for e in range(E)]
         g16 = [held("g16_%d" % e, [P, C, PACK], BF16) for e in range(E)]
         w16 = [[held("w16_%d_%d" % (e, h), [P, HALF, PACK], BF16) for h in range(2)] for e in range(E)]
@@ -58,10 +58,10 @@ def tile_moe_mlp_relu_kernel(tc, xT, dyT, a, w2, gate, offs, out):
         g_scales = [held("gs%d" % e, [P, C], U8) for e in range(E)]
         w_codes = [held("wc%d" % e, [P, H], U32) for e in range(E)]
         w_scales = [held("ws%d" % e, [P, H], U8) for e in range(E)]
-        x_slots = [[held("xs%d_%d" % (e, k), [P, 2, C // 2], BF16) for k in range(K_TILES)] for e in range(E)]
+        x_slots = [[held("xs%d_%d" % (e, k), [P, C], BF16) for k in range(K_TILES)] for e in range(E)]
         x_turned = {}
         gate_column = held("gate_column", [P, PACK], F32)
-        x_codes = [held("xc%d" % e, [P, K], U32) for e in range(E)]
+        x_codes = {0: held("xc0", [P, K], U32)}
         x_scales = [held("xsc%d" % e, [P, K], U8) for e in range(E)]
         da = [[held("da%d_%d" % (e, b), [P, C], BF16) for b in range(H_TILES)] for e in range(E)]
         da_turned = [held("dt%d" % e, [P, H_TILES, P, 2], F32) for e in range(E)]
@@ -107,7 +107,8 @@ def tile_moe_mlp_relu_kernel(tc, xT, dyT, a, w2, gate, offs, out):
         load_dy(0)
         load_gate(0, P)
         load_gate(P, C)
-        load_x(0,0,1024)
+        load_x(0,0,512)
+        load_x(0,512,1024)
         load_dy(1)
         load_x(1,0,1024)
         load_dy(2)
@@ -171,7 +172,7 @@ def tile_moe_mlp_relu_kernel(tc, xT, dyT, a, w2, gate, offs, out):
             copy(out=x16[k][:, c0:c1], in_=x32[k][:, c0:c1])
 
         def gather_x(k, e):
-            nc.scalar.activation(x_slots[e][k][:].rearrange("p u (r s) -> p r u s", s=2), x16[k][:].indirect(slots(e)), COPY)
+            nc.scalar.activation(x_slots[e][k][:], x16[k][:].indirect(slots(e)), COPY)
 
         def turn(key, pairs):
             bank = new_bank(key, [P, len(pairs), 2, P])
@@ -180,7 +181,7 @@ def tile_moe_mlp_relu_kernel(tc, xT, dyT, a, w2, gate, offs, out):
                     nc.tensor.transpose(bank[:, j, u, :], words[u], ident[:])
 
         def turn_x(e, j0, j1):
-            turn(("x", e, j0), [[x_slots[e][k][:, u, :].bitcast(F32) for u in range(2)] for k in range(j0, j1)])
+            turn(("x", e, j0), [[x_slots[e][k][:].bitcast(F32)[:, u:C // 2:2] for u in range(2)] for k in range(j0, j1)])
 
         def turn_da(e, j0, j1):
             turn(("da", e, j0), [[da[e][b][:].bitcast(F32)[:, u:C // 2:2] for u in range(2)] for b in range(j0, j1)])
@@ -202,6 +203,8 @@ def tile_moe_mlp_relu_kernel(tc, xT, dyT, a, w2, gate, offs, out):
             quantize(codes[:, cols], scales[:, cols], values, fmt)
 
         def quantize_x(e, j0, j1):
+            if e not in x_codes:
+                x_codes.setdefault(e, keep.tile([P, K], U32, name="xc1", tag="a1_0", align_bytes=64))
             quantize_turned(x_codes[e], x_scales[e], x_turned[e], j0, j1, E4M3)
 
         def quantize_da(e, j0, j1):
@@ -216,6 +219,11 @@ def tile_moe_mlp_relu_kernel(tc, xT, dyT, a, w2, gate, offs, out):
         def take_out(e, k, copy):
             copy(out=results[e][k][:], in_=banks[("out", e, k)][:])
 
+        def out_in_halves(e, k, copy):
+            for h in range(2):
+                copy(out=results[e][k][:, half(h)], in_=banks[("out", e, k)][:, half(h)])
+                nc.sync.dma_start(out[e, k * P:(k + 1) * P, half(h)], results[e][k][:, half(h)])
+
         def store(e, k):
             nc.sync.dma_start(out[e, k * P:(k + 1) * P, :], results[e][k][:])
 
@@ -226,18 +234,22 @@ def tile_moe_mlp_relu_kernel(tc, xT, dyT, a, w2, gate, offs, out):
         for t in range(1,4):
             for e in range(2):
                 gather_g(t,e)
-        for k in range(2):
-            round_x(k,0,1024,on_scalar)
-            for e in range(2):
-                gather_x(k,e)
-        round_x(2,0,512,on_scalar)
+        round_x(0,0,512,on_scalar)
+        round_x(0,512,1024,on_scalar)
         for e in range(2):
-            round_g(e,0,on_scalar)
-            round_g(e,1,on_vector)
-        quantize_g(0)
+            gather_x(0,e)
+        round_x(1,0,1024,on_scalar)
+        for e in range(2):
+            gather_x(1,e)
+        round_x(2,0,512,on_scalar)
+        round_g(0,0,on_scalar)
+        round_g(0,1,on_vector)
+        round_g(1,0,on_scalar)
+        round_g(1,1,on_vector)
         round_w(0,0,on_vector)
-        quantize_g(1)
+        quantize_g(0)
         quantize_w(0,0)
+        quantize_g(1)
         round_w(0,1,on_vector)
         for e in range(2):
             turn_x(e,0,2)
@@ -264,11 +276,12 @@ def tile_moe_mlp_relu_kernel(tc, xT, dyT, a, w2, gate, offs, out):
         turn_da(0,2,4)
         gather_x(2,1)
         quantize_da(0,0,2)
+        take_da(0,2,4,on_scalar)
         for b in range(2,4):
             product_dh(1,b)
-            mask_dh(1,b)
-        take_da(0,2,4,on_scalar)
+        mask_dh(1,2)
         quantize_da(0,2,4)
+        mask_dh(1,3)
         quantize_x(1,0,2)
         turn_x(0,2,3)
         take_x(0,2,3,on_scalar)
@@ -279,14 +292,21 @@ def tile_moe_mlp_relu_kernel(tc, xT, dyT, a, w2, gate, offs, out):
         take_x(1,2,3,on_scalar)
         turn_da(1,2,3)
         take_da(1,2,3,on_scalar)
+        for k in range(2):
+            product_out(0,k)
         turn_da(1,3,4)
         take_da(1,3,4,on_vector)
+        product_out(0,2)
         quantize_da(1,0,2)
         quantize_x(1,2,3)
         quantize_da(1,2,3)
         quantize_da(1,3,4)
-        for e in range(2):
-            for k in range(3):
-                product_out(e,k)
-                take_out(e,k,on_vector if e==1 and k!=1 else on_scalar)
-                store(e,k)
+        for k in range(3):
+            take_out(0,k,on_scalar)
+            store(0,k)
+        for k in range(3):
+            product_out(1,k)
+        out_in_halves(1,0,on_vector)
+        for k in (1,2):
+            take_out(1,k,on_vector if k!=1 else on_scalar)
+            store(1,k)

@@ -60,7 +60,7 @@ def tile_moe_mlp_relu_kernel(tc, xT, dyT, a, w2, gate, offs, out):
         w_scales = [held("ws%d" % e, [P, H], U8) for e in range(E)]
         x_slots = [[held("xs%d_%d" % (e, k), [P, C], BF16) for k in range(K_TILES)] for e in range(E)]
         x_turned = {}
-        gate_column = held("gate_column", [P, PACK], F32)
+        gate_column = held("gate_column", [P, E, PACK], F32)
         x_codes = {0: held("xc0", [P, K], U32)}
         x_scales = [held("xsc%d" % e, [P, K], U8) for e in range(E)]
         da = [[held("da%d_%d" % (e, b), [P, C], BF16) for b in range(H_TILES)] for e in range(E)]
@@ -83,11 +83,8 @@ def tile_moe_mlp_relu_kernel(tc, xT, dyT, a, w2, gate, offs, out):
 
         dy_rows = dyT.rearrange("(p t) c -> t p c", t=PACK)
 
-        def load_gate(c0, c1):
-            nc.sync.dma_start(gates[0][:, c0:c1], gate[0:P, c0:c1])
-
         def load_gate_column():
-            nc.sync.dma_start(gate_column[:], gate[0, C:2 * C].rearrange("(n q) -> n q", q=PACK))
+            nc.sync.dma_start(gate_column[:], gate[0, :].rearrange("(e n q) -> n e q", e=E, q=PACK))
 
         def load_dy(t):
             nc.sync.dma_start(dy[t][:], dy_rows[t])
@@ -102,18 +99,15 @@ def tile_moe_mlp_relu_kernel(tc, xT, dyT, a, w2, gate, offs, out):
             rows = a[h * HALF:(h + 1) * HALF, e * C:(e + 1) * C]
             nc.sync.dma_start(saved[e][h][:], rows.rearrange("(b p) c -> p b c", p=P))
 
-        nc.sync.dma_start(offsets[:], offs)
         load_gate_column()
         load_dy(0)
-        load_gate(0, P)
-        load_gate(P, C)
-        load_x(0,0,512)
-        load_x(0,512,1024)
+        nc.sync.dma_start(offsets[:], offs)
+        load_x(0,0,1024)
         load_dy(1)
         load_x(1,0,1024)
         load_dy(2)
-        load_x(2,0,512)
         load_dy(3)
+        load_x(2,0,512)
         load_w(0)
         load_a(0,0)
         load_w(1)
@@ -131,11 +125,14 @@ def tile_moe_mlp_relu_kernel(tc, xT, dyT, a, w2, gate, offs, out):
         def slots(e, c0=0, c1=C):
             return offsets[:, (e * C + c0) // 16:(e * C + c1) // 16]
 
-        def spread_gate():
-            bank = new_bank("gate", [P, PACK, P])
+        def spread(e):
+            bank = new_bank(("gate", e), [P, PACK, P])
             for q in range(PACK):
-                nc.tensor.transpose(bank[:, q, :], gate_column[:, q:q + 1].to_broadcast([P, P]), ident[:])
-            nc.scalar.activation(gates[1][:].rearrange("p (n q) -> p n q", q=PACK), bank[:].rearrange("p q n -> p n q"), COPY)
+                nc.tensor.transpose(bank[:, q, :], gate_column[:, e, q:q + 1].to_broadcast([P, P]), ident[:])
+
+        def take_gate(e, c0, c1):
+            rows = slice(c0 // PACK, c1 // PACK)
+            nc.scalar.activation(gates[e][:, c0:c1].rearrange("p (n q) -> p n q", q=PACK), banks[("gate", e)][:, :, rows].rearrange("p q n -> p n q"), COPY)
 
         def half(h):
             return slice(h * HALF, (h + 1) * HALF)
@@ -227,15 +224,18 @@ def tile_moe_mlp_relu_kernel(tc, xT, dyT, a, w2, gate, offs, out):
         def store(e, k):
             nc.sync.dma_start(out[e, k * P:(k + 1) * P, :], results[e][k][:])
 
-        spread_gate()
-        gather_g(0, 0, 0, P)
-        gather_g(0, 0, P, C)
+        spread(0)
+        take_gate(0, 0, HALF)
+        take_gate(0, HALF, C)
+        spread(1)
+        take_gate(1, 0, C)
+        gather_g(0, 0, 0, HALF)
+        gather_g(0, 0, HALF, C)
         gather_g(0,1)
         for t in range(1,4):
             for e in range(2):
                 gather_g(t,e)
-        round_x(0,0,512,on_scalar)
-        round_x(0,512,1024,on_scalar)
+        round_x(0,0,1024,on_scalar)
         for e in range(2):
             gather_x(0,e)
         round_x(1,0,1024,on_scalar)

@@ -58,12 +58,15 @@ def tile_moe_mlp_relu_kernel(tc, xT, dyT, a, w2, gate, offs, out):
         g_scales = [held("gs%d" % e, [P, C], U8) for e in range(E)]
         w_codes = [held("wc%d" % e, [P, H], U32) for e in range(E)]
         w_scales = [held("ws%d" % e, [P, H], U8) for e in range(E)]
-        x_slots = [[held("xs%d_%d" % (e, k), [P, C], BF16) for k in range(K_TILES)] for e in range(E)]
+        x_slots = [[held("xs%d_%d" % (e, k), [P, C], BF16) for k in range(K_TILES - e)] for e in range(E)]
         x_turned = {}
-        gate_column = held("gate_column", [P, E, PACK], F32)
+        gate_column = held("gate_column", [P, PACK], F32)
+        gate_runs = held("gate_runs", [P, QUAD], F32)
+        gate_turned = held("gate_turned", [P, QUAD], F32)
+        gate_wide = held("gate_wide", [P, C // QUAD, QUAD], F32)
         x_codes = {0: held("xc0", [P, K], U32)}
         x_scales = [held("xsc%d" % e, [P, K], U8) for e in range(E)]
-        da = [[held("da%d_%d" % (e, b), [P, C], BF16) for b in range(H_TILES)] for e in range(E)]
+        da = [[keep.tile([P, C], BF16, name="da%d_%d" % (e, b), tag="da%d_%d" % (e, b), align_bytes=64) for b in range(H_TILES)] for e in range(E)]
         da_turned = [held("dt%d" % e, [P, H_TILES, P, 2], F32) for e in range(E)]
         da_codes = [held("dc%d" % e, [P, H], U32) for e in range(E)]
         da_scales = [held("ds%d" % e, [P, H], U8) for e in range(E)]
@@ -84,7 +87,8 @@ def tile_moe_mlp_relu_kernel(tc, xT, dyT, a, w2, gate, offs, out):
         dy_rows = dyT.rearrange("(p t) c -> t p c", t=PACK)
 
         def load_gate_column():
-            nc.sync.dma_start(gate_column[:], gate[0, :].rearrange("(e n q) -> n e q", e=E, q=PACK))
+            nc.sync.dma_start(gate_runs[:], gate[0:P // QUAD, :].rearrange("q (c b) -> (q c) b", b=QUAD))
+            nc.sync.dma_start(gate_column[:], gate[0, C:2 * C].rearrange("(n q) -> n q", q=PACK))
 
         def load_dy(t):
             nc.sync.dma_start(dy[t][:], dy_rows[t])
@@ -104,8 +108,8 @@ def tile_moe_mlp_relu_kernel(tc, xT, dyT, a, w2, gate, offs, out):
         nc.sync.dma_start(offsets[:], offs)
         load_x(0,0,1024)
         load_dy(1)
-        load_x(1,0,1024)
         load_dy(2)
+        load_x(1,0,1024)
         load_dy(3)
         load_x(2,0,512)
         load_w(0)
@@ -128,7 +132,7 @@ def tile_moe_mlp_relu_kernel(tc, xT, dyT, a, w2, gate, offs, out):
         def spread(e):
             bank = new_bank(("gate", e), [P, PACK, P])
             for q in range(PACK):
-                nc.tensor.transpose(bank[:, q, :], gate_column[:, e, q:q + 1].to_broadcast([P, P]), ident[:])
+                nc.tensor.transpose(bank[:, q, :], gate_column[:, q:q + 1].to_broadcast([P, P]), ident[:])
 
         def take_gate(e, c0, c1):
             rows = slice(c0 // PACK, c1 // PACK)
@@ -169,6 +173,8 @@ def tile_moe_mlp_relu_kernel(tc, xT, dyT, a, w2, gate, offs, out):
             copy(out=x16[k][:, c0:c1], in_=x32[k][:, c0:c1])
 
         def gather_x(k, e):
+            if k == len(x_slots[e]):
+                x_slots[e].append(keep.tile([P, C], BF16, name="xs_last", tag="da0_3", align_bytes=64))
             nc.scalar.activation(x_slots[e][k][:], x16[k][:].indirect(slots(e)), COPY)
 
         def turn(key, pairs):
@@ -224,9 +230,10 @@ def tile_moe_mlp_relu_kernel(tc, xT, dyT, a, w2, gate, offs, out):
         def store(e, k):
             nc.sync.dma_start(out[e, k * P:(k + 1) * P, :], results[e][k][:])
 
-        spread(0)
-        take_gate(0, 0, HALF)
-        take_gate(0, HALF, C)
+        nc.vector.transpose(gate_turned[:], gate_runs[:])
+        on_vector(out=gate_wide[:], in_=gate_turned[:, 0:C // QUAD].unsqueeze(2).to_broadcast([P, C // QUAD, QUAD]))
+        for h in range(2):
+            nc.vector.transpose(gates[0][:, half(h)], gate_wide[:].rearrange("p c r -> p (c r)")[:, half(h)])
         spread(1)
         take_gate(1, 0, C)
         gather_g(0, 0, 0, HALF)
@@ -274,9 +281,9 @@ def tile_moe_mlp_relu_kernel(tc, xT, dyT, a, w2, gate, offs, out):
             mask_dh(1,b)
         take_da(0,0,2,on_scalar)
         turn_da(0,2,4)
-        gather_x(2,1)
         quantize_da(0,0,2)
         take_da(0,2,4,on_scalar)
+        gather_x(2,1)
         for b in range(2,4):
             product_dh(1,b)
         mask_dh(1,2)
@@ -288,25 +295,23 @@ def tile_moe_mlp_relu_kernel(tc, xT, dyT, a, w2, gate, offs, out):
         quantize_x(0,2,3)
         turn_da(1,0,2)
         take_da(1,0,2,on_scalar)
-        turn_x(1,2,3)
-        take_x(1,2,3,on_scalar)
         turn_da(1,2,3)
         take_da(1,2,3,on_scalar)
         for k in range(2):
             product_out(0,k)
         turn_da(1,3,4)
         take_da(1,3,4,on_vector)
+        turn_x(1,2,3)
+        take_x(1,2,3,on_scalar)
         product_out(0,2)
         quantize_da(1,0,2)
-        quantize_x(1,2,3)
         quantize_da(1,2,3)
         quantize_da(1,3,4)
+        quantize_x(1,2,3)
         for k in range(3):
             take_out(0,k,on_scalar)
             store(0,k)
         for k in range(3):
             product_out(1,k)
-        out_in_halves(1,0,on_vector)
-        for k in (1,2):
             take_out(1,k,on_vector if k!=1 else on_scalar)
             store(1,k)

@@ -106,7 +106,8 @@ def tile_moe_mlp_relu_kernel(tc, xT, dyT, a, w2, gate, offs, out):
         load_gate_column()
         load_dy(0)
         nc.sync.dma_start(offsets[:], offs)
-        load_x(0,0,1024)
+        load_x(0,0,512)
+        load_x(0,512,1024)
         load_dy(1)
         load_dy(2)
         load_x(1,0,1024)
@@ -147,8 +148,8 @@ def tile_moe_mlp_relu_kernel(tc, xT, dyT, a, w2, gate, offs, out):
         def gather_g(t, e, c0=0, c1=C):
             nc.vector.tensor_tensor(g32[e][:, t, c0:c1], dy[t][:].indirect(slots(e, c0, c1)), gates[e][:, c0:c1], MULT)
 
-        def round_g(e, h, copy):
-            interleave(copy, g16[e][:, half(h), :], g32[e][:, :, half(h)])
+        def round_g(e, c0, c1, copy):
+            interleave(copy, g16[e][:, c0:c1, :], g32[e][:, :, c0:c1])
 
         def round_w(e, h, copy):
             interleave(copy, w16[e][h][:], w32[e][:, :, half(h)])
@@ -242,17 +243,18 @@ def tile_moe_mlp_relu_kernel(tc, xT, dyT, a, w2, gate, offs, out):
         for t in range(1,4):
             for e in range(2):
                 gather_g(t,e)
-        round_x(0,0,1024,on_scalar)
+        round_x(0,0,512,on_scalar)
+        round_x(0,512,1024,on_scalar)
         for e in range(2):
             gather_x(0,e)
         round_x(1,0,1024,on_scalar)
         for e in range(2):
             gather_x(1,e)
         round_x(2,0,512,on_scalar)
-        round_g(0,0,on_scalar)
-        round_g(0,1,on_vector)
-        round_g(1,0,on_scalar)
-        round_g(1,1,on_vector)
+        round_g(0,0,HALF,on_scalar)
+        round_g(0,HALF,C,on_vector)
+        round_g(1,0,3 * P,on_scalar)
+        round_g(1,3 * P,C,on_vector)
         round_w(0,0,on_vector)
         quantize_g(0)
         quantize_w(0,0)

@@ -51,7 +51,8 @@ def tile_moe_mlp_relu_kernel(tc, xT, dyT, a, w2, gate, offs, out):
         x16 = [held("x16_%d" % k, [P, T], BF16) for k in range(K_TILES)]
         w32 = [held("w32_%d" % e, [P, PACK, H], F32) for e in range(E)]
         saved = [[keep.tile([P, 2, C], F32, name="a%d_%d" % (e, h), tag="a%d_%d" % (e, h), align_bytes=64) for h in range(2)] for e in range(E)]
-        g32 = [keep.tile([P, PACK, C], F32, name="g32_%d" % e, tag="g32_%d" % e, align_bytes=64) for e in range(E)]
+        stage = [held("stage%d" % e, [P, HALF + PACK * C], F32) for e in range(E)]
+        g32 = [stage[e][:, HALF:].rearrange("p (t c) -> p t c", t=PACK) for e in range(E)]
         g16 = [held("g16_%d" % e, [P, C, PACK], BF16) for e in range(E)]
         w16 = [[held("w16_%d_%d" % (e, h), [P, HALF, PACK], BF16) for h in range(2)] for e in range(E)]
         g_codes = [held("gc%d" % e, [P, C], U32) for e in range(E)]
@@ -59,7 +60,7 @@ def tile_moe_mlp_relu_kernel(tc, xT, dyT, a, w2, gate, offs, out):
         w_codes = [held("wc%d" % e, [P, H], U32) for e in range(E)]
         w_scales = [held("ws%d" % e, [P, H], U8) for e in range(E)]
         x_slots = [[held("xs%d_%d" % (e, k), [P, C], BF16) for k in range(K_TILES - e)] for e in range(E)]
-        x_turned = {}
+        x_turned = [stage[e][:, 0:K_TILES * HALF].rearrange("p (k m u) -> p k m u", k=K_TILES, u=2) for e in range(E)]
         gate_column = held("gate_column", [P, PACK], F32)
         gate_runs = held("gate_runs", [P, QUAD], F32)
         gate_turned = held("gate_turned", [P, QUAD], F32)
@@ -109,8 +110,8 @@ def tile_moe_mlp_relu_kernel(tc, xT, dyT, a, w2, gate, offs, out):
         load_x(0,0,512)
         load_x(0,512,1024)
         load_dy(1)
-        load_dy(2)
         load_x(1,0,1024)
+        load_dy(2)
         load_dy(3)
         load_x(2,0,512)
         load_w(0)
@@ -151,8 +152,8 @@ def tile_moe_mlp_relu_kernel(tc, xT, dyT, a, w2, gate, offs, out):
         def round_g(e, c0, c1, copy):
             interleave(copy, g16[e][:, c0:c1, :], g32[e][:, :, c0:c1])
 
-        def round_w(e, h, copy):
-            interleave(copy, w16[e][h][:], w32[e][:, :, half(h)])
+        def round_w(e, h, copy, c0=0, c1=HALF):
+            interleave(copy, w16[e][h][:, c0:c1, :], w32[e][:, :, h * HALF + c0:h * HALF + c1])
 
         def quantize_g(e):
             quantize(g_codes[e][:], g_scales[e][:], g16[e][:].rearrange("p c t -> p (c t)"), E5M2)
@@ -194,8 +195,6 @@ def tile_moe_mlp_relu_kernel(tc, xT, dyT, a, w2, gate, offs, out):
             copy(out=turned, in_=banks[key][:].rearrange("p j u m -> p j m u"))
 
         def take_x(e, j0, j1, copy):
-            if j0 == 0:
-                x_turned[e] = keep.tile([P, K_TILES, P, 2], F32, name="xt%d" % e, tag="g32_%d" % e, align_bytes=64)
             take(("x", e, j0), x_turned[e][:, j0:j1], copy)
 
         def take_da(e, j0, j1, copy):
@@ -249,6 +248,9 @@ def tile_moe_mlp_relu_kernel(tc, xT, dyT, a, w2, gate, offs, out):
             gather_x(0,e)
         round_x(1,0,1024,on_scalar)
         for e in range(2):
+            turn_x(e,0,1)
+            take_x(e,0,1,on_scalar)
+        for e in range(2):
             gather_x(1,e)
         round_x(2,0,512,on_scalar)
         round_g(0,0,HALF,on_scalar)
@@ -259,10 +261,11 @@ def tile_moe_mlp_relu_kernel(tc, xT, dyT, a, w2, gate, offs, out):
         quantize_g(0)
         quantize_w(0,0)
         quantize_g(1)
-        round_w(0,1,on_vector)
+        round_w(0,1,on_vector,0,P)
+        round_w(0,1,on_scalar,P,HALF)
         for e in range(2):
-            turn_x(e,0,2)
-            take_x(e,0,2,on_scalar)
+            turn_x(e,1,2)
+            take_x(e,1,2,on_scalar)
         quantize_x(0,0,2)
         quantize_w(0,1)
         round_w(1,0,on_scalar)
@@ -304,11 +307,11 @@ def tile_moe_mlp_relu_kernel(tc, xT, dyT, a, w2, gate, offs, out):
         turn_da(1,3,4)
         take_da(1,3,4,on_vector)
         turn_x(1,2,3)
-        take_x(1,2,3,on_scalar)
         product_out(0,2)
         quantize_da(1,0,2)
         quantize_da(1,2,3)
         quantize_da(1,3,4)
+        take_x(1,2,3,on_vector)
         quantize_x(1,2,3)
         for k in range(3):
             take_out(0,k,on_scalar)

@@ -25,6 +25,7 @@ K_TILES = K // P
 H_TILES = H // P
 LIST_COLS = C // 16
 HALF = 2 * P
+RUN = 16
 QUAD = 32
 BANKS = 8
 
@@ -143,6 +144,9 @@ def tile_moe_mlp_relu_kernel(tc, xT, dyT, a, w2, gate, offs, out):
         def half(h):
             return slice(h * HALF, (h + 1) * HALF)
 
+        def runs(columns):
+            return columns.rearrange("p (q u m) -> p q u m", u=2, m=RUN)
+
         def quantize(codes, scales, values, fmt):
             nc.vector.quantize_mx(out=codes.bitcast(fmt), scales=scales, in_=values)
 
@@ -168,8 +172,10 @@ def tile_moe_mlp_relu_kernel(tc, xT, dyT, a, w2, gate, offs, out):
                                 rhs=g_codes[e][:].bitcast(E5M2), rhs_scale=g_scales[e][:], start=True, stop=True)
 
         def mask_dh(e, b):
-            nc.vector.scalar_tensor_tensor(
-                da[e][b][:], saved[e][b // 2][:, b % 2, :], 0.0, banks[("dh", e, b)][:], IS_GT, MULT)
+            for u in range(2):
+                nc.vector.scalar_tensor_tensor(
+                    da[e][b][:, half(u)].rearrange("p (q m) -> p q m", m=RUN), runs(saved[e][b // 2][:, b % 2, :])[:, :, u, :], 0.0,
+                    runs(banks[("dh", e, b)][:])[:, :, u, :], IS_GT, MULT)
 
         def round_x(k, c0, c1, copy):
             copy(out=x16[k][:, c0:c1], in_=x32[k][:, c0:c1])
@@ -177,7 +183,7 @@ def tile_moe_mlp_relu_kernel(tc, xT, dyT, a, w2, gate, offs, out):
         def gather_x(k, e):
             if k == len(x_slots[e]):
                 x_slots[e].append(keep.tile([P, C], BF16, name="xs_last", tag="da0_3", align_bytes=64))
-            nc.scalar.activation(x_slots[e][k][:], x16[k][:].indirect(slots(e)), COPY)
+            nc.scalar.activation(x_slots[e][k][:].rearrange("p (u q m) -> p q u m", u=2, m=RUN), x16[k][:].indirect(slots(e)), COPY)
 
         def turn(key, pairs):
             bank = new_bank(key, [P, len(pairs), 2, P])
@@ -186,10 +192,10 @@ def tile_moe_mlp_relu_kernel(tc, xT, dyT, a, w2, gate, offs, out):
                     nc.tensor.transpose(bank[:, j, u, :], words[u], ident[:])
 
         def turn_x(e, j0, j1):
-            turn(("x", e, j0), [[x_slots[e][k][:].bitcast(F32)[:, u:C // 2:2] for u in range(2)] for k in range(j0, j1)])
+            turn(("x", e, j0), [[x_slots[e][k][:].bitcast(F32)[:, u * P:(u + 1) * P] for u in range(2)] for k in range(j0, j1)])
 
         def turn_da(e, j0, j1):
-            turn(("da", e, j0), [[da[e][b][:].bitcast(F32)[:, u:C // 2:2] for u in range(2)] for b in range(j0, j1)])
+            turn(("da", e, j0), [[da[e][b][:].bitcast(F32)[:, u * P:(u + 1) * P] for u in range(2)] for b in range(j0, j1)])
 
         def take(key, turned, copy):
             copy(out=turned, in_=banks[key][:].rearrange("p j u m -> p j m u"))

@@ -324,5 +324,5 @@ def tile_moe_mlp_relu_kernel(tc, xT, dyT, a, w2, gate, offs, out):
             store(0,k)
         for k in range(3):
             product_out(1,k)
-            take_out(1,k,on_vector if k!=1 else on_scalar)
+            take_out(1,k,on_scalar if k!=1 else on_vector)
             store(1,k)

@@ -25,8 +25,9 @@ K_TILES = K // P
 H_TILES = H // P
 LIST_COLS = C // 16
 HALF = 2 * P
-RUN = 16
 QUAD = 32
+VECTOR_TILES = 34
+SCALAR_TILES = 26
 BANKS = 8
 
 
@@ -36,8 +37,13 @@ def interleave(copy, dst, src):
 
 def tile_moe_mlp_relu_kernel(tc, xT, dyT, a, w2, gate, offs, out):
     nc = tc.nc
-    on_scalar = nc.scalar.copy
-    on_vector = nc.vector.tensor_copy
+
+    def on_scalar(out, in_):
+        nc.scalar.copy(out=out, in_=in_)
+
+    def on_vector(out, in_):
+        nc.vector.tensor_copy(out=out, in_=in_)
+
     with ExitStack() as ctx:
         keep = ctx.enter_context(tc.tile_pool(name="keep", bufs=1))
         psum = ctx.enter_context(tc.psum_pool(name="psum", bufs=BANKS))
@@ -46,40 +52,35 @@ def tile_moe_mlp_relu_kernel(tc, xT, dyT, a, w2, gate, offs, out):
             return keep.tile(shape, dtype, name=name, align_bytes=64)
 
         offsets = keep.tile([P, E * LIST_COLS], U16, name="offsets")
-        gates = [held("gate%d" % e, [P, C], F32) for e in range(E)]
+        gate0 = held("gate0", [P, C], F32)
         dy = [held("dy%d" % t, [P, T], F32) for t in range(PACK)]
         x32 = [held("x32_%d" % k, [P, T], F32) for k in range(K_TILES)]
-        x16 = [held("x16_%d" % k, [P, T], BF16) for k in range(K_TILES)]
         w32 = [held("w32_%d" % e, [P, PACK, H], F32) for e in range(E)]
-        saved = [[keep.tile([P, 2, C], F32, name="a%d_%d" % (e, h), tag="a%d_%d" % (e, h), align_bytes=64) for h in range(2)] for e in range(E)]
-        stage = [held("stage%d" % e, [P, HALF + PACK * C], F32) for e in range(E)]
-        g32 = [stage[e][:, HALF:].rearrange("p (t c) -> p t c", t=PACK) for e in range(E)]
+        saved = {}
+        g32 = [held("g32_%d" % e, [P, PACK, C], F32) for e in range(E)]
         g16 = [held("g16_%d" % e, [P, C, PACK], BF16) for e in range(E)]
-        w16 = [[held("w16_%d_%d" % (e, h), [P, HALF, PACK], BF16) for h in range(2)] for e in range(E)]
-        g_codes = [held("gc%d" % e, [P, C], U32) for e in range(E)]
         g_scales = [held("gs%d" % e, [P, C], U8) for e in range(E)]
-        w_codes = [held("wc%d" % e, [P, H], U32) for e in range(E)]
         w_scales = [held("ws%d" % e, [P, H], U8) for e in range(E)]
-        x_slots = [[held("xs%d_%d" % (e, k), [P, C], BF16) for k in range(K_TILES - e)] for e in range(E)]
-        x_turned = [stage[e][:, 0:K_TILES * HALF].rearrange("p (k m u) -> p k m u", k=K_TILES, u=2) for e in range(E)]
         gate_column = held("gate_column", [P, PACK], F32)
         gate_runs = held("gate_runs", [P, QUAD], F32)
         gate_turned = held("gate_turned", [P, QUAD], F32)
         gate_wide = held("gate_wide", [P, C // QUAD, QUAD], F32)
-        x_codes = {0: held("xc0", [P, K], U32)}
         x_scales = [held("xsc%d" % e, [P, K], U8) for e in range(E)]
-        da = [[keep.tile([P, C], BF16, name="da%d_%d" % (e, b), tag="da%d_%d" % (e, b), align_bytes=64) for b in range(H_TILES)] for e in range(E)]
-        da_turned = [held("dt%d" % e, [P, H_TILES, P, 2], F32) for e in range(E)]
-        da_codes = [held("dc%d" % e, [P, H], U32) for e in range(E)]
         da_scales = [held("ds%d" % e, [P, H], U8) for e in range(E)]
-        results = [[held("res%d_%d" % (e, k), [P, H], F32) for k in range(K_TILES)] for e in range(E)]
+
+        made = {}
+
+        def fresh(copy, key, shape, dtype):
+            tag, bufs = ("by_vector", VECTOR_TILES) if copy is on_vector else ("by_scalar", SCALAR_TILES)
+            made[key] = keep.tile(shape, dtype, name="_".join(str(part) for part in key), tag=tag, bufs=bufs, align_bytes=64)
+            return made[key]
 
         ident = held("ident", [P, P], F32)
         ones = held("ones", [P, QUAD], F32)
         column = held("column", [P, QUAD], F32)
         row = held("row", [P, QUAD], F32)
         nc.vector.memset(ones[:], 1.0)
-        nc.vector.memset(ident[:], 0.0)
+        nc.scalar.activation(ident[:].rearrange("p (q c) -> p q c", c=QUAD), ones[:].unsqueeze(1).to_broadcast([P, P // QUAD, QUAD]), COPY, scale=0.0)
         nc.vector.tensor_tensor_scan(column[:], ones[:], ones[:], 0.0, MULT, ADD)
         nc.vector.transpose(row[:], column[:])
         for q0 in range(0, P, QUAD):
@@ -88,40 +89,29 @@ def tile_moe_mlp_relu_kernel(tc, xT, dyT, a, w2, gate, offs, out):
 
         dy_rows = dyT.rearrange("(p t) c -> t p c", t=PACK)
 
-        def load_gate_column():
+        def load_gate_runs():
             nc.sync.dma_start(gate_runs[:], gate[0:P // QUAD, :].rearrange("q (c b) -> (q c) b", b=QUAD))
+
+        def load_gate_column():
             nc.sync.dma_start(gate_column[:], gate[0, C:2 * C].rearrange("(n q) -> n q", q=PACK))
 
         def load_dy(t):
             nc.sync.dma_start(dy[t][:], dy_rows[t])
 
-        def load_x(k, c0, c1):
-            nc.sync.dma_start(x32[k][:, c0:c1], xT[k * P:(k + 1) * P, c0:c1])
+        def load_offsets():
+            nc.sync.dma_start(offsets[:], offs)
+
+        def load_x(k):
+            nc.sync.dma_start(x32[k][:], xT[k * P:(k + 1) * P, :])
 
         def load_w(e):
             nc.sync.dma_start(w32[e][:], w2[e].rearrange("(p t) i -> p t i", t=PACK))
 
-        def load_a(e, h):
-            rows = a[h * HALF:(h + 1) * HALF, e * C:(e + 1) * C]
-            nc.sync.dma_start(saved[e][h][:], rows.rearrange("(b p) c -> p b c", p=P))
-
-        load_gate_column()
-        load_dy(0)
-        nc.sync.dma_start(offsets[:], offs)
-        load_x(0,0,512)
-        load_x(0,512,1024)
-        load_dy(1)
-        load_x(1,0,1024)
-        load_dy(2)
-        load_dy(3)
-        load_x(2,0,512)
-        load_w(0)
-        load_a(0,0)
-        load_w(1)
-        load_x(2,512,1024)
-        load_a(0,1)
-        load_a(1,0)
-        load_a(1,1)
+        def load_a(e, b0, b1):
+            rows = held("a%d_%d" % (e, b0), [P, b1 - b0, C], F32)
+            nc.sync.dma_start(rows[:], a[b0 * P:b1 * P, e * C:(e + 1) * C].rearrange("(b p) c -> p b c", p=P))
+            for b in range(b0, b1):
+                saved[(e, b)] = rows[:, b - b0, :]
 
         banks = {}
 
@@ -137,192 +127,251 @@ def tile_moe_mlp_relu_kernel(tc, xT, dyT, a, w2, gate, offs, out):
             for q in range(PACK):
                 nc.tensor.transpose(bank[:, q, :], gate_column[:, q:q + 1].to_broadcast([P, P]), ident[:])
 
-        def take_gate(e, c0, c1):
-            rows = slice(c0 // PACK, c1 // PACK)
-            nc.scalar.activation(gates[e][:, c0:c1].rearrange("p (n q) -> p n q", q=PACK), banks[("gate", e)][:, :, rows].rearrange("p q n -> p n q"), COPY)
-
         def half(h):
             return slice(h * HALF, (h + 1) * HALF)
-
-        def runs(columns):
-            return columns.rearrange("p (q u m) -> p q u m", u=2, m=RUN)
 
         def quantize(codes, scales, values, fmt):
             nc.vector.quantize_mx(out=codes.bitcast(fmt), scales=scales, in_=values)
 
-        def gather_g(t, e, c0=0, c1=C):
-            nc.vector.tensor_tensor(g32[e][:, t, c0:c1], dy[t][:].indirect(slots(e, c0, c1)), gates[e][:, c0:c1], MULT)
+        def spread_gate0():
+            nc.vector.transpose(gate_turned[:], gate_runs[:])
+            on_vector(out=gate_wide[:], in_=gate_turned[:, 0:C // QUAD].unsqueeze(2).to_broadcast([P, C // QUAD, QUAD]))
+            for h in range(2):
+                nc.vector.transpose(gate0[:, half(h)], gate_wide[:].rearrange("p c r -> p (c r)")[:, half(h)])
 
-        def round_g(e, c0, c1, copy):
-            interleave(copy, g16[e][:, c0:c1, :], g32[e][:, :, c0:c1])
+        def gather_g0(t, c0=0, c1=C):
+            nc.vector.tensor_tensor(g32[0][:, t, c0:c1], dy[t][:].indirect(slots(0, c0, c1)), gate0[:, c0:c1], MULT)
 
-        def round_w(e, h, copy, c0=0, c1=HALF):
-            interleave(copy, w16[e][h][:, c0:c1, :], w32[e][:, :, h * HALF + c0:h * HALF + c1])
+        def gather_dy1(t):
+            nc.scalar.activation(g32[1][:, t, :], dy[t][:].indirect(slots(1)), COPY)
+
+        def gate_round_g1():
+            gate1 = banks[("gate", 1)][:].rearrange("p q n -> p n q").unsqueeze(2)
+            nc.vector.tensor_tensor(
+                g16[1][:].rearrange("p (n q) t -> p n t q", q=PACK),
+                g32[1][:].rearrange("p t (n q) -> p n t q", q=PACK),
+                gate1.to_broadcast([P, P, PACK, PACK]), MULT)
+
+        def round_g0(c0, c1, copy):
+            interleave(copy, g16[0][:, c0:c1, :], g32[0][:, :, c0:c1])
 
         def quantize_g(e):
-            quantize(g_codes[e][:], g_scales[e][:], g16[e][:].rearrange("p c t -> p (c t)"), E5M2)
+            quantize(fresh(on_vector, ("gc", e), [P, C], U32)[:], g_scales[e][:], g16[e][:].rearrange("p c t -> p (c t)"), E5M2)
 
-        def quantize_w(e, h):
-            quantize(w_codes[e][:, half(h)], w_scales[e][:, half(h)], w16[e][h][:].rearrange("p i t -> p (i t)"), E4M3)
+        def round_w(e, b0, b1, copy):
+            w16 = fresh(copy, ("w16", e, b0), [P, (b1 - b0) * P, PACK], BF16)
+            interleave(copy, w16[:], w32[e][:, :, b0 * P:b1 * P])
+
+        def quantize_w(e, b0, b1):
+            codes = fresh(on_vector, ("wc", e, b0), [P, (b1 - b0) * P], U32)
+            quantize(codes[:], w_scales[e][:, b0 * P:b1 * P], made[("w16", e, b0)][:].rearrange("p i t -> p (i t)"), E4M3)
+            for b in range(b0, b1):
+                made[("w_codes", e, b)] = codes[:, (b - b0) * P:(b - b0 + 1) * P]
 
         def product_dh(e, b):
-            cols = slice(b * P, (b + 1) * P)
             dh = new_bank(("dh", e, b), [P, C])
-            nc.tensor.matmul_mx(out=dh[:], lhsT=w_codes[e][:, cols].bitcast(E4M3), lhsT_scale=w_scales[e][:, cols],
-                                rhs=g_codes[e][:].bitcast(E5M2), rhs_scale=g_scales[e][:], start=True, stop=True)
+            nc.tensor.matmul_mx(out=dh[:], lhsT=made[("w_codes", e, b)].bitcast(E4M3), lhsT_scale=w_scales[e][:, b * P:(b + 1) * P],
+                                rhs=made[("gc", e)][:].bitcast(E5M2), rhs_scale=g_scales[e][:], start=True, stop=True)
 
         def mask_dh(e, b):
-            for u in range(2):
-                nc.vector.scalar_tensor_tensor(
-                    da[e][b][:, half(u)].rearrange("p (q m) -> p q m", m=RUN), runs(saved[e][b // 2][:, b % 2, :])[:, :, u, :], 0.0,
-                    runs(banks[("dh", e, b)][:])[:, :, u, :], IS_GT, MULT)
-
-        def round_x(k, c0, c1, copy):
-            copy(out=x16[k][:, c0:c1], in_=x32[k][:, c0:c1])
+            da = fresh(on_vector, ("da", e, b), [P, C], BF16)
+            nc.vector.scalar_tensor_tensor(da[:], saved[(e, b)], 0.0, banks[("dh", e, b)][:], IS_GT, MULT)
 
         def gather_x(k, e):
-            if k == len(x_slots[e]):
-                x_slots[e].append(keep.tile([P, C], BF16, name="xs_last", tag="da0_3", align_bytes=64))
-            nc.scalar.activation(x_slots[e][k][:].rearrange("p (u q m) -> p q u m", u=2, m=RUN), x16[k][:].indirect(slots(e)), COPY)
+            x_slots = fresh(on_scalar, ("x", e, k), [P, C], BF16)
+            nc.scalar.activation(x_slots[:], x32[k][:].indirect(slots(e)), COPY)
 
-        def turn(key, pairs):
-            bank = new_bank(key, [P, len(pairs), 2, P])
-            for j, words in enumerate(pairs):
+        def turn(*keys):
+            bank = new_bank(keys, [P, len(keys), 2, P])
+            for j, key in enumerate(keys):
                 for u in range(2):
-                    nc.tensor.transpose(bank[:, j, u, :], words[u], ident[:])
+                    nc.tensor.transpose(bank[:, j, u, :], made[key][:].bitcast(F32)[:, u:2 * P:2], ident[:])
 
-        def turn_x(e, j0, j1):
-            turn(("x", e, j0), [[x_slots[e][k][:].bitcast(F32)[:, u * P:(u + 1) * P] for u in range(2)] for k in range(j0, j1)])
+        def take(copy, *keys):
+            turned = fresh(copy, ("turned",) + keys[0], [P, len(keys), P, 2], F32)
+            copy(out=turned[:], in_=banks[keys][:].rearrange("p j u m -> p j m u"))
+            for j, key in enumerate(keys):
+                made[("turned",) + key] = turned[:, j:]
 
-        def turn_da(e, j0, j1):
-            turn(("da", e, j0), [[da[e][b][:].bitcast(F32)[:, u * P:(u + 1) * P] for u in range(2)] for b in range(j0, j1)])
+        def turn_x(e, k0, k1):
+            turn(*[("x", e, k) for k in range(k0, k1)])
 
-        def take(key, turned, copy):
-            copy(out=turned, in_=banks[key][:].rearrange("p j u m -> p j m u"))
+        def take_x(e, k0, k1, copy):
+            take(copy, *[("x", e, k) for k in range(k0, k1)])
 
-        def take_x(e, j0, j1, copy):
-            take(("x", e, j0), x_turned[e][:, j0:j1], copy)
+        def turn_xx(k):
+            turn(*[("x", e, k) for e in range(E)])
 
-        def take_da(e, j0, j1, copy):
-            take(("da", e, j0), da_turned[e][:, j0:j1], copy)
+        def take_xx(k, copy):
+            take(copy, *[("x", e, k) for e in range(E)])
 
-        def quantize_turned(codes, scales, turned, j0, j1, fmt):
-            cols = slice(P * j0, P * j1)
-            values = turned[:, j0:j1].rearrange("p j m u -> p (j m u)").bitcast(BF16)
-            quantize(codes[:, cols], scales[:, cols], values, fmt)
+        def turn_da(e, b0, b1):
+            turn(*[("da", e, b) for b in range(b0, b1)])
 
-        def quantize_x(e, j0, j1):
-            if e not in x_codes:
-                x_codes.setdefault(e, keep.tile([P, K], U32, name="xc1", tag="a1_0", align_bytes=64))
-            quantize_turned(x_codes[e], x_scales[e], x_turned[e], j0, j1, E4M3)
+        def take_da(e, b0, b1, copy):
+            take(copy, *[("da", e, b) for b in range(b0, b1)])
 
-        def quantize_da(e, j0, j1):
-            quantize_turned(da_codes[e], da_scales[e], da_turned[e], j0, j1, E5M2)
+        def turned_values(key, count):
+            return made[("turned",) + key][:, 0:count].rearrange("p j m u -> p (j m u)").bitcast(BF16)
+
+        def quantize_x(e, k0, k1):
+            codes = fresh(on_vector, ("xc", e, k0), [P, (k1 - k0) * P], U32)
+            quantize(codes[:], x_scales[e][:, k0 * P:k1 * P], turned_values(("x", e, k0), k1 - k0), E4M3)
+            for k in range(k0, k1):
+                made[("x_codes", e, k)] = (codes[:, (k - k0) * P:(k - k0 + 1) * P], x_scales[e][:, k * P:(k + 1) * P])
+
+        def quantize_xx(k):
+            codes = fresh(on_vector, ("xxc", k), [P, E * P], U32)
+            scales = held("xxs%d" % k, [P, E * P], U8)
+            quantize(codes[:], scales[:], turned_values(("x", 0, k), E), E4M3)
+            for e in range(E):
+                made[("x_codes", e, k)] = (codes[:, e * P:(e + 1) * P], scales[:, e * P:(e + 1) * P])
+
+        def quantize_da(e, b0, b1):
+            if b0 % 2:
+                codes = made[("dc", e, b0 // 2)][:, P:HALF]
+            else:
+                codes = fresh(on_vector, ("dc", e, b0 // 2), [P, HALF], U32)[:, 0:(b1 - b0) * P]
+            quantize(codes, da_scales[e][:, b0 * P:b1 * P], turned_values(("da", e, b0), b1 - b0), E5M2)
 
         def product_out(e, k):
-            cols = slice(k * P, (k + 1) * P)
             acc = new_bank(("out", e, k), [P, H])
-            nc.tensor.matmul_mx(out=acc[:], lhsT=x_codes[e][:, cols].bitcast(E4M3), lhsT_scale=x_scales[e][:, cols],
-                                rhs=da_codes[e][:].bitcast(E5M2), rhs_scale=da_scales[e][:], start=True, stop=True)
+            codes, scales = made[("x_codes", e, k)]
+            for h in range(2):
+                nc.tensor.matmul_mx(out=acc[:, half(h)], lhsT=codes.bitcast(E4M3), lhsT_scale=scales,
+                                    rhs=made[("dc", e, h)][:].bitcast(E5M2), rhs_scale=da_scales[e][:, half(h)], start=True, stop=True)
 
         def take_out(e, k, copy):
-            copy(out=results[e][k][:], in_=banks[("out", e, k)][:])
+            copy(out=fresh(copy, ("res", e, k), [P, H], F32)[:], in_=banks[("out", e, k)][:])
 
-        def out_in_halves(e, k, copy):
-            for h in range(2):
-                copy(out=results[e][k][:, half(h)], in_=banks[("out", e, k)][:, half(h)])
-                nc.sync.dma_start(out[e, k * P:(k + 1) * P, half(h)], results[e][k][:, half(h)])
+        def product_half(e, h, k0, k1):
+            acc = new_bank(("out", e, h, k0), [P, k1 - k0, HALF])
+            for k in range(k0, k1):
+                codes, scales = made[("x_codes", e, k)]
+                nc.tensor.matmul_mx(out=acc[:, k - k0, :], lhsT=codes.bitcast(E4M3), lhsT_scale=scales,
+                                    rhs=made[("dc", e, h)][:].bitcast(E5M2), rhs_scale=da_scales[e][:, half(h)], start=True, stop=True)
+
+        def take_half(e, h, k0, k1, copy):
+            copy(out=fresh(copy, ("res", e, h, k0), [P, k1 - k0, HALF], F32)[:], in_=banks[("out", e, h, k0)][:])
+
+        def store_half(e, h, k0, k1):
+            nc.sync.dma_start(out[e, k0 * P:k1 * P, half(h)].rearrange("(k p) i -> p k i", p=P), made[("res", e, h, k0)][:])
 
         def store(e, k):
-            nc.sync.dma_start(out[e, k * P:(k + 1) * P, :], results[e][k][:])
+            nc.sync.dma_start(out[e, k * P:(k + 1) * P, :], made[("res", e, k)][:])
 
-        nc.vector.transpose(gate_turned[:], gate_runs[:])
-        on_vector(out=gate_wide[:], in_=gate_turned[:, 0:C // QUAD].unsqueeze(2).to_broadcast([P, C // QUAD, QUAD]))
-        for h in range(2):
-            nc.vector.transpose(gates[0][:, half(h)], gate_wide[:].rearrange("p c r -> p (c r)")[:, half(h)])
+        load_gate_runs()
+        load_dy(0)
+        load_offsets()
+        load_dy(1)
+        load_gate_column()
+        load_dy(2)
+        load_dy(3)
+        load_x(0)
+        load_x(1)
+        load_w(0)
+        load_x(2)
+        load_a(0, 0, 2)
+        load_a(0, 2, 4)
+        load_w(1)
+        load_a(1, 0, 2)
+        load_a(1, 2, 3)
+        load_a(1, 3, 4)
+        spread_gate0()
         spread(1)
-        take_gate(1, 0, C)
-        gather_g(0, 0, 0, HALF)
-        gather_g(0, 0, HALF, C)
-        gather_g(0,1)
-        for t in range(1,4):
-            for e in range(2):
-                gather_g(t,e)
-        round_x(0,0,512,on_scalar)
-        round_x(0,512,1024,on_scalar)
-        for e in range(2):
-            gather_x(0,e)
-        round_x(1,0,1024,on_scalar)
-        for e in range(2):
-            turn_x(e,0,1)
-            take_x(e,0,1,on_scalar)
-        for e in range(2):
-            gather_x(1,e)
-        round_x(2,0,512,on_scalar)
-        round_g(0,0,HALF,on_scalar)
-        round_g(0,HALF,C,on_vector)
-        round_g(1,0,3 * P,on_scalar)
-        round_g(1,3 * P,C,on_vector)
-        round_w(0,0,on_vector)
+        gather_g0(0, 0, HALF)
+        gather_g0(0, HALF, C)
+        for t in range(1, PACK):
+            gather_g0(t)
+        for t in range(PACK):
+            gather_dy1(t)
+
+        round_g0(0, C, on_vector)
+        gate_round_g1()
         quantize_g(0)
-        quantize_w(0,0)
+        for e in range(E):
+            gather_x(0, e)
+        turn_xx(0)
+        gather_x(1, 0)
+        turn_x(0, 1, 2)
+        take_xx(0, on_scalar)
+        round_w(0, 3, 4, on_scalar)
+        gather_x(1, 1)
+        round_w(0, 0, 2, on_vector)
+        round_w(0, 2, 3, on_vector)
+        quantize_w(0, 0, 2)
+        quantize_w(0, 2, 3)
+        quantize_w(0, 3, 4)
         quantize_g(1)
-        round_w(0,1,on_vector,0,P)
-        round_w(0,1,on_scalar,P,HALF)
-        for e in range(2):
-            turn_x(e,1,2)
-            take_x(e,1,2,on_scalar)
-        quantize_x(0,0,2)
-        quantize_w(0,1)
-        round_w(1,0,on_scalar)
-        round_x(2,512,1024,on_scalar)
-        round_w(1,1,on_scalar)
-        for b in range(2):
-            product_dh(0,b)
-            mask_dh(0,b)
-        quantize_w(1,0)
-        for b in range(2,4):
-            product_dh(0,b)
-            mask_dh(0,b)
-        quantize_w(1,1)
-        turn_da(0,0,2)
-        gather_x(2,0)
-        for b in range(2):
-            product_dh(1,b)
-            mask_dh(1,b)
-        take_da(0,0,2,on_scalar)
-        turn_da(0,2,4)
-        quantize_da(0,0,2)
-        take_da(0,2,4,on_scalar)
-        gather_x(2,1)
-        for b in range(2,4):
-            product_dh(1,b)
-        mask_dh(1,2)
-        quantize_da(0,2,4)
-        mask_dh(1,3)
-        quantize_x(1,0,2)
-        turn_x(0,2,3)
-        take_x(0,2,3,on_scalar)
-        quantize_x(0,2,3)
-        turn_da(1,0,2)
-        take_da(1,0,2,on_scalar)
-        turn_da(1,2,3)
-        take_da(1,2,3,on_scalar)
-        for k in range(2):
-            product_out(0,k)
-        turn_da(1,3,4)
-        take_da(1,3,4,on_vector)
-        turn_x(1,2,3)
-        product_out(0,2)
-        quantize_da(1,0,2)
-        quantize_da(1,2,3)
-        quantize_da(1,3,4)
-        take_x(1,2,3,on_vector)
-        quantize_x(1,2,3)
-        for k in range(3):
-            take_out(0,k,on_scalar)
-            store(0,k)
-        for k in range(3):
-            product_out(1,k)
-            take_out(1,k,on_scalar if k!=1 else on_vector)
-            store(1,k)
+        quantize_xx(0)
+        product_dh(0, 0)
+        product_dh(0, 1)
+        turn_x(1, 1, 2)
+        gather_x(2, 0)
+        take_x(0, 1, 2, on_scalar)
+        gather_x(2, 1)
+        take_x(1, 1, 2, on_scalar)
+        product_dh(0, 2)
+        product_dh(0, 3)
+        mask_dh(0, 0)
+        mask_dh(0, 1)
+        turn_x(0, 2, 3)
+        turn_da(0, 0, 2)
+        turn_x(1, 2, 3)
+        take_x(0, 2, 3, on_scalar)
+        take_da(0, 0, 2, on_scalar)
+        mask_dh(0, 2)
+        mask_dh(0, 3)
+        turn_da(0, 2, 4)
+        quantize_x(0, 1, 2)
+        quantize_x(0, 2, 3)
+        round_w(1, 2, 4, on_scalar)
+        take_da(0, 2, 4, on_scalar)
+        take_x(1, 2, 3, on_scalar)
+        round_w(1, 0, 1, on_vector)
+        round_w(1, 1, 2, on_vector)
+        quantize_w(1, 0, 1)
+        quantize_w(1, 1, 2)
+        product_dh(1, 0)
+        product_dh(1, 1)
+        quantize_da(0, 0, 2)
+        quantize_w(1, 2, 4)
+        quantize_da(0, 2, 4)
+        product_dh(1, 2)
+        product_out(0, 0)
+        product_dh(1, 3)
+        product_out(0, 1)
+        mask_dh(1, 0)
+        mask_dh(1, 1)
+        take_out(0, 0, on_scalar)
+        store(0, 0)
+        take_out(0, 1, on_scalar)
+        store(0, 1)
+        product_out(0, 2)
+        turn_da(1, 0, 2)
+        mask_dh(1, 2)
+        mask_dh(1, 3)
+        take_da(1, 0, 2, on_scalar)
+        turn_da(1, 2, 3)
+        turn_da(1, 3, 4)
+        take_out(0, 2, on_scalar)
+        store(0, 2)
+        quantize_x(1, 1, 2)
+        quantize_x(1, 2, 3)
+        quantize_da(1, 0, 2)
+        take_da(1, 2, 3, on_vector)
+        take_da(1, 3, 4, on_scalar)
+        product_half(1, 0, 0, 2)
+        product_half(1, 0, 2, 3)
+        quantize_da(1, 2, 3)
+        quantize_da(1, 3, 4)
+        product_half(1, 1, 0, 2)
+        product_half(1, 1, 2, 3)
+        take_half(1, 0, 0, 2, on_scalar)
+        store_half(1, 0, 0, 2)
+        take_half(1, 0, 2, 3, on_vector)
+        store_half(1, 0, 2, 3)
+        take_half(1, 1, 0, 2, on_vector)
+        store_half(1, 1, 0, 2)
+        take_half(1, 1, 2, 3, on_scalar)
+        store_half(1, 1, 2, 3)

@@ -146,11 +146,13 @@ def tile_moe_mlp_relu_kernel(tc, xT, dyT, a, w2, gate, offs, out):
             nc.scalar.activation(g32[1][:, t, :], dy[t][:].indirect(slots(1)), COPY)
 
         def gate_round_g1():
-            gate1 = banks[("gate", 1)][:].rearrange("p q n -> p n q").unsqueeze(2)
-            nc.vector.tensor_tensor(
-                g16[1][:].rearrange("p (n q) t -> p n t q", q=PACK),
-                g32[1][:].rearrange("p t (n q) -> p n t q", q=PACK),
-                gate1.to_broadcast([P, P, PACK, PACK]), MULT)
+            for j in range(2):
+                pair = slice(2 * j, 2 * j + 2)
+                gate1 = banks[("gate", 1)][:, pair, :].rearrange("p s n -> p n s").unsqueeze(2)
+                nc.vector.tensor_tensor(
+                    g16[1][:].rearrange("p (n q) t -> p n t q", q=PACK)[:, :, :, pair],
+                    g32[1][:].rearrange("p t (n q) -> p n t q", q=PACK)[:, :, :, pair],
+                    gate1.to_broadcast([P, P, PACK, 2]), MULT)
 
         def round_g0(c0, c1, copy):
             interleave(copy, g16[0][:, c0:c1, :], g32[0][:, :, c0:c1])
@@ -304,62 +306,57 @@ def tile_moe_mlp_relu_kernel(tc, xT, dyT, a, w2, gate, offs, out):
         quantize_w(0, 3, 4)
         quantize_g(1)
         quantize_xx(0)
-        product_dh(0, 0)
-        product_dh(0, 1)
+        for b in range(H_TILES):
+            product_dh(0, b)
         turn_x(1, 1, 2)
         gather_x(2, 0)
         take_x(0, 1, 2, on_scalar)
         gather_x(2, 1)
         take_x(1, 1, 2, on_scalar)
-        product_dh(0, 2)
-        product_dh(0, 3)
-        mask_dh(0, 0)
-        mask_dh(0, 1)
-        turn_x(0, 2, 3)
+        for b in range(H_TILES):
+            mask_dh(0, b)
+        turn_xx(2)
         turn_da(0, 0, 2)
-        turn_x(1, 2, 3)
-        take_x(0, 2, 3, on_scalar)
-        take_da(0, 0, 2, on_scalar)
-        mask_dh(0, 2)
-        mask_dh(0, 3)
         turn_da(0, 2, 4)
-        quantize_x(0, 1, 2)
-        quantize_x(0, 2, 3)
-        round_w(1, 2, 4, on_scalar)
+        take_xx(2, on_scalar)
+        take_da(0, 0, 2, on_scalar)
         take_da(0, 2, 4, on_scalar)
-        take_x(1, 2, 3, on_scalar)
+        quantize_x(0, 1, 2)
+        quantize_x(1, 1, 2)
+        round_w(1, 2, 3, on_scalar)
+        round_w(1, 3, 4, on_scalar)
         round_w(1, 0, 1, on_vector)
-        round_w(1, 1, 2, on_vector)
+        quantize_xx(2)
         quantize_w(1, 0, 1)
+        round_w(1, 1, 2, on_vector)
+        quantize_da(0, 0, 2)
         quantize_w(1, 1, 2)
+        quantize_da(0, 2, 4)
+        quantize_w(1, 2, 3)
         product_dh(1, 0)
         product_dh(1, 1)
-        quantize_da(0, 0, 2)
-        quantize_w(1, 2, 4)
-        quantize_da(0, 2, 4)
-        product_dh(1, 2)
         product_out(0, 0)
-        product_dh(1, 3)
-        product_out(0, 1)
+        product_dh(1, 2)
         mask_dh(1, 0)
+        quantize_w(1, 3, 4)
+        product_out(0, 1)
+        product_dh(1, 3)
+        product_out(0, 2)
         mask_dh(1, 1)
         take_out(0, 0, on_scalar)
         store(0, 0)
         take_out(0, 1, on_scalar)
         store(0, 1)
-        product_out(0, 2)
         turn_da(1, 0, 2)
         mask_dh(1, 2)
         mask_dh(1, 3)
         take_da(1, 0, 2, on_scalar)
         turn_da(1, 2, 3)
         turn_da(1, 3, 4)
-        take_out(0, 2, on_scalar)
+        take_out(0, 2, on_vector)
         store(0, 2)
-        quantize_x(1, 1, 2)
-        quantize_x(1, 2, 3)
         quantize_da(1, 0, 2)
-        take_da(1, 2, 3, on_vector)
+        take_da(1, 2, 3, on_scalar)
         take_da(1, 3, 4, on_scalar)
         product_half(1, 0, 0, 2)
         product_half(1, 0, 2, 3)

@@ -26,7 +26,7 @@ H_TILES = H // P
 LIST_COLS = C // 16
 HALF = 2 * P
 QUAD = 32
-VECTOR_TILES = 34
+VECTOR_TILES = 38
 SCALAR_TILES = 26
 BANKS = 8
 
@@ -53,6 +53,7 @@ def tile_moe_mlp_relu_kernel(tc, xT, dyT, a, w2, gate, offs, out):
 
         offsets = keep.tile([P, E * LIST_COLS], U16, name="offsets")
         gate0 = held("gate0", [P, C], F32)
+        gate1 = held("gate1", [P, C], F32)
         dy = [held("dy%d" % t, [P, T], F32) for t in range(PACK)]
         x32 = [held("x32_%d" % k, [P, T], F32) for k in range(K_TILES)]
         w32 = [held("w32_%d" % e, [P, PACK, H], F32) for e in range(E)]
@@ -130,6 +131,9 @@ def tile_moe_mlp_relu_kernel(tc, xT, dyT, a, w2, gate, offs, out):
         def half(h):
             return slice(h * HALF, (h + 1) * HALF)
 
+        def pairs(columns, u):
+            return columns.rearrange("p (r u s) -> p r u s", u=2, s=2)[:, :, u, :]
+
         def quantize(codes, scales, values, fmt):
             nc.vector.quantize_mx(out=codes.bitcast(fmt), scales=scales, in_=values)
 
@@ -145,14 +149,14 @@ def tile_moe_mlp_relu_kernel(tc, xT, dyT, a, w2, gate, offs, out):
         def gather_dy1(t):
             nc.scalar.activation(g32[1][:, t, :], dy[t][:].indirect(slots(1)), COPY)
 
+        def take_gate1():
+            nc.scalar.activation(gate1[:].rearrange("p (n q) -> p n q", q=PACK), banks[("gate", 1)][:].rearrange("p q n -> p n q"), COPY)
+
         def gate_round_g1():
-            for j in range(2):
-                pair = slice(2 * j, 2 * j + 2)
-                gate1 = banks[("gate", 1)][:, pair, :].rearrange("p s n -> p n s").unsqueeze(2)
-                nc.vector.tensor_tensor(
-                    g16[1][:].rearrange("p (n q) t -> p n t q", q=PACK)[:, :, :, pair],
-                    g32[1][:].rearrange("p t (n q) -> p n t q", q=PACK)[:, :, :, pair],
-                    gate1.to_broadcast([P, P, PACK, 2]), MULT)
+            nc.vector.tensor_tensor(
+                g16[1][:].rearrange("p (m s) t -> p m t s", s=2),
+                g32[1][:].rearrange("p t (m s) -> p m t s", s=2),
+                gate1[:].rearrange("p (m s) -> p m s", s=2).unsqueeze(2).to_broadcast([P, HALF, PACK, 2]), MULT)
 
         def round_g0(c0, c1, copy):
             interleave(copy, g16[0][:, c0:c1, :], g32[0][:, :, c0:c1])
@@ -176,18 +180,21 @@ def tile_moe_mlp_relu_kernel(tc, xT, dyT, a, w2, gate, offs, out):
                                 rhs=made[("gc", e)][:].bitcast(E5M2), rhs_scale=g_scales[e][:], start=True, stop=True)
 
         def mask_dh(e, b):
-            da = fresh(on_vector, ("da", e, b), [P, C], BF16)
-            nc.vector.scalar_tensor_tensor(da[:], saved[(e, b)], 0.0, banks[("dh", e, b)][:], IS_GT, MULT)
+            da = fresh(on_vector, ("da", e, b), [P, 2, P, 2], BF16)
+            for u in range(2):
+                nc.vector.scalar_tensor_tensor(da[:, u], pairs(saved[(e, b)], u), 0.0, pairs(banks[("dh", e, b)][:], u), IS_GT, MULT)
+            made[("words", "da", e, b)] = [da[:, u].rearrange("p r s -> p (r s)").bitcast(F32) for u in range(2)]
 
         def gather_x(k, e):
             x_slots = fresh(on_scalar, ("x", e, k), [P, C], BF16)
             nc.scalar.activation(x_slots[:], x32[k][:].indirect(slots(e)), COPY)
+            made[("words", "x", e, k)] = [x_slots[:].bitcast(F32)[:, u:2 * P:2] for u in range(2)]
 
         def turn(*keys):
             bank = new_bank(keys, [P, len(keys), 2, P])
             for j, key in enumerate(keys):
                 for u in range(2):
-                    nc.tensor.transpose(bank[:, j, u, :], made[key][:].bitcast(F32)[:, u:2 * P:2], ident[:])
+                    nc.tensor.transpose(bank[:, j, u, :], made[("words",) + key][u], ident[:])
 
         def take(copy, *keys):
             turned = fresh(copy, ("turned",) + keys[0], [P, len(keys), P, 2], F32)
@@ -239,7 +246,7 @@ def tile_moe_mlp_relu_kernel(tc, xT, dyT, a, w2, gate, offs, out):
         def product_out(e, k):
             acc = new_bank(("out", e, k), [P, H])
             codes, scales = made[("x_codes", e, k)]
-            for h in range(2):
+            for h in (1, 0):
                 nc.tensor.matmul_mx(out=acc[:, half(h)], lhsT=codes.bitcast(E4M3), lhsT_scale=scales,
                                     rhs=made[("dc", e, h)][:].bitcast(E5M2), rhs_scale=da_scales[e][:, half(h)], start=True, stop=True)
 
@@ -263,10 +270,10 @@ def tile_moe_mlp_relu_kernel(tc, xT, dyT, a, w2, gate, offs, out):
             nc.sync.dma_start(out[e, k * P:(k + 1) * P, :], made[("res", e, k)][:])
 
         load_gate_runs()
+        load_gate_column()
         load_dy(0)
         load_offsets()
         load_dy(1)
-        load_gate_column()
         load_dy(2)
         load_dy(3)
         load_x(0)
@@ -281,6 +288,7 @@ def tile_moe_mlp_relu_kernel(tc, xT, dyT, a, w2, gate, offs, out):
         load_a(1, 3, 4)
         spread_gate0()
         spread(1)
+        take_gate1()
         gather_g0(0, 0, HALF)
         gather_g0(0, HALF, C)
         for t in range(1, PACK):
@@ -296,8 +304,8 @@ def tile_moe_mlp_relu_kernel(tc, xT, dyT, a, w2, gate, offs, out):
         turn_xx(0)
         gather_x(1, 0)
         turn_x(0, 1, 2)
-        take_xx(0, on_scalar)
         round_w(0, 3, 4, on_scalar)
+        take_xx(0, on_scalar)
         gather_x(1, 1)
         round_w(0, 0, 2, on_vector)
         round_w(0, 2, 3, on_vector)
@@ -308,67 +316,69 @@ def tile_moe_mlp_relu_kernel(tc, xT, dyT, a, w2, gate, offs, out):
         quantize_xx(0)
         for b in range(H_TILES):
             product_dh(0, b)
-        turn_x(1, 1, 2)
         gather_x(2, 0)
         take_x(0, 1, 2, on_scalar)
-        gather_x(2, 1)
-        take_x(1, 1, 2, on_scalar)
         for b in range(H_TILES):
             mask_dh(0, b)
-        turn_xx(2)
         turn_da(0, 0, 2)
+        turn_x(1, 1, 2)
         turn_da(0, 2, 4)
-        take_xx(2, on_scalar)
+        turn_x(0, 2, 3)
         take_da(0, 0, 2, on_scalar)
+        take_x(1, 1, 2, on_scalar)
         take_da(0, 2, 4, on_scalar)
-        quantize_x(0, 1, 2)
-        quantize_x(1, 1, 2)
-        round_w(1, 2, 3, on_scalar)
+        take_x(0, 2, 3, on_scalar)
         round_w(1, 3, 4, on_scalar)
+        gather_x(2, 1)
+        quantize_x(0, 1, 2)
         round_w(1, 0, 1, on_vector)
-        quantize_xx(2)
-        quantize_w(1, 0, 1)
         round_w(1, 1, 2, on_vector)
+        quantize_w(1, 0, 1)
         quantize_da(0, 0, 2)
         quantize_w(1, 1, 2)
-        quantize_da(0, 2, 4)
-        quantize_w(1, 2, 3)
         product_dh(1, 0)
         product_dh(1, 1)
+        round_w(1, 2, 3, on_vector)
+        quantize_x(0, 2, 3)
+        quantize_da(0, 2, 4)
+        quantize_w(1, 2, 3)
+        quantize_w(1, 3, 4)
         product_out(0, 0)
         product_dh(1, 2)
-        mask_dh(1, 0)
-        quantize_w(1, 3, 4)
         product_out(0, 1)
         product_dh(1, 3)
         product_out(0, 2)
+        mask_dh(1, 0)
         mask_dh(1, 1)
+        turn_da(1, 0, 2)
+        turn_x(1, 2, 3)
         take_out(0, 0, on_scalar)
         store(0, 0)
         take_out(0, 1, on_scalar)
         store(0, 1)
-        turn_da(1, 0, 2)
         mask_dh(1, 2)
-        mask_dh(1, 3)
-        take_da(1, 0, 2, on_scalar)
         turn_da(1, 2, 3)
+        take_da(1, 0, 2, on_scalar)
+        take_x(1, 2, 3, on_scalar)
+        mask_dh(1, 3)
         turn_da(1, 3, 4)
-        take_out(0, 2, on_vector)
+        quantize_x(1, 1, 2)
+        take_da(1, 2, 3, on_scalar)
+        take_out(0, 2, on_scalar)
         store(0, 2)
         quantize_da(1, 0, 2)
-        take_da(1, 2, 3, on_scalar)
-        take_da(1, 3, 4, on_scalar)
+        quantize_x(1, 2, 3)
+        take_da(1, 3, 4, on_vector)
         product_half(1, 0, 0, 2)
         product_half(1, 0, 2, 3)
         quantize_da(1, 2, 3)
         quantize_da(1, 3, 4)
-        product_half(1, 1, 0, 2)
-        product_half(1, 1, 2, 3)
+        for k in range(K_TILES):
+            product_half(1, 1, k, k + 1)
         take_half(1, 0, 0, 2, on_scalar)
         store_half(1, 0, 0, 2)
         take_half(1, 0, 2, 3, on_vector)
         store_half(1, 0, 2, 3)
-        take_half(1, 1, 0, 2, on_vector)
-        store_half(1, 1, 0, 2)
-        take_half(1, 1, 2, 3, on_scalar)
-        store_half(1, 1, 2, 3)
+        for k in range(K_TILES):
+            take_half(1, 1, k, k + 1, on_vector if k == 1 else on_scalar)
+            store_half(1, 1, k, k + 1)

@@ -81,7 +81,7 @@ def tile_moe_mlp_relu_kernel(tc, xT, dyT, a, w2, gate, offs, out):
         column = held("column", [P, QUAD], F32)
         row = held("row", [P, QUAD], F32)
         nc.vector.memset(ones[:], 1.0)
-        nc.scalar.activation(ident[:].rearrange("p (q c) -> p q c", c=QUAD), ones[:].unsqueeze(1).to_broadcast([P, P // QUAD, QUAD]), COPY, scale=0.0)
+        nc.vector.memset(ident[:], 0.0)
         nc.vector.tensor_tensor_scan(column[:], ones[:], ones[:], 0.0, MULT, ADD)
         nc.vector.transpose(row[:], column[:])
         for q0 in range(0, P, QUAD):

@@ -26,8 +26,8 @@ H_TILES = H // P
 LIST_COLS = C // 16
 HALF = 2 * P
 QUAD = 32
-VECTOR_TILES = 38
-SCALAR_TILES = 26
+VECTOR_TILES = 40
+SCALAR_TILES = 23
 BANKS = 8
 
 
@@ -139,7 +139,9 @@ def tile_moe_mlp_relu_kernel(tc, xT, dyT, a, w2, gate, offs, out):
 
         def spread_gate0():
             nc.vector.transpose(gate_turned[:], gate_runs[:])
-            on_vector(out=gate_wide[:], in_=gate_turned[:, 0:C // QUAD].unsqueeze(2).to_broadcast([P, C // QUAD, QUAD]))
+            for h in range(2):
+                runs = slice(h * HALF // QUAD, (h + 1) * HALF // QUAD)
+                on_vector(out=gate_wide[:, runs, :], in_=gate_turned[:, runs].unsqueeze(2).to_broadcast([P, HALF // QUAD, QUAD]))
             for h in range(2):
                 nc.vector.transpose(gate0[:, half(h)], gate_wide[:].rearrange("p c r -> p (c r)")[:, half(h)])
 
@@ -291,12 +293,15 @@ def tile_moe_mlp_relu_kernel(tc, xT, dyT, a, w2, gate, offs, out):
         take_gate1()
         gather_g0(0, 0, HALF)
         gather_g0(0, HALF, C)
-        for t in range(1, PACK):
+        for t in range(1, PACK - 1):
             gather_g0(t)
+        gather_g0(PACK - 1, 0, HALF)
+        gather_g0(PACK - 1, HALF, C)
         for t in range(PACK):
             gather_dy1(t)
 
-        round_g0(0, C, on_vector)
+        round_g0(0, HALF, on_vector)
+        round_g0(HALF, C, on_vector)
         gate_round_g1()
         quantize_g(0)
         for e in range(E):
@@ -362,23 +367,20 @@ def tile_moe_mlp_relu_kernel(tc, xT, dyT, a, w2, gate, offs, out):
         take_x(1, 2, 3, on_scalar)
         mask_dh(1, 3)
         turn_da(1, 3, 4)
-        quantize_x(1, 1, 2)
-        take_da(1, 2, 3, on_scalar)
-        take_out(0, 2, on_scalar)
+        take_out(0, 2, on_vector)
         store(0, 2)
         quantize_da(1, 0, 2)
+        quantize_x(1, 1, 2)
         quantize_x(1, 2, 3)
-        take_da(1, 3, 4, on_vector)
-        product_half(1, 0, 0, 2)
-        product_half(1, 0, 2, 3)
+        take_da(1, 2, 3, on_scalar)
+        take_da(1, 3, 4, on_scalar)
+        for k in range(K_TILES):
+            product_half(1, 0, k, k + 1)
         quantize_da(1, 2, 3)
         quantize_da(1, 3, 4)
         for k in range(K_TILES):
             product_half(1, 1, k, k + 1)
-        take_half(1, 0, 0, 2, on_scalar)
-        store_half(1, 0, 0, 2)
-        take_half(1, 0, 2, 3, on_vector)
-        store_half(1, 0, 2, 3)
-        for k in range(K_TILES):
-            take_half(1, 1, k, k + 1, on_vector if k == 1 else on_scalar)
-            store_half(1, 1, k, k + 1)
+        for h in range(2):
+            for k in range(K_TILES):
+                take_half(1, h, k, k + 1, on_vector if (k + h) % 2 else on_scalar)
+                store_half(1, h, k, k + 1)

@@ -25,24 +25,25 @@ K_TILES = K // P
 H_TILES = H // P
 LIST_COLS = C // 16
 HALF = 2 * P
+G0_ON_SCALAR = C // 8
 QUAD = 32
-VECTOR_TILES = 40
-SCALAR_TILES = 23
+VECTOR_TILES = 34
+SCALAR_TILES = 24
 BANKS = 8
 
 
 def interleave(copy, dst, src):
-    copy(out=dst.rearrange("p (c i) t -> p c t i", i=4), in_=src.rearrange("p t (c i) -> p c t i", i=4))
+    copy(dst.rearrange("p (c i) t -> p c t i", i=4), src.rearrange("p t (c i) -> p c t i", i=4))
 
 
 def tile_moe_mlp_relu_kernel(tc, xT, dyT, a, w2, gate, offs, out):
     nc = tc.nc
 
-    def on_scalar(out, in_):
-        nc.scalar.copy(out=out, in_=in_)
+    def on_scalar(dst, src):
+        nc.scalar.copy(out=dst, in_=src)
 
-    def on_vector(out, in_):
-        nc.vector.tensor_copy(out=out, in_=in_)
+    def on_vector(dst, src):
+        nc.vector.tensor_copy(out=dst, in_=src)
 
     with ExitStack() as ctx:
         keep = ctx.enter_context(tc.tile_pool(name="keep", bufs=1))
@@ -53,7 +54,6 @@ def tile_moe_mlp_relu_kernel(tc, xT, dyT, a, w2, gate, offs, out):
 
         offsets = keep.tile([P, E * LIST_COLS], U16, name="offsets")
         gate0 = held("gate0", [P, C], F32)
-        gate1 = held("gate1", [P, C], F32)
         dy = [held("dy%d" % t, [P, T], F32) for t in range(PACK)]
         x32 = [held("x32_%d" % k, [P, T], F32) for k in range(K_TILES)]
         w32 = [held("w32_%d" % e, [P, PACK, H], F32) for e in range(E)]
@@ -66,13 +66,12 @@ def tile_moe_mlp_relu_kernel(tc, xT, dyT, a, w2, gate, offs, out):
         gate_runs = held("gate_runs", [P, QUAD], F32)
         gate_turned = held("gate_turned", [P, QUAD], F32)
         gate_wide = held("gate_wide", [P, C // QUAD, QUAD], F32)
-        x_scales = [held("xsc%d" % e, [P, K], U8) for e in range(E)]
         da_scales = [held("ds%d" % e, [P, H], U8) for e in range(E)]
 
         made = {}
 
-        def fresh(copy, key, shape, dtype):
-            tag, bufs = ("by_vector", VECTOR_TILES) if copy is on_vector else ("by_scalar", SCALAR_TILES)
+        def fresh(writer, key, shape, dtype):
+            tag, bufs = ("by_vector", VECTOR_TILES) if writer is on_vector else ("by_scalar", SCALAR_TILES)
             made[key] = keep.tile(shape, dtype, name="_".join(str(part) for part in key), tag=tag, bufs=bufs, align_bytes=64)
             return made[key]
 
@@ -84,9 +83,11 @@ def tile_moe_mlp_relu_kernel(tc, xT, dyT, a, w2, gate, offs, out):
         nc.vector.memset(ident[:], 0.0)
         nc.vector.tensor_tensor_scan(column[:], ones[:], ones[:], 0.0, MULT, ADD)
         nc.vector.transpose(row[:], column[:])
+        diagonal = held("diagonal", [P, QUAD], F32)
+        nc.vector.tensor_tensor(diagonal[:], column[:], row[:], IS_EQUAL)
         for q0 in range(0, P, QUAD):
             part = slice(q0, q0 + QUAD)
-            nc.vector.tensor_tensor(ident[part, part], column[part, :], row[part, :], IS_EQUAL)
+            nc.scalar.activation(ident[part, part], diagonal[part, :], COPY)
 
         dy_rows = dyT.rearrange("(p t) c -> t p c", t=PACK)
 
@@ -123,11 +124,6 @@ def tile_moe_mlp_relu_kernel(tc, xT, dyT, a, w2, gate, offs, out):
         def slots(e, c0=0, c1=C):
             return offsets[:, (e * C + c0) // 16:(e * C + c1) // 16]
 
-        def spread(e):
-            bank = new_bank(("gate", e), [P, PACK, P])
-            for q in range(PACK):
-                nc.tensor.transpose(bank[:, q, :], gate_column[:, q:q + 1].to_broadcast([P, P]), ident[:])
-
         def half(h):
             return slice(h * HALF, (h + 1) * HALF)
 
@@ -141,9 +137,14 @@ def tile_moe_mlp_relu_kernel(tc, xT, dyT, a, w2, gate, offs, out):
             nc.vector.transpose(gate_turned[:], gate_runs[:])
             for h in range(2):
                 runs = slice(h * HALF // QUAD, (h + 1) * HALF // QUAD)
-                on_vector(out=gate_wide[:, runs, :], in_=gate_turned[:, runs].unsqueeze(2).to_broadcast([P, HALF // QUAD, QUAD]))
+                on_vector(gate_wide[:, runs, :], gate_turned[:, runs].unsqueeze(2).to_broadcast([P, HALF // QUAD, QUAD]))
             for h in range(2):
                 nc.vector.transpose(gate0[:, half(h)], gate_wide[:].rearrange("p c r -> p (c r)")[:, half(h)])
+
+        def spread_gate1():
+            bank = new_bank("gate1", [P, PACK, P])
+            for q in range(PACK):
+                nc.tensor.transpose(bank[:, q, :], gate_column[:, q:q + 1].to_broadcast([P, P]), ident[:])
 
         def gather_g0(t, c0=0, c1=C):
             nc.vector.tensor_tensor(g32[0][:, t, c0:c1], dy[t][:].indirect(slots(0, c0, c1)), gate0[:, c0:c1], MULT)
@@ -151,14 +152,14 @@ def tile_moe_mlp_relu_kernel(tc, xT, dyT, a, w2, gate, offs, out):
         def gather_dy1(t):
             nc.scalar.activation(g32[1][:, t, :], dy[t][:].indirect(slots(1)), COPY)
 
-        def take_gate1():
-            nc.scalar.activation(gate1[:].rearrange("p (n q) -> p n q", q=PACK), banks[("gate", 1)][:].rearrange("p q n -> p n q"), COPY)
-
         def gate_round_g1():
-            nc.vector.tensor_tensor(
-                g16[1][:].rearrange("p (m s) t -> p m t s", s=2),
-                g32[1][:].rearrange("p t (m s) -> p m t s", s=2),
-                gate1[:].rearrange("p (m s) -> p m s", s=2).unsqueeze(2).to_broadcast([P, HALF, PACK, 2]), MULT)
+            for j in range(2):
+                pair = slice(2 * j, 2 * j + 2)
+                gate1 = banks["gate1"][:, pair, :].rearrange("p s n -> p n s").unsqueeze(2)
+                nc.vector.tensor_tensor(
+                    g16[1][:].rearrange("p (n q) t -> p n t q", q=PACK)[:, :, :, pair],
+                    g32[1][:].rearrange("p t (n q) -> p n t q", q=PACK)[:, :, :, pair],
+                    gate1.to_broadcast([P, P, PACK, 2]), MULT)
 
         def round_g0(c0, c1, copy):
             interleave(copy, g16[0][:, c0:c1, :], g32[0][:, :, c0:c1])
@@ -200,84 +201,69 @@ def tile_moe_mlp_relu_kernel(tc, xT, dyT, a, w2, gate, offs, out):
 
         def take(copy, *keys):
             turned = fresh(copy, ("turned",) + keys[0], [P, len(keys), P, 2], F32)
-            copy(out=turned[:], in_=banks[keys][:].rearrange("p j u m -> p j m u"))
-            for j, key in enumerate(keys):
-                made[("turned",) + key] = turned[:, j:]
+            copy(turned[:], banks[keys][:].rearrange("p j u m -> p j m u"))
 
-        def turn_x(e, k0, k1):
-            turn(*[("x", e, k) for k in range(k0, k1)])
+        def turned_values(key):
+            return made[("turned",) + key][:].rearrange("p j m u -> p (j m u)").bitcast(BF16)
 
-        def take_x(e, k0, k1, copy):
-            take(copy, *[("x", e, k) for k in range(k0, k1)])
+        def x_keys(k, experts):
+            return [("x", e, k) for e in experts]
 
-        def turn_xx(k):
-            turn(*[("x", e, k) for e in range(E)])
+        def turn_x(k, *experts):
+            turn(*x_keys(k, experts))
 
-        def take_xx(k, copy):
-            take(copy, *[("x", e, k) for e in range(E)])
+        def take_x(k, *experts):
+            take(on_scalar, *x_keys(k, experts))
+
+        def quantize_x(k, *experts):
+            codes = fresh(on_vector, ("xc", experts[0], k), [P, len(experts) * P], U32)
+            scales = held("xs%d_%d" % (experts[0], k), [P, len(experts) * P], U8)
+            quantize(codes[:], scales[:], turned_values(("x", experts[0], k)), E4M3)
+            for j, e in enumerate(experts):
+                made[("x_codes", e, k)] = (codes[:, j * P:(j + 1) * P], scales[:, j * P:(j + 1) * P])
 
         def turn_da(e, b0, b1):
             turn(*[("da", e, b) for b in range(b0, b1)])
 
-        def take_da(e, b0, b1, copy):
-            take(copy, *[("da", e, b) for b in range(b0, b1)])
-
-        def turned_values(key, count):
-            return made[("turned",) + key][:, 0:count].rearrange("p j m u -> p (j m u)").bitcast(BF16)
-
-        def quantize_x(e, k0, k1):
-            codes = fresh(on_vector, ("xc", e, k0), [P, (k1 - k0) * P], U32)
-            quantize(codes[:], x_scales[e][:, k0 * P:k1 * P], turned_values(("x", e, k0), k1 - k0), E4M3)
-            for k in range(k0, k1):
-                made[("x_codes", e, k)] = (codes[:, (k - k0) * P:(k - k0 + 1) * P], x_scales[e][:, k * P:(k + 1) * P])
-
-        def quantize_xx(k):
-            codes = fresh(on_vector, ("xxc", k), [P, E * P], U32)
-            scales = held("xxs%d" % k, [P, E * P], U8)
-            quantize(codes[:], scales[:], turned_values(("x", 0, k), E), E4M3)
-            for e in range(E):
-                made[("x_codes", e, k)] = (codes[:, e * P:(e + 1) * P], scales[:, e * P:(e + 1) * P])
+        def take_da(e, b0, b1):
+            take(on_scalar, *[("da", e, b) for b in range(b0, b1)])
 
         def quantize_da(e, b0, b1):
             if b0 % 2:
                 codes = made[("dc", e, b0 // 2)][:, P:HALF]
             else:
                 codes = fresh(on_vector, ("dc", e, b0 // 2), [P, HALF], U32)[:, 0:(b1 - b0) * P]
-            quantize(codes, da_scales[e][:, b0 * P:b1 * P], turned_values(("da", e, b0), b1 - b0), E5M2)
+            quantize(codes, da_scales[e][:, b0 * P:b1 * P], turned_values(("da", e, b0)), E5M2)
 
-        def product_out(e, k):
-            acc = new_bank(("out", e, k), [P, H])
+        def product_pass(acc, e, h, k):
             codes, scales = made[("x_codes", e, k)]
+            nc.tensor.matmul_mx(out=acc, lhsT=codes.bitcast(E4M3), lhsT_scale=scales,
+                                rhs=made[("dc", e, h)][:].bitcast(E5M2), rhs_scale=da_scales[e][:, half(h)], start=True, stop=True)
+
+        def product_out0(k):
+            acc = new_bank(("out", 0, k), [P, H])
             for h in (1, 0):
-                nc.tensor.matmul_mx(out=acc[:, half(h)], lhsT=codes.bitcast(E4M3), lhsT_scale=scales,
-                                    rhs=made[("dc", e, h)][:].bitcast(E5M2), rhs_scale=da_scales[e][:, half(h)], start=True, stop=True)
+                product_pass(acc[:, half(h)], 0, h, k)
 
-        def take_out(e, k, copy):
-            copy(out=fresh(copy, ("res", e, k), [P, H], F32)[:], in_=banks[("out", e, k)][:])
+        def finish_out0(k, copy):
+            result = fresh(copy, ("res", 0, k), [P, H], F32)
+            copy(result[:], banks[("out", 0, k)][:])
+            nc.sync.dma_start(out[0, k * P:(k + 1) * P, :], result[:])
 
-        def product_half(e, h, k0, k1):
-            acc = new_bank(("out", e, h, k0), [P, k1 - k0, HALF])
-            for k in range(k0, k1):
-                codes, scales = made[("x_codes", e, k)]
-                nc.tensor.matmul_mx(out=acc[:, k - k0, :], lhsT=codes.bitcast(E4M3), lhsT_scale=scales,
-                                    rhs=made[("dc", e, h)][:].bitcast(E5M2), rhs_scale=da_scales[e][:, half(h)], start=True, stop=True)
+        def product_out1(h, k):
+            product_pass(new_bank(("out", 1, h, k), [P, HALF])[:], 1, h, k)
 
-        def take_half(e, h, k0, k1, copy):
-            copy(out=fresh(copy, ("res", e, h, k0), [P, k1 - k0, HALF], F32)[:], in_=banks[("out", e, h, k0)][:])
-
-        def store_half(e, h, k0, k1):
-            nc.sync.dma_start(out[e, k0 * P:k1 * P, half(h)].rearrange("(k p) i -> p k i", p=P), made[("res", e, h, k0)][:])
-
-        def store(e, k):
-            nc.sync.dma_start(out[e, k * P:(k + 1) * P, :], made[("res", e, k)][:])
+        def finish_out1(h, k, copy):
+            result = fresh(copy, ("res", 1, h, k), [P, HALF], F32)
+            copy(result[:], banks[("out", 1, h, k)][:])
+            nc.sync.dma_start(out[1, k * P:(k + 1) * P, half(h)], result[:])
 
         load_gate_runs()
-        load_gate_column()
         load_dy(0)
         load_offsets()
-        load_dy(1)
-        load_dy(2)
-        load_dy(3)
+        for t in range(1, PACK):
+            load_dy(t)
+        load_gate_column()
         load_x(0)
         load_x(1)
         load_w(0)
@@ -288,29 +274,30 @@ def tile_moe_mlp_relu_kernel(tc, xT, dyT, a, w2, gate, offs, out):
         load_a(1, 0, 2)
         load_a(1, 2, 3)
         load_a(1, 3, 4)
+
         spread_gate0()
-        spread(1)
-        take_gate1()
-        gather_g0(0, 0, HALF)
-        gather_g0(0, HALF, C)
-        for t in range(1, PACK - 1):
-            gather_g0(t)
-        gather_g0(PACK - 1, 0, HALF)
-        gather_g0(PACK - 1, HALF, C)
+        spread_gate1()
+        for t in range(PACK):
+            if t in (0, PACK - 1):
+                gather_g0(t, 0, HALF)
+                gather_g0(t, HALF, C)
+            else:
+                gather_g0(t)
         for t in range(PACK):
             gather_dy1(t)
 
         round_g0(0, HALF, on_vector)
-        round_g0(HALF, C, on_vector)
+        round_g0(HALF, C - G0_ON_SCALAR, on_vector)
+        round_g0(C - G0_ON_SCALAR, C, on_scalar)
         gate_round_g1()
         quantize_g(0)
         for e in range(E):
             gather_x(0, e)
-        turn_xx(0)
+        turn_x(0, 0, 1)
         gather_x(1, 0)
-        turn_x(0, 1, 2)
+        turn_x(1, 0)
         round_w(0, 3, 4, on_scalar)
-        take_xx(0, on_scalar)
+        take_x(0, 0, 1)
         gather_x(1, 1)
         round_w(0, 0, 2, on_vector)
         round_w(0, 2, 3, on_vector)
@@ -318,24 +305,26 @@ def tile_moe_mlp_relu_kernel(tc, xT, dyT, a, w2, gate, offs, out):
         quantize_w(0, 2, 3)
         quantize_w(0, 3, 4)
         quantize_g(1)
-        quantize_xx(0)
+        quantize_x(0, 0, 1)
+
         for b in range(H_TILES):
             product_dh(0, b)
         gather_x(2, 0)
-        take_x(0, 1, 2, on_scalar)
+        take_x(1, 0)
         for b in range(H_TILES):
             mask_dh(0, b)
         turn_da(0, 0, 2)
-        turn_x(1, 1, 2)
+        turn_x(1, 1)
         turn_da(0, 2, 4)
-        turn_x(0, 2, 3)
-        take_da(0, 0, 2, on_scalar)
-        take_x(1, 1, 2, on_scalar)
-        take_da(0, 2, 4, on_scalar)
-        take_x(0, 2, 3, on_scalar)
+        turn_x(2, 0)
+        take_da(0, 0, 2)
+        take_x(1, 1)
+        take_da(0, 2, 4)
+        take_x(2, 0)
         round_w(1, 3, 4, on_scalar)
         gather_x(2, 1)
-        quantize_x(0, 1, 2)
+
+        quantize_x(1, 0)
         round_w(1, 0, 1, on_vector)
         round_w(1, 1, 2, on_vector)
         quantize_w(1, 0, 1)
@@ -344,43 +333,41 @@ def tile_moe_mlp_relu_kernel(tc, xT, dyT, a, w2, gate, offs, out):
         product_dh(1, 0)
         product_dh(1, 1)
         round_w(1, 2, 3, on_vector)
-        quantize_x(0, 2, 3)
         quantize_da(0, 2, 4)
         quantize_w(1, 2, 3)
-        quantize_w(1, 3, 4)
-        product_out(0, 0)
+        product_out0(0)
         product_dh(1, 2)
-        product_out(0, 1)
-        product_dh(1, 3)
-        product_out(0, 2)
+        product_out0(1)
+
         mask_dh(1, 0)
         mask_dh(1, 1)
+        quantize_w(1, 3, 4)
+        quantize_x(2, 0)
+        quantize_x(1, 1)
         turn_da(1, 0, 2)
-        turn_x(1, 2, 3)
-        take_out(0, 0, on_scalar)
-        store(0, 0)
-        take_out(0, 1, on_scalar)
-        store(0, 1)
-        mask_dh(1, 2)
-        turn_da(1, 2, 3)
-        take_da(1, 0, 2, on_scalar)
-        take_x(1, 2, 3, on_scalar)
-        mask_dh(1, 3)
-        turn_da(1, 3, 4)
-        take_out(0, 2, on_vector)
-        store(0, 2)
+        product_dh(1, 3)
+        turn_x(2, 1)
+        product_out0(2)
+        finish_out0(0, on_scalar)
+        finish_out0(1, on_scalar)
+        take_da(1, 0, 2)
+        take_x(2, 1)
+        for b in (2, 3):
+            mask_dh(1, b)
+            turn_da(1, b, b + 1)
+
         quantize_da(1, 0, 2)
-        quantize_x(1, 1, 2)
-        quantize_x(1, 2, 3)
-        take_da(1, 2, 3, on_scalar)
-        take_da(1, 3, 4, on_scalar)
+        finish_out0(2, on_vector)
+        quantize_x(2, 1)
+        for b in (2, 3):
+            take_da(1, b, b + 1)
         for k in range(K_TILES):
-            product_half(1, 0, k, k + 1)
-        quantize_da(1, 2, 3)
-        quantize_da(1, 3, 4)
+            product_out1(0, k)
+        for b in (2, 3):
+            quantize_da(1, b, b + 1)
         for k in range(K_TILES):
-            product_half(1, 1, k, k + 1)
-        for h in range(2):
-            for k in range(K_TILES):
-                take_half(1, h, k, k + 1, on_vector if (k + h) % 2 else on_scalar)
-                store_half(1, h, k, k + 1)
+            product_out1(1, k)
+        for k in range(K_TILES):
+            finish_out1(0, k, on_scalar)
+        for k in range(K_TILES):
+            finish_out1(1, k, on_scalar if k % 2 else on_vector)

@@ -25,10 +25,9 @@ K_TILES = K // P
 H_TILES = H // P
 LIST_COLS = C // 16
 HALF = 2 * P
-G0_ON_SCALAR = C // 8
 QUAD = 32
-VECTOR_TILES = 34
-SCALAR_TILES = 24
+VECTOR_TILES = 29
+SCALAR_TILES = 21
 BANKS = 8
 
 
@@ -45,6 +44,9 @@ def tile_moe_mlp_relu_kernel(tc, xT, dyT, a, w2, gate, offs, out):
     def on_vector(dst, src):
         nc.vector.tensor_copy(out=dst, in_=src)
 
+    def on_gpsimd(dst, src):
+        nc.gpsimd.tensor_scalar(dst, src, 1.0, 0.0, MULT, ADD)
+
     with ExitStack() as ctx:
         keep = ctx.enter_context(tc.tile_pool(name="keep", bufs=1))
         psum = ctx.enter_context(tc.psum_pool(name="psum", bufs=BANKS))
@@ -56,7 +58,7 @@ def tile_moe_mlp_relu_kernel(tc, xT, dyT, a, w2, gate, offs, out):
         gate0 = held("gate0", [P, C], F32)
         dy = [held("dy%d" % t, [P, T], F32) for t in range(PACK)]
         x32 = [held("x32_%d" % k, [P, T], F32) for k in range(K_TILES)]
-        w32 = [held("w32_%d" % e, [P, PACK, H], F32) for e in range(E)]
+        w32 = {}
         saved = {}
         g32 = [held("g32_%d" % e, [P, PACK, C], F32) for e in range(E)]
         g16 = [held("g16_%d" % e, [P, C, PACK], BF16) for e in range(E)]
@@ -106,8 +108,11 @@ def tile_moe_mlp_relu_kernel(tc, xT, dyT, a, w2, gate, offs, out):
         def load_x(k):
             nc.sync.dma_start(x32[k][:], xT[k * P:(k + 1) * P, :])
 
-        def load_w(e):
-            nc.sync.dma_start(w32[e][:], w2[e].rearrange("(p t) i -> p t i", t=PACK))
+        def load_w(e, b0, b1):
+            columns = held("w32_%d_%d" % (e, b0), [P, PACK, (b1 - b0) * P], F32)
+            nc.sync.dma_start(columns[:], w2[e].rearrange("(p t) i -> p t i", t=PACK)[:, :, b0 * P:b1 * P])
+            for b in range(b0, b1):
+                w32[(e, b)] = (columns, (b - b0) * P)
 
         def load_a(e, b0, b1):
             rows = held("a%d_%d" % (e, b0), [P, b1 - b0, C], F32)
@@ -164,12 +169,26 @@ def tile_moe_mlp_relu_kernel(tc, xT, dyT, a, w2, gate, offs, out):
         def round_g0(c0, c1, copy):
             interleave(copy, g16[0][:, c0:c1, :], g32[0][:, :, c0:c1])
 
+        def round_g0_on_gpsimd(c0, c1):
+            on_gpsimd(g16[0][:, c0:c1, :], g32[0][:, :, c0:c1].rearrange("p t c -> p c t"))
+
         def quantize_g(e):
             quantize(fresh(on_vector, ("gc", e), [P, C], U32)[:], g_scales[e][:], g16[e][:].rearrange("p c t -> p (c t)"), E5M2)
 
         def round_w(e, b0, b1, copy):
-            w16 = fresh(copy, ("w16", e, b0), [P, (b1 - b0) * P, PACK], BF16)
-            interleave(copy, w16[:], w32[e][:, :, b0 * P:b1 * P])
+            columns, c0 = w32[(e, b0)]
+            if (e, b0) == (0, 2):
+                w16 = keep.tile([P, HALF, PACK], BF16, name="w16_0_2", tag="shared_w16", align_bytes=64)
+                made[("w16", e, b0)] = w16
+            else:
+                w16 = fresh(copy, ("w16", e, b0), [P, (b1 - b0) * P, PACK], BF16)
+            interleave(copy, w16[:], columns[:, :, c0:c0 + (b1 - b0) * P])
+
+        def round_w_on_gpsimd(e, b0, b1):
+            columns, c0 = w32[(e, b0)]
+            w16 = keep.tile([P, (b1 - b0) * P, PACK], BF16, name="w16_by_gpsimd", tag="shared_w16", align_bytes=64)
+            made[("w16", e, b0)] = w16
+            on_gpsimd(w16[:], columns[:, :, c0:c0 + (b1 - b0) * P].rearrange("p t c -> p c t"))
 
         def quantize_w(e, b0, b1):
             codes = fresh(on_vector, ("wc", e, b0), [P, (b1 - b0) * P], U32)
@@ -212,8 +231,8 @@ def tile_moe_mlp_relu_kernel(tc, xT, dyT, a, w2, gate, offs, out):
         def turn_x(k, *experts):
             turn(*x_keys(k, experts))
 
-        def take_x(k, *experts):
-            take(on_scalar, *x_keys(k, experts))
+        def take_x(copy, k, *experts):
+            take(copy, *x_keys(k, experts))
 
         def quantize_x(k, *experts):
             codes = fresh(on_vector, ("xc", experts[0], k), [P, len(experts) * P], U32)
@@ -225,8 +244,8 @@ def tile_moe_mlp_relu_kernel(tc, xT, dyT, a, w2, gate, offs, out):
         def turn_da(e, b0, b1):
             turn(*[("da", e, b) for b in range(b0, b1)])
 
-        def take_da(e, b0, b1):
-            take(on_scalar, *[("da", e, b) for b in range(b0, b1)])
+        def take_da(copy, e, b0, b1):
+            take(copy, *[("da", e, b) for b in range(b0, b1)])
 
         def quantize_da(e, b0, b1):
             if b0 % 2:
@@ -248,7 +267,9 @@ def tile_moe_mlp_relu_kernel(tc, xT, dyT, a, w2, gate, offs, out):
         def finish_out0(k, copy):
             result = fresh(copy, ("res", 0, k), [P, H], F32)
             copy(result[:], banks[("out", 0, k)][:])
-            nc.sync.dma_start(out[0, k * P:(k + 1) * P, :], result[:])
+
+        def store_out0(k):
+            nc.sync.dma_start(out[0, k * P:(k + 1) * P, :], made[("res", 0, k)][:])
 
         def product_out1(h, k):
             product_pass(new_bank(("out", 1, h, k), [P, HALF])[:], 1, h, k)
@@ -256,7 +277,10 @@ def tile_moe_mlp_relu_kernel(tc, xT, dyT, a, w2, gate, offs, out):
         def finish_out1(h, k, copy):
             result = fresh(copy, ("res", 1, h, k), [P, HALF], F32)
             copy(result[:], banks[("out", 1, h, k)][:])
-            nc.sync.dma_start(out[1, k * P:(k + 1) * P, half(h)], result[:])
+
+        def store_out1(h, k):
+            nc.sync.dma_start(out[1, k * P:(k + 1) * P, half(h)], made[("res", 1, h, k)][:])
+
 
         load_gate_runs()
         load_dy(0)
@@ -266,11 +290,13 @@ def tile_moe_mlp_relu_kernel(tc, xT, dyT, a, w2, gate, offs, out):
         load_gate_column()
         load_x(0)
         load_x(1)
-        load_w(0)
+        load_w(0, 0, 4)
         load_x(2)
         load_a(0, 0, 2)
-        load_a(0, 2, 4)
-        load_w(1)
+        load_w(1, 0, 2)
+        load_a(0, 2, 3)
+        load_a(0, 3, 4)
+        load_w(1, 2, 4)
         load_a(1, 0, 2)
         load_a(1, 2, 3)
         load_a(1, 3, 4)
@@ -285,89 +311,93 @@ def tile_moe_mlp_relu_kernel(tc, xT, dyT, a, w2, gate, offs, out):
                 gather_g0(t)
         for t in range(PACK):
             gather_dy1(t)
-
         round_g0(0, HALF, on_vector)
-        round_g0(HALF, C - G0_ON_SCALAR, on_vector)
-        round_g0(C - G0_ON_SCALAR, C, on_scalar)
+        gather_x(0, 0)
+        round_g0_on_gpsimd(HALF, C)
         gate_round_g1()
-        quantize_g(0)
-        for e in range(E):
-            gather_x(0, e)
+        gather_x(0, 1)
         turn_x(0, 0, 1)
         gather_x(1, 0)
-        turn_x(1, 0)
-        round_w(0, 3, 4, on_scalar)
-        take_x(0, 0, 1)
+        take_x(on_vector, 0, 0, 1)
+        round_w(0, 1, 2, on_scalar)
+        round_w(0, 0, 1, on_vector)
+        round_w(0, 2, 4, on_scalar)
+        quantize_g(0)
         gather_x(1, 1)
-        round_w(0, 0, 2, on_vector)
-        round_w(0, 2, 3, on_vector)
-        quantize_w(0, 0, 2)
-        quantize_w(0, 2, 3)
-        quantize_w(0, 3, 4)
-        quantize_g(1)
-        quantize_x(0, 0, 1)
-
-        for b in range(H_TILES):
-            product_dh(0, b)
+        quantize_w(0, 0, 1)
+        product_dh(0, 0)
         gather_x(2, 0)
-        take_x(1, 0)
-        for b in range(H_TILES):
-            mask_dh(0, b)
-        turn_da(0, 0, 2)
-        turn_x(1, 1)
-        turn_da(0, 2, 4)
-        turn_x(2, 0)
-        take_da(0, 0, 2)
-        take_x(1, 1)
-        take_da(0, 2, 4)
-        take_x(2, 0)
-        round_w(1, 3, 4, on_scalar)
+        quantize_w(0, 1, 2)
+        product_dh(0, 1)
         gather_x(2, 1)
-
-        quantize_x(1, 0)
-        round_w(1, 0, 1, on_vector)
-        round_w(1, 1, 2, on_vector)
-        quantize_w(1, 0, 1)
-        quantize_da(0, 0, 2)
-        quantize_w(1, 1, 2)
+        quantize_x(0, 0, 1)
+        quantize_g(1)
+        quantize_w(0, 2, 4)
+        product_dh(0, 2)
+        product_dh(0, 3)
+        turn_x(1, 0, 1)
+        take_x(on_scalar, 1, 0, 1)
+        round_w_on_gpsimd(1, 0, 2)
+        mask_dh(0, 0)
+        round_w(1, 2, 3, on_scalar)
+        mask_dh(0, 1)
+        turn_da(0, 0, 2)
+        mask_dh(0, 2)
+        mask_dh(0, 3)
+        turn_da(0, 2, 4)
+        turn_x(2, 0, 1)
+        take_da(on_scalar, 0, 2, 4)
+        take_da(on_vector, 0, 0, 2)
+        round_w(1, 3, 4, on_scalar)
+        quantize_w(1, 0, 2)
         product_dh(1, 0)
         product_dh(1, 1)
-        round_w(1, 2, 3, on_vector)
-        quantize_da(0, 2, 4)
+        take_x(on_scalar, 2, 0, 1)
+        quantize_x(1, 0, 1)
+        quantize_da(0, 0, 2)
         quantize_w(1, 2, 3)
-        product_out0(0)
         product_dh(1, 2)
+        quantize_da(0, 2, 4)
+        product_out0(0)
         product_out0(1)
-
-        mask_dh(1, 0)
-        mask_dh(1, 1)
-        quantize_w(1, 3, 4)
-        quantize_x(2, 0)
-        quantize_x(1, 1)
-        turn_da(1, 0, 2)
-        product_dh(1, 3)
-        turn_x(2, 1)
-        product_out0(2)
         finish_out0(0, on_scalar)
+        store_out0(0)
+        mask_dh(1, 0)
         finish_out0(1, on_scalar)
-        take_da(1, 0, 2)
-        take_x(2, 1)
-        for b in (2, 3):
-            mask_dh(1, b)
-            turn_da(1, b, b + 1)
-
+        store_out0(1)
+        quantize_w(1, 3, 4)
+        product_dh(1, 3)
+        mask_dh(1, 1)
+        turn_da(1, 0, 2)
+        take_da(on_scalar, 1, 0, 2)
+        quantize_x(2, 0, 1)
+        product_out0(2)
+        finish_out0(2, on_scalar)
+        store_out0(2)
+        mask_dh(1, 2)
+        turn_da(1, 2, 3)
+        take_da(on_scalar, 1, 2, 3)
+        mask_dh(1, 3)
+        turn_da(1, 3, 4)
+        take_da(on_scalar, 1, 3, 4)
         quantize_da(1, 0, 2)
-        finish_out0(2, on_vector)
-        quantize_x(2, 1)
-        for b in (2, 3):
-            take_da(1, b, b + 1)
-        for k in range(K_TILES):
-            product_out1(0, k)
-        for b in (2, 3):
-            quantize_da(1, b, b + 1)
-        for k in range(K_TILES):
-            product_out1(1, k)
-        for k in range(K_TILES):
-            finish_out1(0, k, on_scalar)
-        for k in range(K_TILES):
-            finish_out1(1, k, on_scalar if k % 2 else on_vector)
+        product_out1(0, 0)
+        product_out1(0, 1)
+        product_out1(0, 2)
+        finish_out1(0, 0, on_scalar)
+        store_out1(0, 0)
+        quantize_da(1, 2, 3)
+        finish_out1(0, 2, on_scalar)
+        quantize_da(1, 3, 4)
+        product_out1(1, 0)
+        product_out1(1, 1)
+        product_out1(1, 2)
+        finish_out1(1, 1, on_scalar)
+        finish_out1(0, 1, on_vector)
+        store_out1(0, 1)
+        finish_out1(1, 0, on_vector)
+        store_out1(0, 2)
+        finish_out1(1, 2, on_vector)
+        store_out1(1, 0)
+        store_out1(1, 1)
+        store_out1(1, 2)

@@ -25,9 +25,10 @@ K_TILES = K // P
 H_TILES = H // P
 LIST_COLS = C // 16
 HALF = 2 * P
+G0_ON_VECTOR = 320
 QUAD = 32
-VECTOR_TILES = 29
-SCALAR_TILES = 21
+VECTOR_TILES = 30
+SCALAR_TILES = 23
 BANKS = 8
 
 
@@ -177,16 +178,12 @@ def tile_moe_mlp_relu_kernel(tc, xT, dyT, a, w2, gate, offs, out):
 
         def round_w(e, b0, b1, copy):
             columns, c0 = w32[(e, b0)]
-            if (e, b0) == (0, 2):
-                w16 = keep.tile([P, HALF, PACK], BF16, name="w16_0_2", tag="shared_w16", align_bytes=64)
-                made[("w16", e, b0)] = w16
-            else:
-                w16 = fresh(copy, ("w16", e, b0), [P, (b1 - b0) * P, PACK], BF16)
+            w16 = fresh(copy, ("w16", e, b0), [P, (b1 - b0) * P, PACK], BF16)
             interleave(copy, w16[:], columns[:, :, c0:c0 + (b1 - b0) * P])
 
         def round_w_on_gpsimd(e, b0, b1):
             columns, c0 = w32[(e, b0)]
-            w16 = keep.tile([P, (b1 - b0) * P, PACK], BF16, name="w16_by_gpsimd", tag="shared_w16", align_bytes=64)
+            w16 = keep.tile([P, (b1 - b0) * P, PACK], BF16, name="w16_by_gpsimd", tag="g16_1", align_bytes=64)
             made[("w16", e, b0)] = w16
             on_gpsimd(w16[:], columns[:, :, c0:c0 + (b1 - b0) * P].rearrange("p t c -> p c t"))
 
@@ -291,9 +288,9 @@ def tile_moe_mlp_relu_kernel(tc, xT, dyT, a, w2, gate, offs, out):
         load_x(0)
         load_x(1)
         load_w(0, 0, 4)
-        load_x(2)
         load_a(0, 0, 2)
         load_w(1, 0, 2)
+        load_x(2)
         load_a(0, 2, 3)
         load_a(0, 3, 4)
         load_w(1, 2, 4)
@@ -305,75 +302,77 @@ def tile_moe_mlp_relu_kernel(tc, xT, dyT, a, w2, gate, offs, out):
         spread_gate1()
         for t in range(PACK):
             if t in (0, PACK - 1):
-                gather_g0(t, 0, HALF)
-                gather_g0(t, HALF, C)
+                cut = G0_ON_VECTOR if t else HALF
+                gather_g0(t, 0, cut)
+                gather_g0(t, cut, C)
             else:
                 gather_g0(t)
         for t in range(PACK):
             gather_dy1(t)
-        round_g0(0, HALF, on_vector)
+        round_g0(0, G0_ON_VECTOR, on_vector)
         gather_x(0, 0)
-        round_g0_on_gpsimd(HALF, C)
+        round_g0_on_gpsimd(G0_ON_VECTOR, C)
         gate_round_g1()
         gather_x(0, 1)
+        quantize_g(0)
         turn_x(0, 0, 1)
         gather_x(1, 0)
-        take_x(on_vector, 0, 0, 1)
-        round_w(0, 1, 2, on_scalar)
-        round_w(0, 0, 1, on_vector)
-        round_w(0, 2, 4, on_scalar)
-        quantize_g(0)
-        gather_x(1, 1)
-        quantize_w(0, 0, 1)
+        round_w(0, 0, 2, on_vector)
+        turn_x(1, 0)
+        round_w(0, 3, 4, on_scalar)
+        round_w(0, 2, 3, on_vector)
+        take_x(on_scalar, 0, 0, 1)
+        quantize_w(0, 0, 2)
         product_dh(0, 0)
-        gather_x(2, 0)
-        quantize_w(0, 1, 2)
         product_dh(0, 1)
-        gather_x(2, 1)
+        gather_x(1, 1)
+        quantize_w(0, 2, 3)
+        product_dh(0, 2)
+        take_x(on_scalar, 1, 0)
+        quantize_w(0, 3, 4)
+        product_dh(0, 3)
+        gather_x(2, 0)
         quantize_x(0, 0, 1)
         quantize_g(1)
-        quantize_w(0, 2, 4)
-        product_dh(0, 2)
-        product_dh(0, 3)
-        turn_x(1, 0, 1)
-        take_x(on_scalar, 1, 0, 1)
         round_w_on_gpsimd(1, 0, 2)
         mask_dh(0, 0)
-        round_w(1, 2, 3, on_scalar)
         mask_dh(0, 1)
         turn_da(0, 0, 2)
+        turn_x(1, 1)
+        take_da(on_scalar, 0, 0, 2)
         mask_dh(0, 2)
+        take_x(on_scalar, 1, 1)
         mask_dh(0, 3)
         turn_da(0, 2, 4)
-        turn_x(2, 0, 1)
+        turn_x(2, 0)
         take_da(on_scalar, 0, 2, 4)
-        take_da(on_vector, 0, 0, 2)
-        round_w(1, 3, 4, on_scalar)
+        quantize_x(1, 0)
+        take_x(on_scalar, 2, 0)
         quantize_w(1, 0, 2)
         product_dh(1, 0)
         product_dh(1, 1)
-        take_x(on_scalar, 2, 0, 1)
-        quantize_x(1, 0, 1)
+        gather_x(2, 1)
         quantize_da(0, 0, 2)
-        quantize_w(1, 2, 3)
-        product_dh(1, 2)
+        round_w(1, 2, 4, on_vector)
         quantize_da(0, 2, 4)
         product_out0(0)
         product_out0(1)
         finish_out0(0, on_scalar)
         store_out0(0)
-        mask_dh(1, 0)
+        quantize_w(1, 2, 4)
+        product_dh(1, 2)
+        product_dh(1, 3)
         finish_out0(1, on_scalar)
         store_out0(1)
-        quantize_w(1, 3, 4)
-        product_dh(1, 3)
+        mask_dh(1, 0)
         mask_dh(1, 1)
         turn_da(1, 0, 2)
+        turn_x(2, 1)
         take_da(on_scalar, 1, 0, 2)
-        quantize_x(2, 0, 1)
+        quantize_x(2, 0)
         product_out0(2)
-        finish_out0(2, on_scalar)
-        store_out0(2)
+        take_x(on_scalar, 2, 1)
+        quantize_x(1, 1)
         mask_dh(1, 2)
         turn_da(1, 2, 3)
         take_da(on_scalar, 1, 2, 3)
@@ -383,21 +382,24 @@ def tile_moe_mlp_relu_kernel(tc, xT, dyT, a, w2, gate, offs, out):
         quantize_da(1, 0, 2)
         product_out1(0, 0)
         product_out1(0, 1)
-        product_out1(0, 2)
         finish_out1(0, 0, on_scalar)
+        finish_out0(2, on_vector)
+        finish_out1(0, 1, on_scalar)
+        store_out0(2)
+        quantize_x(2, 1)
+        product_out1(0, 2)
+        finish_out1(0, 2, on_scalar)
         store_out1(0, 0)
         quantize_da(1, 2, 3)
-        finish_out1(0, 2, on_scalar)
+        store_out1(0, 1)
         quantize_da(1, 3, 4)
         product_out1(1, 0)
         product_out1(1, 1)
         product_out1(1, 2)
         finish_out1(1, 1, on_scalar)
-        finish_out1(0, 1, on_vector)
-        store_out1(0, 1)
-        finish_out1(1, 0, on_vector)
         store_out1(0, 2)
-        finish_out1(1, 2, on_vector)
+        finish_out1(1, 0, on_vector)
         store_out1(1, 0)
+        finish_out1(1, 2, on_vector)
         store_out1(1, 1)
         store_out1(1, 2)

@@ -25,7 +25,7 @@ K_TILES = K // P
 H_TILES = H // P
 LIST_COLS = C // 16
 HALF = 2 * P
-G0_ON_VECTOR = 320
+G0_ON_VECTOR = 256
 QUAD = 32
 VECTOR_TILES = 30
 SCALAR_TILES = 23

@@ -148,9 +148,9 @@ def tile_moe_mlp_relu_kernel(tc, xT, dyT, a, w2, gate, offs, out):
                 nc.vector.transpose(gate0[:, half(h)], gate_wide[:].rearrange("p c r -> p (c r)")[:, half(h)])
 
         def spread_gate1():
-            bank = new_bank("gate1", [P, PACK, P])
+            bank = new_bank("gate1", [P, P, PACK])
             for q in range(PACK):
-                nc.tensor.transpose(bank[:, q, :], gate_column[:, q:q + 1].to_broadcast([P, P]), ident[:])
+                nc.tensor.transpose(bank[:, :, q], gate_column[:, q:q + 1].to_broadcast([P, P]), ident[:])
 
         def gather_g0(t, c0=0, c1=C):
             nc.vector.tensor_tensor(g32[0][:, t, c0:c1], dy[t][:].indirect(slots(0, c0, c1)), gate0[:, c0:c1], MULT)
@@ -159,13 +159,11 @@ def tile_moe_mlp_relu_kernel(tc, xT, dyT, a, w2, gate, offs, out):
             nc.scalar.activation(g32[1][:, t, :], dy[t][:].indirect(slots(1)), COPY)
 
         def gate_round_g1():
-            for j in range(2):
-                pair = slice(2 * j, 2 * j + 2)
-                gate1 = banks["gate1"][:, pair, :].rearrange("p s n -> p n s").unsqueeze(2)
-                nc.vector.tensor_tensor(
-                    g16[1][:].rearrange("p (n q) t -> p n t q", q=PACK)[:, :, :, pair],
-                    g32[1][:].rearrange("p t (n q) -> p n t q", q=PACK)[:, :, :, pair],
-                    gate1.to_broadcast([P, P, PACK, 2]), MULT)
+            gate1 = banks["gate1"][:].rearrange("p m (j s) -> p (m j) s", s=2).unsqueeze(2)
+            nc.vector.tensor_tensor(
+                g16[1][:].rearrange("p (n s) t -> p n t s", s=2),
+                g32[1][:].rearrange("p t (n s) -> p n t s", s=2),
+                gate1.to_broadcast([P, HALF, PACK, 2]), MULT)
 
         def round_g0(c0, c1, copy):
             interleave(copy, g16[0][:, c0:c1, :], g32[0][:, :, c0:c1])

from contextlib import ExitStack

import concourse.mybir as mybir

K, T, E, C, H, N = 384, 1024, 2, 512, 512, 512
FLOPS = 2 * E * C * H * (N + K)
BYTES = 4 * (K * T + N * T + H * E * C + E * N * H + E * C + E * K * H) + 2 * 128 * 64

F32 = mybir.dt.float32
BF16 = mybir.dt.bfloat16
U32 = mybir.dt.uint32
U16 = mybir.dt.uint16
U8 = mybir.dt.uint8
E4M3 = mybir.dt.float8_e4m3fn_x4
E5M2 = mybir.dt.float8_e5m2_x4
COPY = mybir.ActivationFunctionType.Copy
MULT = mybir.AluOpType.mult
ADD = mybir.AluOpType.add
IS_EQUAL = mybir.AluOpType.is_equal
IS_GT = mybir.AluOpType.is_gt

P = 128
PACK = 4
K_TILES = K // P
H_TILES = H // P
LIST_COLS = C // 16
HALF = 2 * P
G0_ON_VECTOR = 256
QUAD = 32
VECTOR_TILES = 30
SCALAR_TILES = 23
BANKS = 8


def interleave(copy, dst, src):
    copy(dst.rearrange("p (c i) t -> p c t i", i=4), src.rearrange("p t (c i) -> p c t i", i=4))


def tile_moe_mlp_relu_kernel(tc, xT, dyT, a, w2, gate, offs, out):
    nc = tc.nc

    def on_scalar(dst, src):
        nc.scalar.copy(out=dst, in_=src)

    def on_vector(dst, src):
        nc.vector.tensor_copy(out=dst, in_=src)

    def on_gpsimd(dst, src):
        nc.gpsimd.tensor_scalar(dst, src, 1.0, 0.0, MULT, ADD)

    with ExitStack() as ctx:
        keep = ctx.enter_context(tc.tile_pool(name="keep", bufs=1))
        psum = ctx.enter_context(tc.psum_pool(name="psum", bufs=BANKS))

        def held(name, shape, dtype):
            return keep.tile(shape, dtype, name=name, align_bytes=64)

        offsets = keep.tile([P, E * LIST_COLS], U16, name="offsets")
        gate0 = held("gate0", [P, C], F32)
        dy = [held("dy%d" % t, [P, T], F32) for t in range(PACK)]
        x32 = [held("x32_%d" % k, [P, T], F32) for k in range(K_TILES)]
        w32 = {}
        saved = {}
        g32 = [held("g32_%d" % e, [P, PACK, C], F32) for e in range(E)]
        g16 = [held("g16_%d" % e, [P, C, PACK], BF16) for e in range(E)]
        g_scales = [held("gs%d" % e, [P, C], U8) for e in range(E)]
        w_scales = [held("ws%d" % e, [P, H], U8) for e in range(E)]
        gate_column = held("gate_column", [P, PACK], F32)
        gate_runs = held("gate_runs", [P, QUAD], F32)
        gate_turned = held("gate_turned", [P, QUAD], F32)
        gate_wide = held("gate_wide", [P, C // QUAD, QUAD], F32)
        da_scales = [held("ds%d" % e, [P, H], U8) for e in range(E)]

        made = {}

        def fresh(writer, key, shape, dtype):
            tag, bufs = ("by_vector", VECTOR_TILES) if writer is on_vector else ("by_scalar", SCALAR_TILES)
            made[key] = keep.tile(shape, dtype, name="_".join(str(part) for part in key), tag=tag, bufs=bufs, align_bytes=64)
            return made[key]

        ident = held("ident", [P, P], F32)
        ones = held("ones", [P, QUAD], F32)
        column = held("column", [P, QUAD], F32)
        row = held("row", [P, QUAD], F32)
        nc.vector.memset(ones[:], 1.0)
        nc.vector.memset(ident[:], 0.0)
        nc.vector.tensor_tensor_scan(column[:], ones[:], ones[:], 0.0, MULT, ADD)
        nc.vector.transpose(row[:], column[:])
        diagonal = held("diagonal", [P, QUAD], F32)
        nc.vector.tensor_tensor(diagonal[:], column[:], row[:], IS_EQUAL)
        for q0 in range(0, P, QUAD):
            part = slice(q0, q0 + QUAD)
            nc.scalar.activation(ident[part, part], diagonal[part, :], COPY)

        dy_rows = dyT.rearrange("(p t) c -> t p c", t=PACK)

        def load_gate_runs():
            nc.sync.dma_start(gate_runs[:], gate[0:P // QUAD, :].rearrange("q (c b) -> (q c) b", b=QUAD))

        def load_gate_column():
            nc.sync.dma_start(gate_column[:], gate[0, C:2 * C].rearrange("(n q) -> n q", q=PACK))

        def load_dy(t):
            nc.sync.dma_start(dy[t][:], dy_rows[t])

        def load_offsets():
            nc.sync.dma_start(offsets[:], offs)

        def load_x(k):
            nc.sync.dma_start(x32[k][:], xT[k * P:(k + 1) * P, :])

        def load_w(e, b0, b1):
            columns = held("w32_%d_%d" % (e, b0), [P, PACK, (b1 - b0) * P], F32)
            nc.sync.dma_start(columns[:], w2[e].rearrange("(p t) i -> p t i", t=PACK)[:, :, b0 * P:b1 * P])
            for b in range(b0, b1):
                w32[(e, b)] = (columns, (b - b0) * P)

        def load_a(e, b0, b1):
            rows = held("a%d_%d" % (e, b0), [P, b1 - b0, C], F32)
            nc.sync.dma_start(rows[:], a[b0 * P:b1 * P, e * C:(e + 1) * C].rearrange("(b p) c -> p b c", p=P))
            for b in range(b0, b1):
                saved[(e, b)] = rows[:, b - b0, :]

        banks = {}

        def new_bank(key, shape):
            banks[key] = psum.tile(shape, F32, name="bank")
            return banks[key]

        def slots(e, c0=0, c1=C):
            return offsets[:, (e * C + c0) // 16:(e * C + c1) // 16]

        def half(h):
            return slice(h * HALF, (h + 1) * HALF)

        def pairs(columns, u):
            return columns.rearrange("p (r u s) -> p r u s", u=2, s=2)[:, :, u, :]

        def quantize(codes, scales, values, fmt):
            nc.vector.quantize_mx(out=codes.bitcast(fmt), scales=scales, in_=values)

        def spread_gate0():
            nc.vector.transpose(gate_turned[:], gate_runs[:])
            for h in range(2):
                runs = slice(h * HALF // QUAD, (h + 1) * HALF // QUAD)
                on_vector(gate_wide[:, runs, :], gate_turned[:, runs].unsqueeze(2).to_broadcast([P, HALF // QUAD, QUAD]))
            for h in range(2):
                nc.vector.transpose(gate0[:, half(h)], gate_wide[:].rearrange("p c r -> p (c r)")[:, half(h)])

        def spread_gate1():
            bank = new_bank("gate1", [P, P, PACK])
            for q in range(PACK):
                nc.tensor.transpose(bank[:, :, q], gate_column[:, q:q + 1].to_broadcast([P, P]), ident[:])

        def gather_g0(t, c0=0, c1=C):
            nc.vector.tensor_tensor(g32[0][:, t, c0:c1], dy[t][:].indirect(slots(0, c0, c1)), gate0[:, c0:c1], MULT)

        def gather_dy1(t):
            nc.scalar.activation(g32[1][:, t, :], dy[t][:].indirect(slots(1)), COPY)

        def gate_round_g1():
            gate1 = banks["gate1"][:].rearrange("p m (j s) -> p (m j) s", s=2).unsqueeze(2)
            nc.vector.tensor_tensor(
                g16[1][:].rearrange("p (n s) t -> p n t s", s=2),
                g32[1][:].rearrange("p t (n s) -> p n t s", s=2),
                gate1.to_broadcast([P, HALF, PACK, 2]), MULT)

        def round_g0(c0, c1, copy):
            interleave(copy, g16[0][:, c0:c1, :], g32[0][:, :, c0:c1])

        def round_g0_on_gpsimd(c0, c1):
            on_gpsimd(g16[0][:, c0:c1, :], g32[0][:, :, c0:c1].rearrange("p t c -> p c t"))

        def quantize_g(e):
            quantize(fresh(on_vector, ("gc", e), [P, C], U32)[:], g_scales[e][:], g16[e][:].rearrange("p c t -> p (c t)"), E5M2)

        def round_w(e, b0, b1, copy):
            columns, c0 = w32[(e, b0)]
            w16 = fresh(copy, ("w16", e, b0), [P, (b1 - b0) * P, PACK], BF16)
            interleave(copy, w16[:], columns[:, :, c0:c0 + (b1 - b0) * P])

        def round_w_on_gpsimd(e, b0, b1):
            columns, c0 = w32[(e, b0)]
            w16 = keep.tile([P, (b1 - b0) * P, PACK], BF16, name="w16_by_gpsimd", tag="g16_1", align_bytes=64)
            made[("w16", e, b0)] = w16
            on_gpsimd(w16[:], columns[:, :, c0:c0 + (b1 - b0) * P].rearrange("p t c -> p c t"))

        def quantize_w(e, b0, b1):
            codes = fresh(on_vector, ("wc", e, b0), [P, (b1 - b0) * P], U32)
            quantize(codes[:], w_scales[e][:, b0 * P:b1 * P], made[("w16", e, b0)][:].rearrange("p i t -> p (i t)"), E4M3)
            for b in range(b0, b1):
                made[("w_codes", e, b)] = codes[:, (b - b0) * P:(b - b0 + 1) * P]

        def product_dh(e, b):
            dh = new_bank(("dh", e, b), [P, C])
            nc.tensor.matmul_mx(out=dh[:], lhsT=made[("w_codes", e, b)].bitcast(E4M3), lhsT_scale=w_scales[e][:, b * P:(b + 1) * P],
                                rhs=made[("gc", e)][:].bitcast(E5M2), rhs_scale=g_scales[e][:], start=True, stop=True)

        def mask_dh(e, b):
            da = fresh(on_vector, ("da", e, b), [P, 2, P, 2], BF16)
            for u in range(2):
                nc.vector.scalar_tensor_tensor(da[:, u], pairs(saved[(e, b)], u), 0.0, pairs(banks[("dh", e, b)][:], u), IS_GT, MULT)
            made[("words", "da", e, b)] = [da[:, u].rearrange("p r s -> p (r s)").bitcast(F32) for u in range(2)]

        def gather_x(k, e):
            x_slots = fresh(on_scalar, ("x", e, k), [P, C], BF16)
            nc.scalar.activation(x_slots[:], x32[k][:].indirect(slots(e)), COPY)
            made[("words", "x", e, k)] = [x_slots[:].bitcast(F32)[:, u:2 * P:2] for u in range(2)]

        def turn(*keys):
            bank = new_bank(keys, [P, len(keys), 2, P])
            for j, key in enumerate(keys):
                for u in range(2):
                    nc.tensor.transpose(bank[:, j, u, :], made[("words",) + key][u], ident[:])

        def take(copy, *keys):
            turned = fresh(copy, ("turned",) + keys[0], [P, len(keys), P, 2], F32)
            copy(turned[:], banks[keys][:].rearrange("p j u m -> p j m u"))

        def turned_values(key):
            return made[("turned",) + key][:].rearrange("p j m u -> p (j m u)").bitcast(BF16)

        def x_keys(k, experts):
            return [("x", e, k) for e in experts]

        def turn_x(k, *experts):
            turn(*x_keys(k, experts))

        def take_x(copy, k, *experts):
            take(copy, *x_keys(k, experts))

        def quantize_x(k, *experts):
            codes = fresh(on_vector, ("xc", experts[0], k), [P, len(experts) * P], U32)
            scales = held("xs%d_%d" % (experts[0], k), [P, len(experts) * P], U8)
            quantize(codes[:], scales[:], turned_values(("x", experts[0], k)), E4M3)
            for j, e in enumerate(experts):
                made[("x_codes", e, k)] = (codes[:, j * P:(j + 1) * P], scales[:, j * P:(j + 1) * P])

        def turn_da(e, b0, b1):
            turn(*[("da", e, b) for b in range(b0, b1)])

        def take_da(copy, e, b0, b1):
            take(copy, *[("da", e, b) for b in range(b0, b1)])

        def quantize_da(e, b0, b1):
            if b0 % 2:
                codes = made[("dc", e, b0 // 2)][:, P:HALF]
            else:
                codes = fresh(on_vector, ("dc", e, b0 // 2), [P, HALF], U32)[:, 0:(b1 - b0) * P]
            quantize(codes, da_scales[e][:, b0 * P:b1 * P], turned_values(("da", e, b0)), E5M2)

        def product_pass(acc, e, h, k):
            codes, scales = made[("x_codes", e, k)]
            nc.tensor.matmul_mx(out=acc, lhsT=codes.bitcast(E4M3), lhsT_scale=scales,
                                rhs=made[("dc", e, h)][:].bitcast(E5M2), rhs_scale=da_scales[e][:, half(h)], start=True, stop=True)

        def product_out0(k):
            acc = new_bank(("out", 0, k), [P, H])
            for h in (1, 0):
                product_pass(acc[:, half(h)], 0, h, k)

        def finish_out0(k, copy):
            result = fresh(copy, ("res", 0, k), [P, H], F32)
            copy(result[:], banks[("out", 0, k)][:])

        def store_out0(k):
            nc.sync.dma_start(out[0, k * P:(k + 1) * P, :], made[("res", 0, k)][:])

        def product_out1(h, k):
            product_pass(new_bank(("out", 1, h, k), [P, HALF])[:], 1, h, k)

        def finish_out1(h, k, copy):
            result = fresh(copy, ("res", 1, h, k), [P, HALF], F32)
            copy(result[:], banks[("out", 1, h, k)][:])

        def store_out1(h, k):
            nc.sync.dma_start(out[1, k * P:(k + 1) * P, half(h)], made[("res", 1, h, k)][:])


        load_gate_runs()
        load_dy(0)
        load_offsets()
        for t in range(1, PACK):
            load_dy(t)
        load_gate_column()
        load_x(0)
        load_x(1)
        load_w(0, 0, 4)
        load_a(0, 0, 2)
        load_w(1, 0, 2)
        load_x(2)
        load_a(0, 2, 3)
        load_a(0, 3, 4)
        load_w(1, 2, 4)
        load_a(1, 0, 2)
        load_a(1, 2, 3)
        load_a(1, 3, 4)

        spread_gate0()
        spread_gate1()
        for t in range(PACK):
            if t in (0, PACK - 1):
                cut = G0_ON_VECTOR if t else HALF
                gather_g0(t, 0, cut)
                gather_g0(t, cut, C)
            else:
                gather_g0(t)
        for t in range(PACK):
            gather_dy1(t)
        round_g0(0, G0_ON_VECTOR, on_vector)
        gather_x(0, 0)
        round_g0_on_gpsimd(G0_ON_VECTOR, C)
        gate_round_g1()
        gather_x(0, 1)
        quantize_g(0)
        turn_x(0, 0, 1)
        gather_x(1, 0)
        round_w(0, 0, 2, on_vector)
        turn_x(1, 0)
        round_w(0, 3, 4, on_scalar)
        round_w(0, 2, 3, on_vector)
        take_x(on_scalar, 0, 0, 1)
        quantize_w(0, 0, 2)
        product_dh(0, 0)
        product_dh(0, 1)
        gather_x(1, 1)
        quantize_w(0, 2, 3)
        product_dh(0, 2)
        take_x(on_scalar, 1, 0)
        quantize_w(0, 3, 4)
        product_dh(0, 3)
        gather_x(2, 0)
        quantize_x(0, 0, 1)
        quantize_g(1)
        round_w_on_gpsimd(1, 0, 2)
        mask_dh(0, 0)
        mask_dh(0, 1)
        turn_da(0, 0, 2)
        turn_x(1, 1)
        take_da(on_scalar, 0, 0, 2)
        mask_dh(0, 2)
        take_x(on_scalar, 1, 1)
        mask_dh(0, 3)
        turn_da(0, 2, 4)
        turn_x(2, 0)
        take_da(on_scalar, 0, 2, 4)
        quantize_x(1, 0)
        take_x(on_scalar, 2, 0)
        quantize_w(1, 0, 2)
        product_dh(1, 0)
        product_dh(1, 1)
        gather_x(2, 1)
        quantize_da(0, 0, 2)
        round_w(1, 2, 4, on_vector)
        quantize_da(0, 2, 4)
        product_out0(0)
        product_out0(1)
        finish_out0(0, on_scalar)
        store_out0(0)
        quantize_w(1, 2, 4)
        product_dh(1, 2)
        product_dh(1, 3)
        finish_out0(1, on_scalar)
        store_out0(1)
        mask_dh(1, 0)
        mask_dh(1, 1)
        turn_da(1, 0, 2)
        turn_x(2, 1)
        take_da(on_scalar, 1, 0, 2)
        quantize_x(2, 0)
        product_out0(2)
        take_x(on_scalar, 2, 1)
        quantize_x(1, 1)
        mask_dh(1, 2)
        turn_da(1, 2, 3)
        take_da(on_scalar, 1, 2, 3)
        mask_dh(1, 3)
        turn_da(1, 3, 4)
        take_da(on_scalar, 1, 3, 4)
        quantize_da(1, 0, 2)
        product_out1(0, 0)
        product_out1(0, 1)
        finish_out1(0, 0, on_scalar)
        finish_out0(2, on_vector)
        finish_out1(0, 1, on_scalar)
        store_out0(2)
        quantize_x(2, 1)
        product_out1(0, 2)
        finish_out1(0, 2, on_scalar)
        store_out1(0, 0)
        quantize_da(1, 2, 3)
        store_out1(0, 1)
        quantize_da(1, 3, 4)
        product_out1(1, 0)
        product_out1(1, 1)
        product_out1(1, 2)
        finish_out1(1, 1, on_scalar)
        store_out1(0, 2)
        finish_out1(1, 0, on_vector)
        store_out1(1, 0)
        finish_out1(1, 2, on_vector)
        store_out1(1, 1)
        store_out1(1, 2)
